import numpy as np, ml_dtypes
CORES = [35,38,43,46]
N = 4
BF = ml_dtypes.bfloat16
def gentries(a):
    return np.ascontiguousarray(a.reshape(8, 16, -1).transpose(0, 2, 1)).reshape(8, -1)
def gtable(e):
    e = np.asarray(e); return np.ascontiguousarray(e.reshape(8, -1, 16).transpose(0, 2, 1)).reshape(128, -1).astype(np.int32)
L, M, B, P = 5, 512, 32, 3
H, F, E, G, LN = (N - 1) * B, (L - 1) * M, L * M, (L - 1) * (N - 1) * B, M // 2
NONE = E + G
LEV = np.concatenate([np.arange(E) // M, np.arange(G) // H, np.array([-1])])
DL = np.broadcast_to((np.arange(F) // M + 1)[:, None], (N, 8, F, 16)); SL = np.broadcast_to(np.concatenate([np.arange(F) // M, np.arange(G) // H]), (N, 8, F + G))
GM = [np.arange(8), 7 - np.arange(8), (8 - np.arange(8)) % 8]
def names(rng, lv, low):
    x = np.where(rng.random(lv.shape) < low, 0, (rng.random(lv.shape) * lv).astype(np.int64))
    y = rng.integers(0, M + H, lv.shape)
    return np.where(y < M, x * M + y, E + x * H + y - M)
def parts(rng):
    A = np.minimum((256 * rng.random((N, 8, E, 16)) ** 0.1666).astype(np.int64), 255); c = np.arange(E)[:, None]
    tight = rng.random((N, 8, E, 1)) < np.where(c < M, 0.0, np.where(c < F, 0.12, 0.3))
    A = np.where(tight, (A * (0.3 + 0.5 * rng.random((N, 8, E, 1)))).astype(np.int64), A)
    dp = names(rng, DL, 0.6); dp = np.where(rng.random(dp.shape) < rng.choice(np.array([0.0, 0.25, 0.5]), (N, 8, 1, 1)), NONE, dp)
    sb = names(rng, SL + 1, 0.3); sb = np.where(rng.random(sb.shape) < 0.0625, NONE, sb)
    return A, dp, sb, rng.integers(0, M, (N, 8, L - 1, N - 1, B)), rng.integers(40, 161, (N, 8, M))
def pack(A, dp, sb, bd, th):
    return {"av": np.ascontiguousarray(A.transpose(0, 1, 3, 2)).reshape(N, 128, E).astype(np.float32).astype(BF),
            "dp": np.ascontiguousarray(dp.transpose(0, 1, 3, 2)).reshape(N, 128, F).astype(np.int32), "sb": np.ascontiguousarray(sb).astype(np.int32),
            "bd": np.stack([gtable(a.reshape(8, -1)) for a in bd]), "th": np.ascontiguousarray(th).astype(np.int32)}
def setup_inputs(rng):
    A, dp, sb, bd, th = parts(rng)
    return pack(A, dp, sb, bd, th)
def setup_inputs_spread(rng):
    A, dp, sb, bd, th = parts(rng)
    A = np.where(rng.random((N, 8, E, 1)) < 0.1, np.exp2(8 * rng.random(A.shape)).astype(np.int64) - 1, 256 - np.exp2(7 * rng.random(A.shape)).astype(np.int64))
    dp = np.where(rng.random(dp.shape) < rng.choice(np.array([0.3, 0.6, 0.9]), (N, 8, F, 1)), NONE, dp)
    bd = np.where(rng.random(bd.shape) < 0.5, (M * rng.random(bd.shape) ** 4).astype(np.int64), bd)
    th = np.where(rng.random(th.shape) < 0.5, np.exp2(8 * rng.random(th.shape)).astype(np.int64) - 1, rng.integers(0, 256, th.shape))
    return pack(A, dp, sb, bd, th)
def setup_inputs_ends(rng):
    A, dp, sb, bd, th = parts(rng)
    A = np.where(rng.random((N, 8, E, 1)) < 0.1, rng.integers(16, 255, A.shape), np.where(rng.random(A.shape) < rng.choice(np.array([0.02, 0.06, 0.15]), (N, 8, 1, 1)), 0, 255))
    A[:, :, 0] = np.where(rng.random((N, 8, 16)) < 0.5, 0, 255)
    c = rng.random((N, 8, F, 1)); x = names(rng, DL, 0.6)
    z = np.where((c > 0.4) & (c < 0.6) & (rng.random(x.shape) < 0.5), 0, NONE)
    dp = np.where(rng.random(x.shape) < np.where(c < 0.6, 0.125, 0.5), x, z)
    sb = np.where(rng.random(sb.shape) < 0.7, np.where(rng.random(sb.shape) < 0.5, 0, NONE), sb)
    bd = np.where(rng.random(bd.shape) < 0.75, np.where(rng.random(bd.shape) < 0.5, 0, M - 1), bd)
    e = np.where(rng.random(th.shape) < 0.5, 0, 255); th = np.where(rng.random(th.shape) < 0.8, e, rng.integers(1, 255, th.shape))
    for j in (F, F + 1, E - 2, E - 1):
        A[:, :, j] = 255; dp[:, :, j - M] = NONE; th[:, :, j - F] = e[:, :, j - F]
    for j in (F, E - 2): dp[:, :, j - M, 15] = NONE - 1
    for j in (F + 1, E - 1): dp[:, :, j - M, 14:] = F - 1
    A[:, :, F - 1] = 0; A[:, :, F - 1, 15] = 254; dp[:, :, F - 1 - M] = NONE
    for j in (F + 2, E - 3): A[:, :, j] = 0; th[:, :, j - F] = e[:, :, j - F]
    for j in (F + 4, E - 5): A[:, :, j] = 255; dp[:, :, j - M] = NONE; th[:, :, j - F] = e[:, :, j - F]
    return pack(A, dp, sb, bd, th)
def couples(rng):
    o = np.concatenate([np.array([0, LN - 1, LN - 3, LN - 2]), 1 + rng.permutation(LN - 4)]).reshape(-1, 2)
    return np.min(o, axis=1), np.max(o, axis=1)
def setup_inputs_crowd(rng):
    A, dp, sb, bd, th = parts(rng); i = np.arange(M)
    for r in range(N):
        for g in range(8):
            kind = (r + g) % 7; z = rng.permutation(M)[:17]; A[r, g, F:] = 10; A[r, g, F + i, rng.integers(0, 16, M)] = 255
            if kind < 2:
                hub = int(z[16]); A[r, g, hub] = rng.integers(70, 121, 16); th[r, g] = rng.integers(0, 21, M)
            elif kind < 4:
                hub = F - M + int(rng.integers(0, M)); dp[r, g, hub - M] = z[:16]; A[r, g, hub] = 255
                A[r, g, z[:16]] = 255; A[r, g, z[:16], rng.permutation(16)] = rng.integers(60, 121, 16); th[r, g] = rng.integers(200, 256, M)
            elif kind == 4:
                hub = F - M + int(rng.integers(0, M)); dp[r, g, hub - M] = z[:16]; dates = rng.permutation(16)
                A[r, g, hub] = 255; A[r, g, hub, dates[:8]] = rng.integers(60, 121, 8)
                A[r, g, z[:16]] = 255; A[r, g, z[:16], np.concatenate([dates[8:], dates[8:]])] = rng.integers(60, 121, 16)
                th[r, g] = np.where(rng.random(M) < 0.5, rng.integers(0, 21, M), rng.integers(200, 256, M))
            else:
                a, b = couples(rng); n = len(a); u = 1 + rng.permutation(M - 1); u[2] = 0
                za, zb = u[:n], u[n:2 * n]; y = rng.random(n) < 0.25; da, db = 2 * rng.integers(0, 8, n), 2 * rng.integers(0, 8, n) + 1
                if kind == 5:
                    y[:2] = False; y[2] = True; da[y] = 0
                w = np.zeros(LN, np.int64); w[a] = np.arange(n); w[b] = np.arange(n)
                dt = np.zeros(LN, np.int64); dt[a] = da; dt[b] = db
                A[r, g, F:] = 10; A[r, g, F + i, dt[i >> 1]] = 255
                if kind == 5:
                    hub = za; A[r, g, hub] = rng.integers(70, 121, (n, 16)); th[r, g] = rng.integers(0, 21, M); A[r, g, za[y], 0] = 0
                    for h in (0, 1):
                        j = 2 * a[y] + h; A[r, g, F + j] = 0; A[r, g, F + j, 0] = 255; th[r, g, j] = 0
                else:
                    y[0] = True; y[1] = False; hub = F - M + 1 + rng.permutation(M - 1)[:n]; hub[1] = M
                    A[r, g, hub] = 255; A[r, g, za] = 255; A[r, g, zb] = 255
                    A[r, g, za, da] = rng.integers(60, 121, n); A[r, g, zb, db] = rng.integers(60, 121, n)
                    s = np.argsort(rng.random((n, 16)), axis=1); dp[r, g, hub - M] = NONE
                    dp[r, g, hub - M, s[:, 0]] = za; dp[r, g, hub - M, s[:, 1]] = zb
                    sb[r, g, za[y]] = za[y]; sb[r, g, zb[0]] = NONE; sb[r, g, za[1]] = NONE
                    bk = rng.random(n) < 0.25; bk[:2] = False; bk[2] = True
                    th[r, g] = np.where(bk[w[i >> 1]], rng.integers(0, 13, M), rng.integers(200, 256, M))
                hub = hub[w[i >> 1]][:, None]
            m = rng.random((M, 16)) < 0.2; m[i, rng.integers(0, 16, M)] = True
            dp[r, g, F - M:] = np.where(m, hub, NONE)
            if kind in (1, 3):
                j = 2 * int(rng.choice(np.array([0, LN - 1, rng.integers(0, LN)]))); dp[r, g, F - M + j:F - M + j + 2] = NONE
    return pack(A, dp, sb, bd, th)
def setup_inputs_chains(rng):
    A, dp, sb, bd, th = parts(rng)
    A[:, :, M:] = rng.integers(254, 256, (N, 8, F, 16)); A[:, :, :M] = rng.choice(np.array([0, 15, 16, 50, 51, 100, 101] + [253] * 20), (N, 8, M, 16))
    odd = ((np.arange(N)[:, None] + np.arange(8)) % 2 == 1)[:, :, None, None]
    x = np.where(odd & (rng.random(DL.shape) < 0.25), E + (DL - 1) * H + rng.integers(0, H, DL.shape), (DL - 1) * M + rng.integers(0, M, DL.shape))
    x = np.where(rng.random((N, 8, F, 1)) < 0.25, x[..., :1], x); k = np.arange(16)
    m = (k == rng.integers(0, 16, (N, 8, F, 1))) | (k == rng.choice(np.array([0, 7, 15]), (N, 8, F, 1)))
    dp = np.where(m, x, NONE); u = rng.integers(0, 4, SL.shape)
    own = np.concatenate([np.arange(F), E + np.arange(G)])
    sb = np.where(u == 0, NONE, np.where(u == 1, own, np.where(u == 2, E + (SL + 1) * H - 1, sb)))
    th = rng.choice(np.array([0, 16, 50, 51, 52, 100, 101, 102, 253, 254, 255]), (N, 8, M))
    return pack(A, dp, sb, bd, th)
def setup_inputs_calm(rng):
    A, dp, sb, bd, th = parts(rng); base = np.array([16, 17, 18, 19, 33, 35, 254, 255]); i = np.arange(LN)
    for r in range(N):
        for g in range(8):
            a = np.where(rng.random(LN) < 0.7, base[(r + g) % 8], rng.choice(base, LN)); z = rng.permutation(M)[:LN]
            A[r, g, z] = np.maximum(a - 64, 0)[:, None]; A[r, g, z, rng.integers(0, 16, LN)] = a
            A[r, g, F:] = 255; A[r, g, F - M + i] = 255
            dp[r, g, F - 2 * M + i] = NONE; dp[r, g, F - 2 * M + i, rng.integers(0, 16, LN)] = z
            hub = np.where(i % 2 == 1, F - M + i, z)
            for h in (0, 1):
                dp[r, g, F - M + 2 * i + h] = NONE; dp[r, g, F - M + 2 * i + h, rng.integers(0, 16, LN)] = hub
            w = i[rng.random(LN) < 0.125]; dp[r, g, F - M + 2 * w + 1, rng.integers(0, 16, len(w))] = E + rng.integers(0, H, len(w))
            th[r, g, 2 * i] = np.maximum(a - rng.choice(np.array([15, 16, 31, 32]), LN), 0); th[r, g, 2 * i + 1] = np.maximum(a - rng.choice(np.array([15, 16, 17]), LN), 0)
    return pack(A, dp, sb, bd, th)
def check_inputs(d):
    bad = []
    for k, lo, hi in (("av", 0, 255), ("dp", 0, NONE), ("sb", 0, NONE), ("bd", 0, M - 1), ("th", 0, 255)):
        x = np.asarray(d[k]).astype(np.float64)
        if not np.all((x >= lo) & (x <= hi)): bad.append("range of " + k)
        elif not np.all(x == np.floor(x)): bad.append("whole numbers in " + k)
    if np.any(LEV[np.clip(np.asarray(d["dp"]).astype(np.int64), 0, NONE)] > np.arange(F) // M): bad.append("levels of dp")
    if np.any(LEV[np.clip(np.asarray(d["sb"]).astype(np.int64), 0, NONE)] > SL): bad.append("levels of sb")
    return bad
def first(want, at):
    lo = np.full((N, 8, E), LN); n, g, i = np.nonzero(want); np.minimum.at(lo, (n, g, at[want]), i)
    return want & (np.take_along_axis(lo, np.where(want, at, 0), 2) == np.arange(LN))
def reference(av, dp, sb, bd, th):
    A = np.ascontiguousarray(av.astype(np.int32).reshape(N, 8, 16, E).transpose(0, 1, 3, 2))
    D = np.ascontiguousarray(dp.astype(np.int64).reshape(N, 8, 16, F).transpose(0, 1, 3, 2))
    S = sb.astype(np.int64); t0 = th.astype(np.int64)
    bl = np.stack([gentries(a) for a in bd]).astype(np.int64).reshape(N, 8, L - 1, N - 1, B)
    ni = np.arange(N)[:, None, None]; gi = np.arange(8)[None, :, None]
    for t in range(P):
        R = np.full((N, 8, NONE + 1, 16), 255, np.int32)
        for l in range(L):
            a = A[:, :, l * M:(l + 1) * M]
            if l > 0:
                ix = D[:, :, (l - 1) * M:l * M].reshape(N, 8, M * 16)
                a = np.minimum(a, np.min(R[ni, gi, ix].reshape(N, 8, M, 16, 16), axis=3))
            R[:, :, l * M:(l + 1) * M] = a
            if l < L - 1:
                for r in range(N):
                    for d in range(1, N):
                        q = r ^ d; h = GM[d % 3]; s = E + l * H + (d - 1) * B
                        R[r, :, s:s + B] = R[q, h[:, None], l * M + bl[q, h, l, d - 1]]
        e = np.broadcast_to(F + 2 * np.arange(LN) + (t & 1), (N, 8, LN))
        re = R[ni, gi, e]; p = np.argmax(re, axis=3); v = np.max(re, axis=3)
        f = e; q = np.full((N, 8, LN), -1); k = np.zeros((N, 8, LN), np.int64)
        for step in range(L - 1):
            go = (f < E) & (A[ni, gi, np.where(f < E, f, 0), p] != v)
            c = D[ni, gi, np.where(go, f - M, 0)]
            k1 = np.argmax(R[ni[..., None], gi[..., None], c, p[..., None]] == v[..., None], axis=3)
            to = np.take_along_axis(c, k1[..., None], 3)[..., 0]
            q = np.where(go, f, q); k = np.where(go, k1, k); f = np.where(go, to, f)
        b = np.take_along_axis(t0, e - F, 2); ok = v >= b
        wa = first((ok & (f < E)) | (~ok & (f == e)), f); wd = first(~ok & (f != e), q)
        na = np.where(ok, np.maximum(v - 16, 0), b); nd = S[ni, gi, np.where(f != e, np.where(f < E, f, f - M), 0)]
        n, g, i = np.nonzero(wa); A[n, g, f[wa], p[wa]] = na[wa]
        n, g, i = np.nonzero(wd); D[n, g, q[wd] - M, k[wd]] = nd[wd]
    return {"ya": np.ascontiguousarray(A.transpose(0, 1, 3, 2)).reshape(N, 128, E).astype(np.float32).astype(BF),
            "yd": np.ascontiguousarray(D.transpose(0, 1, 3, 2)).reshape(N, 128, F).astype(np.float32),
            "yr": np.ascontiguousarray(R[:, :, F:E].transpose(0, 1, 3, 2)).reshape(N, 128, M).astype(np.float32).astype(BF)}

@@ -1,0 +1,676 @@
+from concourse.bass import DstId, RemoteDMATransfer
+from concourse.mybir import AluOpType as Op, ActivationFunctionType as Fn
+
+M, E, G, NONE, LN, NP = 512, 2560, 384, 2944, 256, 3
+IX = 8
+DO = 1024
+DUM = 2960
+HALVES = 2
+PLAN = [("F", 112, 0), ("F", 108, 0), ("R", 96, 0), ("V", 40, 0), ("F", 104, 0), ("S", 60, 1), ("S", 64, 0), ("S", 24, 0)]
+PLANT = [("F", 56, 0), ("V", 32, 0), ("F", 56, 1), ("S", 48, 1), ("S", 64, 0)]
+SEG = [16 * (m + 1) for m in range(16)]
+SEGO = [sum(SEG[:m]) for m in range(17)]
+NVSEG = 7
+
+S_, P_ = "sbuf", "psum"
+f32, bf, f16, i32, u16 = "float32", "bfloat16", "float16", "int32", "uint16"
+BUF = {
+    "A": (bf, 2816), "TT": (bf, 2960), "U": (f32, 2960), "D": (f32, 3216), "YD": (f32, 3216), "SD": (f32, 2960),
+    "dpi": (i32, 2048), "sbi": (i32, 152), "sb2": (f16, 152), "sbh": (f16, 2432), "thi": (i32, 32), "th2": (bf, 32), "thh": (bf, 512), "thB": (bf, 512),
+    "thL": (f32, 32), "bdi": (i32, 24), "bdu": (u16, 24),
+    "GS": (bf, 9728), "SO": (f16, 8192), "SB": (bf, 4096), "PF": (f32, 4096), "PR": (f16, 4096), "X16": (f16, 512),
+    "LU": (u16, 2048), "DLU": (u16, 288), "OLU": (u16, 256),
+    "R16": (bf, 1024), "R8": (bf, 1024), "R0": (bf, 1536), "RM": (bf, 256), "CS": (bf, 2176), "NE": (bf, 2176), "NS": (bf, 2176),
+    "stg": (bf, 12 * 96), "land": (bf, 12 * 96), "yrs": (bf, 512),
+    "VP": (f32, 256), "Ut": (f32, 256), "Tt": (bf, 256), "k2": (f16, 256), "k2a": (f16, 256), "k2b": (f16, 256), "k2c": (f16, 256),
+    "X32": (f32, 512), "S15k": (f16, 128), "nIk": (f16, 128), "nI": (bf, 128), "n16": (bf, 128), "X": (bf, 256), "X2": (bf, 256), "Y": (f16, 256), "KM": (bf, 1024), "SV": (f32, 256), "SW": (f32, 256),
+    "FL": (u16, 80), "H": (f32, 168), "Z": (f32, 160), "MV": (f32, 80), "FQ": (f32, 160), "KO": (f32, 80), "KQ": (f32, 80), "CT": (f32, 80),
+    "E0": (f32, 32), "E0u": (u16, 32), "C32": (f32, 32), "C33": (f32, 32), "W": (f32, 32), "w1": (f32, 32), "w2": (f32, 32), "w3": (f32, 32),
+    "w4": (f32, 32), "ok": (f32, 16), "idl": (f32, 16), "own": (f32, 16), "nwd": (f32, 16), "C34": (f32, 32), "w5": (f32, 16), "w6": (f32, 32), "w7": (f32, 32),
+    "off": (u16, 32), "tg": (u16, 32), "fu": (u16, 16), "kou": (u16, 16), "exu": (u16, 16), "enu": (u16, 4), "XI": (f16, 256),
+    "d1": (bf, 256), "d2": (bf, 256), "d3": (bf, 256), "d4": (bf, 256), "dA": (bf, 256), "oA": (bf, 256), "oD": (f32, 256),
+    "KL": (bf, 256), "ZD": (f32, 256),
+    "pi": (i32, 4), "pj": (i32, 4), "col": (f32, 16), "JmP": (f32, 128), "JA": (f32, 128), "JB": (f32, 256), "J512": (f32, 512), "J5h": (f16, 512),
+    "m16": (f32, 16), "t5": (f32, 80), "m5": (f32, 80),
+    "I": (bf, 128), "BO": (bf, 128), "BOh": (f16, 128), "BOw": (bf, 128), "S15": (f16, 128), "P1": (bf, 128), "P2": (bf, 128),
+    "V0": (f32, 128), "V1": (f32, 128), "S0": (f32, 128), "S1": (f32, 128), "G8": (bf, 128), "G8h": (f16, 128), "G8n": (f16, 128),
+    "CW": (bf, 128), "one": (bf, 512), "NEG": (bf, 256), "DGr": (bf, 256), "tri": (bf, 16),
+}
+SIZE = {f32: 4, i32: 4, bf: 2, f16: 2, u16: 2}
+GAT, FAR, WAKE, HOLD, GAP = 1.56, 3500.0, 60.0, 0.5, 300.0
+BIG = 12582912.0
+CUTS = [0, 10, 13, 15, 16]
+LENGTH = [0.0]
+HOME, _fill = {}, {}
+for _k, (_d, _n) in BUF.items():
+    if _n <= 128 and _k not in ("bdi", "thi", "th2"):
+        HOME[_k] = ("sm_" + _d, _fill.get(_d, 0))
+        _fill[_d] = _fill.get(_d, 0) + -(-_n // 16) * 16
+SCRATCH = {k: (S_, [128, n], d) for k, (d, n) in BUF.items() if k not in HOME}
+for _d, _n in _fill.items():
+    SCRATCH["sm_" + _d] = (S_, [128, _n], _d)
+for _b in range(8):
+    SCRATCH["ps%d" % _b] = (P_, [128, 512], f32)
+NDMA = 24
+SEMAPHORES = ["sv", "ss", "sp", "sg", "sent"] + ["dm%d" % k for k in range(NDMA)] + ["ar%d" % k for k in range(12)]
+ESEM = {"v": "sv", "s": "ss", "p": "sp", "g": "sg"}
+
+
+def V(name, lo=0, hi=None, st=1, p0=0, p1=128):
+    return (name, lo, BUF[name][1] if hi is None else hi, st, p0, p1)
+
+
+def N_(name, lo, n, st=1):
+    return (name, lo, lo + (n - 1) * st + 1, st, 0, 128)
+
+
+def IND(win, off):
+    return ("*", win, off)
+
+
+def build(rank, T, send):
+    ops, chain = [], []
+
+    def ap(x):
+        if not isinstance(x, tuple):
+            return x
+        if x[0] == "*":
+            return ap(x[1]).indirect(ap(x[2]))
+        if x[0] == "@":
+            return x[1]
+        name, o = HOME.get(x[0], (x[0], 0))
+        return T[name][x[4]:x[5], o + x[1]:o + x[2]:x[3]] if x[3] != 1 else T[name][x[4]:x[5], o + x[1]:o + x[2]]
+
+    def span(q, out, ins, kind, two):
+        if kind == "x":
+            return (0.0, 0.0)
+        if kind == "r":
+            return (300.0, 300.0 + FAR)
+        if kind == "d":
+            x = out if out[0] != "@" else ins[0]
+            return (60.0, 2000.0 + (x[5] - x[4]) * (x[2] - x[1]) * SIZE[BUF[x[0]][0]] / 250.0)
+        vs = [x for x in [out] + ins if isinstance(x, tuple)]
+        ind = [x for x in vs if x[0] == "*"]
+        if ind:
+            c = 50.0 + 16 * (ind[0][2][2] - ind[0][2][1]) * (3.8 if out[0] == "*" else GAT)
+        else:
+            n = len(range(out[1], out[2], out[3]))
+            big = [x for x in vs if x[2] - x[1] > 1 or n == 1]
+            ps = any(x[0].startswith("ps") for x in big)
+            if q == "p":
+                c = 30.0 + max(64, n) * (4 if BUF[ins[0][0]][0] == f32 else 1)
+            elif q == "g":
+                c = 130.0 + 2 * n
+            elif q == "s":
+                c = 65.0 + max(64, n)
+            else:
+                half = 0.5 if not ps and all(SIZE[BUF[x[0]][0]] == 2 for x in big) else 1.0
+                c = 50.0 + max(64, n * half * (2 if two and not ps else 1))
+        return (c, c)
+
+    def add(q, call, out, ins, kind="c", two=False):
+        rd, wr = [], []
+        for x in ins:
+            if isinstance(x, tuple) and x[0] == "*":
+                rd += [x[1], x[2]]
+            elif isinstance(x, tuple) and x[0] != "@":
+                rd.append(x)
+        if out is not None and out[0] == "*":
+            rd += [out[1], out[2]]
+            wr.append(out[1])
+        elif out is not None and out[0] != "@":
+            wr.append(out)
+        ops.append((q, call, rd, wr, kind, span(q, out, ins, kind, two)))
+
+    def tt(o, a, b, op): add("v", lambda g: g.vector.tensor_tensor(ap(o), ap(a), ap(b), op), o, [a, b], two=True)
+    def ts(o, a, s1, op0): add("v", lambda g: g.vector.tensor_scalar(ap(o), ap(a), ap(s1), None, op0), o, [a, s1])
+    def ts2(o, a, s1, op0, s2, op1): add("v", lambda g: g.vector.tensor_scalar(ap(o), ap(a), ap(s1), ap(s2), op0, op1), o, [a, s1, s2])
+    def cp(o, a): add("v", lambda g: g.vector.tensor_copy(ap(o), ap(a)), o, [a])
+    def ms(o, c): add("v", lambda g: g.vector.memset(ap(o), c), o, [])
+    def tr(o, a): add("v", lambda g: g.vector.transpose(ap(o), ap(a)), o, [a])
+    def scan(o, a, b, op0, op1): add("v", lambda g: g.vector.tensor_tensor_scan(ap(o), ap(a), ap(b), 0.0, op0, op1), o, [a, b])
+    def act(o, a, bias=0.0, scale=1.0, fn=Fn.Identity):
+        add("s", lambda g: g.scalar.activation(ap(o), ap(a), fn, bias=ap(bias), scale=scale), o, [a, bias])
+    def mm(o, l, r, st=True, en=True): add("p", lambda g: g.tensor.matmul(ap(o), ap(l), ap(r), st, en), o, [l, r])
+    def iota(o, pat, base, ch):
+        if BUF[o[0]][0] == i32:
+            add("g", lambda g: g.iota(ap(o), pat, base, ch), o, [])
+        else:
+            add("g", lambda g: g.iota(ap(o), pat, base, ch, allow_small_or_imprecise_dtypes=True), o, [])
+    def dma(q, o, a):
+        add(q, (lambda g: g.sync.dma_start(ap(o), ap(a))) if q == "y" else (lambda g: g.scalar.dma_start(ap(o), ap(a))), o, [a], "d")
+    def PS(b, lo, n, st=1): return ("ps%d" % b, lo, lo + (n - 1) * st + 1, st, 0, 128)
+    def C(j): return V("col", j, j + 1)
+    def ext(x): return ("@", x)
+    AD, SU, MU, MX, MN, EQ, NQ = Op.add, Op.subtract, Op.mult, Op.max, Op.min, Op.is_equal, Op.not_equal
+
+    dma("y", V("A", 0, M), ext(T.av[:, 0:M]))
+    dma("s", V("bdi"), ext(T.bd[:, :]))
+    dma("y", V("dpi", 0, M), ext(T.dp[:, 0:M]))
+    dma("s", V("A", M, E), ext(T.av[:, M:E]))
+    dma("y", V("dpi", M, 2 * M), ext(T.dp[:, M:2 * M]))
+    dma("y", V("dpi", 2 * M, 4 * M), ext(T.dp[:, 2 * M:4 * M]))
+    dma("y", V("thi"), ext(T.th[:, :]))
+    dma("y", V("sbi"), ext(T.sb[:, :]))
+
+    def fill_s(name, lo, hi, c):
+        for a in range(lo, hi, M):
+            n = min(M, hi - a)
+            act(N_(name, a, n), N_("one", 0, n), 0.0, c)
+
+    def fill_g(name, lo, hi, c):
+        for a in range(lo, hi, 256):
+            n = min(256, hi - a)
+            iota(N_(name, a, n), [[0, n]], c, 0)
+
+    ms(V("one"), 1.0)
+    iota(V("pi", 0, 1), [[0, 1]], 0, 1)
+    iota(V("JmP"), [[1, 128]], 0, -1)
+    iota(V("JA"), [[1, 8], [0, 16]], 0, 0)
+    fill_s("TT", M, E, 0.0); fill_s("TT", E, 2960, 128.0)
+    fill_s("R8", 0, 1024, -0.0625); ms(V("R8", 0, None, 8), 512.0)
+    fill_s("R0", 0, 1536, 0.0); ms(V("R0", 0, None, 16), 512.0)
+    fill_s("R16", 0, 1024, -0.0625); ms(V("R16", 0, None, 16), 512.0)
+    ts(V("pi", 1, 2), V("pi", 0, 1), 4, Op.arith_shift_right)
+    ts(V("pi", 2, 3), V("pi", 0, 1), 15, Op.bitwise_and)
+    cp(V("col", 0, 3), V("pi", 0, 3))
+    cp(V("bdu"), V("bdi"))
+
+    def exchange(k):
+        add("g", send(k), None, [N_("stg", 96 * k, 96)], "r")
+
+    def ghosts(k, l):
+        add("x", k, N_("land", 96 * k, 96), [], "x")
+        for d, P in ((1, "P1"), (2, "P2"), (3, "I")):
+            mm(PS(4, 32 * (d - 1), 32), V(P), N_("land", 96 * k + 32 * (d - 1), 32))
+        act(N_("TT", E + 96 * l, 96), PS(4, 0, 96), -127.0)
+
+    def release0(t):
+        cp(N_("stg", 96 * 4 * t, 96), IND(V("A", 0, M), V("bdu", 0, 6)))
+        exchange(4 * t)
+        ts(V("TT", 0, M), V("A", 0, M), -127.0, AD)
+
+    release0(0)
+    iota(V("JB"), [[0, 16], [1, 16]], 0, 0)
+    iota(V("m16"), [[1, 16]], 0, 0)
+    iota(V("t5"), [[0, 16], [1, 5]], 0, 0)
+    iota(V("m5"), [[16, 16], [0, 5]], 0, 0)
+    iota(V("J512"), [[1, 512]], 0, 0)
+    ts(C(3), C(2), 8.0, Op.is_ge)
+    ts(C(4), C(2), 8.0, Op.is_lt)
+    ts2(V("V0"), V("JmP"), -8.0, EQ, C(3), MU)
+    ts2(V("V1"), V("JmP"), 0.0, EQ, C(3), MU)
+    ts2(V("S0"), V("JmP"), 0.0, EQ, C(4), MU)
+    ts2(V("S1"), V("JmP"), 8.0, EQ, C(4), MU)
+    ts(N_("D", IX + M, M), V("dpi", 0, M), -float(DO), AD)
+
+    def split(plan):
+        return sum(x[1] for x in plan if x[0] == "F")
+
+    def parts(l):
+        plan = PLAN if l < 4 else PLANT
+        ks = [x[1] for x in plan if x[0] == "F"]
+        return [(sum(ks[:i]), k) for i, k in enumerate(ks)] if l == 1 else [(0, sum(ks))]
+
+    def lists(l, par):
+        plan, st = (PLAN, 1) if l < 4 else (PLANT, 2)
+        c0 = IX + l * M + (par if l == 4 else 0)
+        nf, n, lu, b = split(plan), (M if l < 4 else LN), (l - 1) * M, 2 + l % 2
+        if l < 4 and any(x[0] == "R" for x in plan):
+            ts(N_("DLU", 96 * (l - 1), 96), IND(N_("D", IX + l * M, M), V("bdu", 6 * l, 6 * l + 6)), float(DO), AD)
+        if n > nf:
+            ts(N_("LU", lu + nf, n - nf), N_("D", c0 + nf * st, n - nf, st), float(DO), AD)
+        for i, (a, k) in enumerate(parts(l) if nf else []):
+            h, bb = k // 2, b if i % 2 == 0 else 5 - b
+            for j, (a0, a1) in enumerate((("S0", "S1"), ("V0", "V1"))):
+                mm(PS(bb, j * h, h), V(a0), N_("D", c0 + a * st, h, 2 * st), True, False)
+                mm(PS(bb, j * h, h), V(a1), N_("D", c0 + (a + 1) * st, h, 2 * st), False, True)
+            ts(N_("LU", lu + a, k), PS(bb, 0, k), float(DO), AD)
+
+    def own_keys(l, par):
+        n, st = (M, 1) if l < 4 else (LN, 2)
+        mm(PS(l % 2, 0, n), V("CW", p1=64), V("one", 0, n, p1=64), True, False)
+        mm(PS(l % 2, 0, n), V("I"), N_("A", l * M + (par if l == 4 else 0), n, st), False, True)
+
+    lists(1, 0)
+    ts(V("I"), V("JmP"), 0.0, EQ)
+    ts2(C(5), C(1), -32.0, MU, 112.0, AD)
+    ts(V("P1"), V("JmP"), C(5), EQ)
+    ts2(C(6), C(1), 0.0, Op.is_gt, 128.0, MU)
+    ts2(C(6), C(1), -32.0, MU, C(6), AD)
+    ts(V("P2"), V("JmP"), C(6), EQ)
+    ms(V("CW", p1=64), 0.0); ms(V("CW", p1=1), -128.0); ms(V("CW", p0=32, p1=33), 0.03125)
+    own_keys(1, 0)
+
+    def late_setup(step):
+        if step == 0:
+            ts(N_("D", IX + 2 * M, M), V("dpi", M, 2 * M), -float(DO), AD)
+            fill_g("U", 0, IX + M, 1000); fill_g("U", IX + 4 * M, 2960, 1000)
+            fill_g("D", 0, IX + M, 0); fill_g("D", IX + E, 3216, 0)
+            fill_g("A", E, 2816, 0)
+            fill_g("SD", 0, IX, 0); fill_g("SD", IX + 4 * M, IX + E, 0); fill_g("SD", IX + NONE, 2960, 0)
+            fill_g("CS", 0, 2176, 0); fill_g("H", 0, 168, 0)
+            ts(V("BO"), V("JA"), C(1), EQ)
+            ts(V("BOh"), V("JA"), C(1), EQ)
+            ts2(V("BOw"), V("JA"), C(1), EQ, float(DO + IX), MU)
+            ts(C(7), C(2), 15.0, EQ)
+            ts2(V("S15"), V("JA"), C(1), EQ, C(7), MU)
+            ts(V("G8"), V("JA"), C(0), EQ)
+            ts(V("G8h"), V("JA"), C(0), EQ)
+            ts2(V("G8n"), V("JA"), C(0), EQ, -1.0, MU)
+            ts2(V("NEG"), V("JB"), C(2), NQ, -4096.0, MU)
+            ts2(C(8), C(2), -1.0, MU, 15.0, AD)
+            ts(V("DGr"), V("JB"), C(8), EQ)
+            ts2(V("tri"), V("JB", 0, 16), C(8), Op.is_le, 0.5, MU)
+            ts2(C(9), C(2), -1.0, MU, -24577.0, AD)
+            ts2(C(10), C(2), 0.0625, MU, 0.0625, AD)
+            ts(V("S15k"), V("S15"), 2048.0, MU)
+            ts(V("nIk"), V("I"), -2048.0, MU)
+            ts(V("nI"), V("I"), -1.0, MU)
+            ts(V("n16"), V("I"), -16.0, MU)
+            ms(V("RM"), 0.0); ms(V("RM", 0, None, 16), -8192.0)
+            cp(V("th2"), V("thi"))
+            dma("y", V("thh", p1=8), V("th2"))
+            cp(V("J5h", p1=8), V("J512", p1=8))
+            ts(V("sb2"), V("sbi"), -float(DO), AD)
+            dma("y", V("sbh", p1=8), V("sb2"))
+            mm(PS(5, 0, M), V("G8", p1=8), V("thh", p1=8))
+            act(V("thB"), PS(5, 0, M), -127.0)
+            for j in range(5):
+                n = M if j < 4 else G
+                b = 6 + j % 2
+                mm(PS(b, 0, n), V("G8h", p1=8), V("sbh", j * M, j * M + n, p1=8), True, False)
+                mm(PS(b, 0, n), V("G8n", p1=8), V("J5h", 0, n, p1=8), False, True)
+                nm = j * M if j < 4 else E
+                act(N_("SD", IX + nm, n), PS(b, 0, n), float(DO - nm))
+        if step == 1:
+            ts(N_("D", IX + 3 * M, M), V("dpi", 2 * M, 3 * M), -float(DO), AD)
+            ts(N_("D", IX + 4 * M, M), V("dpi", 3 * M, 4 * M), -float(DO), AD)
+        if step == 2:
+            ts2(V("w1", 0, 16), V("m16"), 16.0, MU, C(2), AD)
+            for par in (0, 1):
+                ts2(N_("E0", 16 * par, 16), V("w1", 0, 16), 2.0, MU, float(4 * M + IX + par), AD)
+            cp(V("E0u"), V("E0"))
+            ts(V("C33", 0, 16), V("w1", 0, 16), float(E), AD)
+            ts(V("C33", 16, 32), V("w1", 0, 16), float(DUM), AD)
+            ts(V("w3", 0, 16), V("C33", 0, 16), float(IX), AD)
+            cp(V("w3", 16, 32), V("C33", 16, 32))
+            ts(V("C34"), V("C33"), 0.5, MU)
+            ms(V("C32", 0, 16), IX + 1023.5); ms(V("C32", 16, 32), float(IX + E))
+            ts2(V("t5"), V("t5"), -1.0, AD, 0.0, MX)
+            ts2(V("t5"), V("t5"), 256.0, MU, C(2), AD)
+            tt(V("CT"), V("t5"), V("m5"), AD)
+            ts2(V("exu"), V("m16"), -1.0, MU, 15.0, AD)
+            ts2(C(11), C(2), 1.0, AD, 8.0, MU)
+            ts2(C(12), C(2), 2.0, AD, C(11), MU)
+            ms(V("enu"), 0)
+            for j in (0, 1):
+                ts(V("enu", j, j + 1), C(12), -1.0, AD)
+            for m in range(16):
+                cp(N_("CS", SEGO[m], 16), V("tri"))
+
+    def level(t, l, fill):
+        plan, n = (PLAN, M) if l < 4 else (PLANT, LN)
+        nf, lu, win = split(plan), (l - 1) * M, V("TT", 0, NONE + 1)
+        fo, so = 0, nf
+        done, tail = {"F": 0, "S": nf}, []
+
+        def cols(j):
+            a, kk = [x for x in parts(l) if x[0] <= fo][-1]
+            return N_("LU", lu + a + j * (kk // 2) + (fo - a) // 2, k // 2)
+
+        def finish(c, k, ends):
+            u = N_("U", IX + l * M + c, k) if l < 4 else N_("Ut", c, k)
+            tt(u, ends, PS(l % 2, c, k), MN)
+            if l == 4 or c + k == n:
+                ts(N_("X16", c, k), u, 1536.484375, AD)
+                if l < 4:
+                    tail.append((c, k))
+            else:
+                ts2(N_("X32", c, k), u, 0.484375, AD, BIG, AD)
+
+        for j, (kind, k, fin) in enumerate(plan):
+            if kind == "F":
+                e0, e = 8 * fo, 8 * k
+                act(N_("PF", e0, e), IND(win, cols(0)), -0.5)
+            elif kind == "S":
+                act(N_("GS", 16 * so, 16 * k), IND(win, N_("LU", lu + so, k)))
+            elif kind == "R":
+                act(N_("GS", 8192, 1536), IND(win, N_("DLU", 96 * (l - 1), 96)), 127.0)
+            if kind != "V":
+                chain.append(len(ops) - 1)
+            if j == 0:
+                fill()
+            if kind == "F":
+                tt(N_("PR", e0, e), IND(win, cols(1)), N_("PF", e0, e), MN)
+                scan(N_("SO", e0, e), N_("R8", 0, e), N_("PR", e0, e), AD, MN)
+                fo += k
+                if fin or fo == nf:
+                    finish(done["F"], fo - done["F"], N_("SO", 8 * done["F"] + 7, fo - done["F"], 8))
+                    done["F"] = fo
+            elif kind in "SV":
+                if kind == "V":
+                    cp(N_("GS", 16 * so, 16 * k), IND(win, N_("LU", lu + so, k)))
+                scan(N_("SO", 16 * so, 16 * k), N_("R16", 0, 16 * k), N_("GS", 16 * so, 16 * k), AD, MN)
+                so += k
+                if fin or so == n:
+                    finish(done["S"], so - done["S"], N_("SO", 16 * done["S"] + 15, so - done["S"], 16))
+                    done["S"] = so
+            else:
+                scan(N_("SB", 0, 1536), N_("R0", 0, 1536), N_("GS", 8192, 1536), AD, MN)
+                x = 4 * t + l
+                tt(N_("stg", 96 * x, 96), IND(N_("A", l * M, M), V("bdu", 6 * l, 6 * l + 6)), N_("SB", 15, 96, 16), MN)
+                exchange(x)
+        if l < 4:
+            c, k = tail[0]
+            act(N_("TT", l * M, c), N_("X32", 0, c), -BIG)
+            ts(N_("TT", l * M + c, k), N_("X16", c, k), -1536.0, AD)
+
+        if l < 4 and not any(x[0] == "R" for x in plan):
+            ts(N_("stg", 96 * (4 * t + l), 96), IND(N_("TT", l * M, M), V("bdu", 6 * l, 6 * l + 6)), 127.0, AD)
+            exchange(4 * t + l)
+
+    def odd_tops():
+        for a, n in ((0, 1536), (1536, 1536), (3072, 1024)):
+            add("v", lambda g, a=a, n=n: g.vector.tensor_tensor_scan(ap(N_("SB", a, n)), ap(N_("R0", 0, n)), ap(N_("GS", a, n)), 0.0, AD, MN),
+                N_("SB", a, n), [N_("R0", 0, n), N_("GS", a, n), N_("A", 0, 16)])
+        tt(N_("yrs", 1, LN, 2), N_("SB", 15, LN, 16), N_("A", 4 * M + 1, LN, 2), MN)
+
+    for t in range(NP):
+        par, last = t & 1, t == NP - 1
+        if t == 0:
+            late_setup(0)
+        ghosts(4 * t, 0)
+        for l in range(1, 5):
+            def fill(l=l):
+                if t == 0 and l < 3:
+                    late_setup(l)
+                if l < 4:
+                    own_keys(l + 1, par)
+                    lists(l + 1, par)
+                elif last:
+                    ts(V("OLU"), N_("D", IX + 4 * M + 1, LN, 2), float(DO), AD)
+            level(t, l, fill)
+            if l < 4:
+                ghosts(4 * t + l, l)
+        hn = LN // HALVES
+        hs = [(h, h * hn, h * hn // 16, hn // 16) for h in range(HALVES)]
+        for h in hs:
+            def Hf(name): return N_(name, h[1], hn)
+            ts2(Hf("k2"), Hf("X16"), 16.0, MU, C(9), AD)
+            ts(Hf("Tt"), Hf("X16"), -1536.0, AD)
+            tr(Hf("k2a"), Hf("k2"))
+            scan(Hf("k2b"), N_("RM", 0, hn), Hf("k2a"), AD, MX)
+            tr(Hf("k2c"), Hf("k2b"))
+            mm(PS(4 + h[0], 0, hn), V("nIk"), Hf("k2"), True, False)
+            mm(PS(4 + h[0], 0, hn), V("I"), Hf("Tt"), False, False)
+            mm(PS(4 + h[0], 0, hn), V("S15k"), Hf("k2c"), False, True)
+            act(Hf("VP"), PS(4 + h[0], 0, hn))
+            act(Hf("d1"), PS(4 + h[0], 0, hn), -256.0, fn=Fn.Relu)
+        act(N_("H", 1, 16, 5), N_("E0", 16 * par, 16))
+        if last:
+            act(V("yrs", 0, M, 2), V("Tt"), 127.0)
+            for j in range(16):
+                act(N_("GS", 256 * j, 256), IND(V("TT", 0, NONE + 1), N_("OLU", 16 * j, 16)), 127.0)
+
+        def aside(s):
+            if s == 1:
+                act(V("d2"), V("Tt"), -111.0, -1.0, fn=Fn.Relu)
+                mm(PS(6, 0, LN), V("I"), V("thB", par, M, 2), True, False)
+                mm(PS(6, 0, LN), V("nI"), V("Tt"), False, False)
+                mm(PS(6, 0, LN), V("nI"), V("d1"), False, True)
+                act(V("d3"), PS(6, 0, LN), fn=Fn.Relu)
+            if s == 2:
+                mm(PS(7, 0, LN), V("nI"), V("d2"), True, False)
+                mm(PS(7, 0, LN), V("nI"), V("d1"), False, False)
+                mm(PS(7, 0, LN), V("n16"), V("d3"), False, True)
+                act(V("d4"), PS(7, 0, LN), 16.0, fn=Fn.Relu)
+                ts(V("w5"), N_("H", 2, 16, 5), 0.0, NQ)
+                mm(PS(6, 0, LN), V("I"), V("NEG"), True, False)
+                mm(PS(6, 0, LN), V("BO"), V("d3"), False, True)
+                scan(V("SW"), V("RM"), PS(6, 0, LN), AD, MX)
+                ts(V("ok"), N_("SW", 15, 16, 16), 0.0, Op.is_gt)
+            if s == 3:
+                mm(PS(6, 0, LN), V("I"), V("d3"), True, False)
+                mm(PS(6, 0, LN), V("nI"), V("d4"), False, True)
+                act(V("dA"), PS(6, 0, LN))
+                tt(V("W", 16, 32), V("w5"), V("ok"), MU)
+                ts2(V("nwd"), V("W", 16, 32), -1.0, MU, 1.0, AD)
+
+        for s in range(1, 5):
+            def lst(h): return N_("E0u", 16 * par + h[2], h[3]) if s == 1 else N_("FL", 16 * (s - 1) + h[2], h[3])
+            for h in hs:
+                if s == 1:
+                    tt(N_("X", h[1], hn), N_("Ut", h[1], hn), N_("VP", h[1], hn), SU)
+                else:
+                    tt(N_("X", h[1], hn), IND(V("U"), lst(h)), N_("VP", h[1], hn), SU)
+                act(N_("X2", h[1], hn), N_("X", h[1], hn), 1.0, fn=Fn.Relu)
+                mm(PS(3 - h[0], 0, hn), V("I"), N_("NEG", 0, hn), True, False)
+                mm(PS(1 - h[0], 0, hn), V("BO"), N_("X2", h[1], hn))
+            for h in hs:
+                km = N_("KM", LN * (s - 1) + h[1], hn)
+                ts(km, PS(1 - h[0], 0, hn), C(10), EQ)
+                mm(PS(3 - h[0], 0, hn), V("BOw"), km, False, False)
+                tt(N_("Y", h[1], hn), IND(V("D", 0, DUM), lst(h)), km, MU)
+                mm(PS(3 - h[0], 0, hn), V("BOh"), N_("Y", h[1], hn), False, True)
+            if HALVES == 1:
+                aside(s)
+            for h in hs:
+                scan(N_("SV", h[1], hn), N_("RM", 0, hn), PS(3 - h[0], 0, hn), AD, MX)
+                ends = N_("SV", h[1] + 15, h[3], 16)
+                if s < 4:
+                    cp(N_("FL", 16 * s + h[2], h[3]), ends)
+                    act(N_("H", 1 + s + 5 * h[2], h[3], 5), ends)
+            if s == 4:
+                cp(N_("H", 5, 16, 5), N_("SV", 15, 16, 16))
+            if HALVES > 1:
+                aside(s)
+            if last and s == 1:
+                for a in range(IX + M, IX + E, M):
+                    act(N_("YD", a, M), N_("D", a, M), float(DO))
+                act(V("YD", 0, IX + M), V("D", 0, IX + M))
+                act(V("YD", IX + E), V("D", IX + E))
+        ts(V("MV"), N_("H", 1, 80), 0.0, NQ)
+        ts(N_("Z", 0, 80), N_("H", 1, 80), 0.0, EQ)
+        tt(N_("H", 81, 80), N_("H", 0, 80), V("MV"), MU)
+        ts(N_("Z", 80, 80), N_("H", 1, 80), 0.0, EQ)
+        scan(V("FQ"), V("Z"), N_("H", 1, 160), MU, AD)
+        fq = N_("FQ", 4, 32, 5)
+        ts(V("own"), N_("FQ", 4, 16, 5), float(E + IX), Op.is_lt)
+        tt(V("w1"), fq, V("C32"), SU)
+        tt(V("W", 0, 16), V("own"), V("nwd"), MU)
+        tt(V("w2"), V("w1"), V("W"), MU)
+        tt(V("idl"), V("w2", 0, 16), V("w2", 16, 32), AD)
+        tt(V("XI"), IND(V("idl"), V("exu")), V("DGr"), MU)
+        mm(PS(7, 0, LN), V("BOh"), V("XI"))
+        mm(PS(6, 0, LN), V("BOh"), V("XI"))
+        dw = V("YD") if last else V("D")
+        tt(V("w6"), fq, V("w3"), SU)
+        tt(V("w7"), V("w6"), V("W"), MU)
+        tt(V("w4"), V("w7"), V("C33"), AD)
+        cp(V("tg"), V("w4"))
+        tt(V("KO"), V("MV"), V("CT"), MU)
+        cp(V("fu"), N_("FQ", 4, 16, 5))
+        scan(V("KQ"), V("Z", 0, 80), V("KO"), MU, AD)
+        cp(V("kou"), N_("KQ", 4, 16, 5))
+        for m in range(NVSEG, 16):
+            act(N_("NE", SEGO[m], SEG[m]), PS(7, LN - SEG[m], SEG[m]), V("idl", m, m + 1), -1.0, fn=Fn.Abs)
+            chain.append(len(ops) - 1)
+        act(V("oA"), IND(V("A"), V("tg", 0, 16)))
+        act(V("oD"), IND(dw, V("tg", 16, 32)))
+        act(V("KL"), IND(V("KM"), V("kou")))
+        for m in range(NVSEG):
+            ts(N_("NE", SEGO[m], SEG[m]), PS(6, LN - SEG[m], SEG[m]), V("idl", m, m + 1), NQ)
+        for a, b in zip(CUTS, CUTS[1:]):
+            add("v", lambda g, a=a, b=b: g.vector.tensor_tensor_scan(ap(V("NS", SEGO[a], SEGO[b])), ap(V("NE", SEGO[a], SEGO[b])),
+                ap(V("CS", SEGO[a], SEGO[b])), 0.0, MN, MX), V("NS", SEGO[a], SEGO[b]), [V("NE", SEGO[a], SEGO[b]), V("CS", SEGO[a], SEGO[b])])
+        tt(V("w1"), IND(V("NS"), V("enu", 0, 2)), V("w7"), MU)
+        tt(V("w2"), V("w1"), V("C34"), AD)
+        ts(V("off"), V("w2"), 2.0, MU)
+
+        def write_a():
+            tt(IND(V("A"), V("off", 0, 16)), V("oA"), V("dA"), AD)
+
+        def write_d():
+            tt(IND(dw, V("off", 16, 32)), V("oD"), V("ZD"), AD)
+
+        if not last:
+            tt(V("ZD"), IND(V("SD"), V("fu")), V("KL"), MU)
+            write_a()
+            release0(t + 1)
+            write_d()
+            own_keys(1, 0)
+            lists(1, 0)
+        else:
+            tt(V("ZD"), IND(V("SD"), V("fu")), V("KL"), MU)
+            write_d()
+            dma("y", ext(T.yd[:, :]), N_("YD", IX + M, 4 * M))
+            write_a()
+            dma("y", ext(T.ya[:, :]), V("A", 0, E))
+            odd_tops()
+            dma("y", ext(T.yr[:, :]), V("yrs"))
+    return ops, chain
+
+
+def arrange(ops, deps, chain):
+    n = len(ops)
+    soft = {b: a for a, b in zip(chain, chain[1:]) if a not in deps[b]}
+    deps = [d | {soft[i]} if i in soft else d for i, d in enumerate(deps)]
+    after = [[] for _ in range(n)]
+    for i in range(n):
+        for j in deps[i]:
+            after[j].append(i)
+    prio = [0.0] * n
+    for i in range(n - 1, -1, -1):
+        prio[i] = ops[i][5][1] + max([prio[k] + WAKE for k in after[i]], default=0.0)
+    left, ready = [len(d) for d in deps], [0.0] * n
+    free = {q: 0.0 for q in "vspgyx"}
+    open_ = {q: [i for i in range(n) if ops[i][0] == q and not deps[i]] for q in free}
+    order = []
+    while len(order) < n:
+        pick = None
+        for q, cand in open_.items():
+            if not cand:
+                continue
+            t = max(free[q], min(ready[i] for i in cand))
+            b = max((i for i in cand if ready[i] <= t), key=lambda i: (prio[i], -i))
+            for h in cand:
+                if t < ready[h] < t + HOLD * ops[b][5][0] and prio[h] > prio[b] + GAP:
+                    b = h
+            s = max(free[q], ready[b])
+            if pick is None or s < pick[0]:
+                pick = (s, q, b)
+        s, q, b = pick
+        open_[q].remove(b)
+        order.append(b)
+        free[q] = s + ops[b][5][0]
+        for k in after[b]:
+            ready[k] = max(ready[k], s + ops[b][5][1] + (0.0 if (q == "p" and ops[k][0] == "p") or soft.get(k) == b else WAKE))
+            left[k] -= 1
+            if not left[k]:
+                open_[ops[k][0]].append(k)
+        LENGTH[0] = s + ops[b][5][1]
+    return order
+
+
+def emit(g, T, steps, landed, sent):
+    ops, chain = steps
+    seen, deps, sends = {}, [], []
+    for i, (q, call, rd, wr, kind, _) in enumerate(ops):
+        d = set()
+        if kind == "r":
+            d.update(sends[-1:])
+            sends.append(i)
+        if kind == "x":
+            d.add(sends[call])
+        for views, w in ((rd, False), (wr, True)):
+            for x in views:
+                psum = x[0].startswith("ps")
+                for (j, lo, hi, p0, p1, jw) in seen.get(x[0], []):
+                    meet = lo < x[2] and x[1] < hi and p0 < x[5] and x[4] < p1
+                    if (meet and (w or jw)) or (psum and (ops[j][0] != q or q == "p")):
+                        d.add(j)
+        for views, w in ((rd, False), (wr, True)):
+            for x in views:
+                old = seen.get(x[0], [])
+                if w:
+                    old = [a for a in old if not (x[3] == 1 and x[1] <= a[1] and a[2] <= x[2] and x[4] <= a[3] and a[4] <= x[5] and a[0] in d)]
+                seen[x[0]] = old + [(i, x[1], x[2], x[4], x[5], w)]
+        d.discard(i)
+        deps.append(d)
+    order = arrange(ops, deps, chain)
+    place = {i: k for k, i in enumerate(order)}
+    upto, need, marked = {}, {}, set()
+    for i in order:
+        q, kind = ops[i][0], ops[i][4]
+        best = {}
+        for j in deps[i]:
+            key = ops[j][0] if ops[j][4] == "c" else j
+            if key not in best or place[j] > place[best[key]]:
+                best[key] = j
+        w = []
+        if kind != "x":
+            for key, j in best.items():
+                if ops[j][4] != "r" and not (q == "p" and key == "p") and upto.get((q, key), -1) < place[j]:
+                    upto[(q, key)] = place[j]
+                    w.append(j)
+                    marked.add(j)
+        need[i] = w
+    queue = {"v": g.vector, "s": g.scalar, "p": g.tensor, "g": g, "y": g.sync}
+    token, count, nd = {}, {k: 0 for k in ESEM}, 0
+    for i in order:
+        q, call, kind = ops[i][0], ops[i][1], ops[i][4]
+        if kind == "x":
+            token[i] = (T.sem["ar%d" % call], landed)
+            continue
+        for j in need[i]:
+            queue[q].wait_ge(*token[j])
+        ins = call(g)
+        if kind == "d":
+            token[i] = (T.sem["dm%d" % nd], 16)
+            ins.then_inc(token[i][0], 16)
+            nd += 1
+        elif kind == "c" and i in marked:
+            count[q] += 1
+            token[i] = (T.sem[ESEM[q]], count[q])
+            ins.then_inc(token[i][0], 1)
+    for k in range(nd):
+        g.sync.wait_ge(T.sem["dm%d" % k], 16)
+    g.wait_ge(T.sem.sent, sent)
+
+
+def rank_program(g, core, T, topo):
+    rank = T.rank_of(core)
+    if rank is None:
+        return
+
+    def masks(r):
+        src = T.cores[r]
+        dsts = {d: T.cores[r ^ d] for d in (1, 2, 3)}
+        far = [d for d in dsts if topo.chip(dsts[d]) != topo.chip(src)]
+        out, used = {}, set()
+        for group in (far, [d for d in dsts if d not in far]):
+            for j, d in enumerate(group):
+                free = [e for e in topo.engines(src, dsts[d]) if e not in used]
+                n = 1
+                while 2 * n <= len(free) // (len(group) - j):
+                    n *= 2
+                out[d] = free[:n]
+                used.update(out[d])
+        return out
+
+    mine = masks(rank)
+
+    def send(k):
+        def call(g):
+            tr = []
+            for d in (1, 2, 3):
+                rid, pid, _ = topo.addr(T.cores[rank ^ d])
+                a = 96 * k + 32 * (d - 1)
+                tr.append(RemoteDMATransfer(dst_ids=[DstId(rid=rid, pnc=pid)], dma_engine_mask=sum(1 << e for e in mine[d]),
+                                            remote_sem=T.sem["ar%d" % k], src=T.stg[:, a:a + 32], dst=T.land[:, a:a + 32]))
+            return g.remote_dma_fused(tr, local_sem=T.sem.sent)
+        return call
+
+    landed = sum(len(masks(rank ^ d)[d]) for d in (1, 2, 3))
+    emit(g, T, build(rank, T, send), landed, 12 * sum(len(mine[d]) for d in mine))

@@ -2,44 +2,41 @@ from concourse.bass import DstId, RemoteDMATransfer
 from concourse.mybir import AluOpType as Op, ActivationFunctionType as Fn
 
 M, E, G, NONE, LN, NP = 512, 2560, 384, 2944, 256, 3
-IX = 8
-DO = 1024
-DUM = 2960
+IX = 1
+WA, WS, WT, WN = IX + E, IX + E + 4 * M + 1, IX + E + 5 * M + 1, 5896
+STOP = -1000
 HALVES = 2
-PLAN = [("F", 112, 0), ("F", 108, 0), ("R", 96, 0), ("V", 40, 0), ("F", 104, 0), ("S", 60, 1), ("S", 64, 0), ("S", 24, 0)]
-PLANT = [("F", 56, 0), ("V", 32, 0), ("F", 56, 1), ("S", 48, 1), ("S", 64, 0)]
-SEG = [16 * (m + 1) for m in range(16)]
-SEGO = [sum(SEG[:m]) for m in range(17)]
-NVSEG = 7
+BLOCKS = 4
+PLAN = [("F", 112, 0), ("F", 112, 0), ("R", 96, 0), ("V", 64, 0), ("F", 112, 1), ("S", 48, 1), ("S", 40, 0), ("S", 24, 0)]
+PLANT = [("F", 64, 0), ("F", 64, 1), ("F", 64, 0), ("S", 32, 0), ("V", 32, 0)]
+LISTQ = {1: "vv", 2: "ss", 3: "vs", 4: "sv"}
 
 S_, P_ = "sbuf", "psum"
 f32, bf, f16, i32, u16 = "float32", "bfloat16", "float16", "int32", "uint16"
 BUF = {
-    "A": (bf, 2816), "TT": (bf, 2960), "U": (f32, 2960), "D": (f32, 3216), "YD": (f32, 3216), "SD": (f32, 2960),
+    "W": (f32, WN), "U": (f32, WN), "T0": (i32, 2960), "T1": (i32, 2960), "SD": (f32, 2960), "A0": (bf, M),
     "dpi": (i32, 2048), "sbi": (i32, 152), "sb2": (f16, 152), "sbh": (f16, 2432), "thi": (i32, 32), "th2": (bf, 32), "thh": (bf, 512), "thB": (bf, 512),
-    "thL": (f32, 32), "bdi": (i32, 24), "bdu": (u16, 24),
-    "GS": (bf, 9728), "SO": (f16, 8192), "SB": (bf, 4096), "PF": (f32, 4096), "PR": (f16, 4096), "X16": (f16, 512),
+    "bdi": (i32, 24), "bd0": (u16, 6), "bdW": (u16, 24),
+    "GS": (bf, 9728), "SO": (f16, 8192), "SB": (bf, 4096), "PF": (f32, 4096), "PR": (f16, 4096),
     "LU": (u16, 2048), "DLU": (u16, 288), "OLU": (u16, 256),
-    "R16": (bf, 1024), "R8": (bf, 1024), "R0": (bf, 1536), "RM": (bf, 256), "CS": (bf, 2176), "NE": (bf, 2176), "NS": (bf, 2176),
+    "R16": (bf, 1024), "R8": (bf, 1024), "R0": (bf, 1536), "RM": (bf, 256), "RM0": (bf, 256),
     "stg": (bf, 12 * 96), "land": (bf, 12 * 96), "yrs": (bf, 512),
-    "VP": (f32, 256), "Ut": (f32, 256), "Tt": (bf, 256), "k2": (f16, 256), "k2a": (f16, 256), "k2b": (f16, 256), "k2c": (f16, 256),
-    "X32": (f32, 512), "S15k": (f16, 128), "nIk": (f16, 128), "nI": (bf, 128), "n16": (bf, 128), "X": (bf, 256), "X2": (bf, 256), "Y": (f16, 256), "KM": (bf, 1024), "SV": (f32, 256), "SW": (f32, 256),
-    "FL": (u16, 80), "H": (f32, 168), "Z": (f32, 160), "MV": (f32, 80), "FQ": (f32, 160), "KO": (f32, 80), "KQ": (f32, 80), "CT": (f32, 80),
-    "E0": (f32, 32), "E0u": (u16, 32), "C32": (f32, 32), "C33": (f32, 32), "W": (f32, 32), "w1": (f32, 32), "w2": (f32, 32), "w3": (f32, 32),
-    "w4": (f32, 32), "ok": (f32, 16), "idl": (f32, 16), "own": (f32, 16), "nwd": (f32, 16), "C34": (f32, 32), "w5": (f32, 16), "w6": (f32, 32), "w7": (f32, 32),
-    "off": (u16, 32), "tg": (u16, 32), "fu": (u16, 16), "kou": (u16, 16), "exu": (u16, 16), "enu": (u16, 4), "XI": (f16, 256),
-    "d1": (bf, 256), "d2": (bf, 256), "d3": (bf, 256), "d4": (bf, 256), "dA": (bf, 256), "oA": (bf, 256), "oD": (f32, 256),
-    "KL": (bf, 256), "ZD": (f32, 256),
-    "pi": (i32, 4), "pj": (i32, 4), "col": (f32, 16), "JmP": (f32, 128), "JA": (f32, 128), "JB": (f32, 256), "J512": (f32, 512), "J5h": (f16, 512),
-    "m16": (f32, 16), "t5": (f32, 80), "m5": (f32, 80),
-    "I": (bf, 128), "BO": (bf, 128), "BOh": (f16, 128), "BOw": (bf, 128), "S15": (f16, 128), "P1": (bf, 128), "P2": (bf, 128),
-    "V0": (f32, 128), "V1": (f32, 128), "S0": (f32, 128), "S1": (f32, 128), "G8": (bf, 128), "G8h": (f16, 128), "G8n": (f16, 128),
-    "CW": (bf, 128), "one": (bf, 512), "NEG": (bf, 256), "DGr": (bf, 256), "tri": (bf, 16),
+    "Ti": (i32, 256), "Tb": (bf, 256), "k2": (f16, 256), "k2a": (f16, 256), "k2b": (f16, 256), "k2c": (f16, 256), "DM": (bf, 256), "n1": (f16, 256),
+    "X": (f16, 256), "X1": (f16, 256), "Dg": (f16, 256), "Y": (f16, 256), "SV": (f32, 256), "SW": (f32, 256), "FL": (u16, 64),
+    "H": (f32, 96), "Hd": (f32, 80), "Z": (f32, 80), "MV": (f32, 80), "G1": (f32, 80), "G2": (f32, 80), "CC": (f32, 80), "CM": (f32, 80),
+    "FT": (f32, 80), "FF": (f32, 80), "nl": (f32, 16), "lane": (f32, 16), "E0": (f32, 32), "E0u": (u16, 32), "T00": (f32, 32), "SP5": (f32, 160),
+    "SPd": (f32, 512), "m5": (f32, 80), "ex5": (u16, 16), "rp5": (u16, 6), "r5i": (i32, 6), "tg": (u16, 16), "fu": (u16, 16), "off": (u16, 16),
+    "XI": (f16, 256), "AE": (f32, 256), "EQ": (bf, 1024), "OF": (f32, 256), "XL": (f16, 256), "ab": (bf, 256), "KL": (bf, 256),
+    "d2": (bf, 256), "d3": (bf, 256), "d4": (bf, 256), "d5": (bf, 256), "mv": (bf, 256), "oW": (f32, 256), "oW2": (f32, 256), "ZD": (f32, 256),
+    "pi": (i32, 4), "col": (f32, 16), "JmP": (f32, 128), "JB": (f32, 256), "J512": (f32, 512), "J5h": (f16, 512), "m16": (f32, 16),
+    "I": (bf, 128), "I32": (f32, 128), "nI": (bf, 128), "I16": (bf, 128), "n16": (bf, 128), "n512": (bf, 128), "I4k": (bf, 128), "nI4k": (bf, 128),
+    "BO": (bf, 128), "BOa": (bf, 128), "BO4k": (bf, 128), "nBO4k": (bf, 128), "BOw": (bf, 128), "BOp": (bf, 128), "S15": (bf, 128),
+    "P1": (bf, 128), "P2": (bf, 128), "V0": (f32, 128), "V1": (f32, 128), "S0": (f32, 128), "S1": (f32, 128), "G8": (bf, 128), "G8n": (bf, 128),
+    "CW": (bf, 128), "one": (bf, 512), "DG": (bf, 256), "NEG": (bf, 256), "POS": (bf, 256), "TRI": (bf, 256), "CQ": (bf, 256),
 }
 SIZE = {f32: 4, i32: 4, bf: 2, f16: 2, u16: 2}
-GAT, FAR, WAKE, HOLD, GAP = 1.56, 3500.0, 60.0, 0.5, 300.0
-BIG = 12582912.0
-CUTS = [0, 10, 13, 15, 16]
+GAT, FAR, WAKE, HOLD, GAP, PE = 1.56, 3500.0, 60.0, 0.5, 300.0, 0.7
+HALF = 0.498
 LENGTH = [0.0]
 HOME, _fill = {}, {}
 for _k, (_d, _n) in BUF.items():
@@ -51,7 +48,7 @@ for _d, _n in _fill.items():
     SCRATCH["sm_" + _d] = (S_, [128, _n], _d)
 for _b in range(8):
     SCRATCH["ps%d" % _b] = (P_, [128, 512], f32)
-NDMA = 24
+NDMA = 40
 SEMAPHORES = ["sv", "ss", "sp", "sg", "sent"] + ["dm%d" % k for k in range(NDMA)] + ["ar%d" % k for k in range(12)]
 ESEM = {"v": "sv", "s": "ss", "p": "sp", "g": "sg"}
 
@@ -88,7 +85,7 @@ def build(rank, T, send):
             return (300.0, 300.0 + FAR)
         if kind == "d":
             x = out if out[0] != "@" else ins[0]
-            return (60.0, 2000.0 + (x[5] - x[4]) * (x[2] - x[1]) * SIZE[BUF[x[0]][0]] / 250.0)
+            return (60.0 if q != "g" else 600.0, 2000.0 + (x[5] - x[4]) * (x[2] - x[1]) * SIZE[BUF[x[0]][0]] / 250.0)
         vs = [x for x in [out] + ins if isinstance(x, tuple)]
         ind = [x for x in vs if x[0] == "*"]
         if ind:
@@ -98,9 +95,9 @@ def build(rank, T, send):
             big = [x for x in vs if x[2] - x[1] > 1 or n == 1]
             ps = any(x[0].startswith("ps") for x in big)
             if q == "p":
-                c = 30.0 + max(64, n) * (4 if BUF[ins[0][0]][0] == f32 else 1)
+                c = 30.0 + PE * max(64, n) * (4 if BUF[ins[0][0]][0] == f32 else 1)
             elif q == "g":
-                c = 130.0 + 2 * n
+                c = 150.0 + 2 * n
             elif q == "s":
                 c = 65.0 + max(64, n)
             else:
@@ -128,26 +125,34 @@ def build(rank, T, send):
     def cp(o, a): add("v", lambda g: g.vector.tensor_copy(ap(o), ap(a)), o, [a])
     def ms(o, c): add("v", lambda g: g.vector.memset(ap(o), c), o, [])
     def tr(o, a): add("v", lambda g: g.vector.transpose(ap(o), ap(a)), o, [a])
-    def scan(o, a, b, op0, op1): add("v", lambda g: g.vector.tensor_tensor_scan(ap(o), ap(a), ap(b), 0.0, op0, op1), o, [a, b])
+    def scan(o, a, b, op0, op1, also=()):
+        add("v", lambda g: g.vector.tensor_tensor_scan(ap(o), ap(a), ap(b), 0.0, op0, op1), o, [a, b] + list(also))
     def act(o, a, bias=0.0, scale=1.0, fn=Fn.Identity):
-        add("s", lambda g: g.scalar.activation(ap(o), ap(a), fn, bias=ap(bias), scale=scale), o, [a, bias])
+        add("s", lambda g: g.scalar.activation(ap(o), ap(a), fn, bias=ap(bias), scale=ap(scale)), o, [a, bias, scale])
+    def move(q, o, a): cp(o, a) if q == "v" else act(o, a)
     def mm(o, l, r, st=True, en=True): add("p", lambda g: g.tensor.matmul(ap(o), ap(l), ap(r), st, en), o, [l, r])
+    def total(o, terms):
+        for j, (l, r) in enumerate(terms):
+            mm(o, l, r, j == 0, j == len(terms) - 1)
     def iota(o, pat, base, ch):
         if BUF[o[0]][0] == i32:
             add("g", lambda g: g.iota(ap(o), pat, base, ch), o, [])
         else:
             add("g", lambda g: g.iota(ap(o), pat, base, ch, allow_small_or_imprecise_dtypes=True), o, [])
+    def pick(o, a, pat, op, base, ch): add("g", lambda g: g.affine_select(ap(o), ap(a), pat, op, 0.0, base, ch), o, [a])
     def dma(q, o, a):
-        add(q, (lambda g: g.sync.dma_start(ap(o), ap(a))) if q == "y" else (lambda g: g.scalar.dma_start(ap(o), ap(a))), o, [a], "d")
+        add(q, lambda g: {"y": g.sync, "s": g.scalar, "g": g}[q].dma_start(ap(o), ap(a)), o, [a], "d")
     def PS(b, lo, n, st=1): return ("ps%d" % b, lo, lo + (n - 1) * st + 1, st, 0, 128)
     def C(j): return V("col", j, j + 1)
     def ext(x): return ("@", x)
+    def TW(l): return "T%d" % (l % 2)
+    def acol(l): return WA + l * M if l < 4 else WT
     AD, SU, MU, MX, MN, EQ, NQ = Op.add, Op.subtract, Op.mult, Op.max, Op.min, Op.is_equal, Op.not_equal
+    RELU = Fn.Relu
 
-    dma("y", V("A", 0, M), ext(T.av[:, 0:M]))
+    dma("y", V("A0"), ext(T.av[:, 0:M]))
     dma("s", V("bdi"), ext(T.bd[:, :]))
     dma("y", V("dpi", 0, M), ext(T.dp[:, 0:M]))
-    dma("s", V("A", M, E), ext(T.av[:, M:E]))
     dma("y", V("dpi", M, 2 * M), ext(T.dp[:, M:2 * M]))
     dma("y", V("dpi", 2 * M, 4 * M), ext(T.dp[:, 2 * M:4 * M]))
     dma("y", V("thi"), ext(T.th[:, :]))
@@ -166,35 +171,45 @@ def build(rank, T, send):
     ms(V("one"), 1.0)
     iota(V("pi", 0, 1), [[0, 1]], 0, 1)
     iota(V("JmP"), [[1, 128]], 0, -1)
-    iota(V("JA"), [[1, 8], [0, 16]], 0, 0)
-    fill_s("TT", M, E, 0.0); fill_s("TT", E, 2960, 128.0)
+    ms(V("T1", M, 3 * M), 0); fill_s("T1", 3 * M, E, 0.0); ms(V("T1", E, 2960), 128)
     fill_s("R8", 0, 1024, -0.0625); ms(V("R8", 0, None, 8), 512.0)
     fill_s("R0", 0, 1536, 0.0); ms(V("R0", 0, None, 16), 512.0)
     fill_s("R16", 0, 1024, -0.0625); ms(V("R16", 0, None, 16), 512.0)
     ts(V("pi", 1, 2), V("pi", 0, 1), 4, Op.arith_shift_right)
     ts(V("pi", 2, 3), V("pi", 0, 1), 15, Op.bitwise_and)
     cp(V("col", 0, 3), V("pi", 0, 3))
-    cp(V("bdu"), V("bdi"))
+    cp(V("bd0"), V("bdi", 0, 6))
+    fill_g("W", 0, IX + M, 0); fill_g("W", WS - 1, WT, 0); fill_g("W", WT + M, WN, 0)
 
     def exchange(k):
         add("g", send(k), None, [N_("stg", 96 * k, 96)], "r")
+
+    def mirror(l):
+        for a, n in ((l * M, M), (E + 96 * l, 96)):
+            dma("y", N_(TW(l), a, n), N_(TW(l + 1), a, n))
 
     def ghosts(k, l):
         add("x", k, N_("land", 96 * k, 96), [], "x")
         for d, P in ((1, "P1"), (2, "P2"), (3, "I")):
             mm(PS(4, 32 * (d - 1), 32), V(P), N_("land", 96 * k + 32 * (d - 1), 32))
-        act(N_("TT", E + 96 * l, 96), PS(4, 0, 96), -127.0)
+        act(N_(TW(l + 1), E + 96 * l, 96), PS(4, 0, 96), -127.0)
+        if l < 3:
+            mirror(l)
 
     def release0(t):
-        cp(N_("stg", 96 * 4 * t, 96), IND(V("A", 0, M), V("bdu", 0, 6)))
+        if t == 0:
+            cp(N_("stg", 0, 96), IND(V("A0"), V("bd0")))
+        else:
+            cp(N_("stg", 96 * 4 * t, 96), IND(V("W", E, WA + M), V("bdW", 0, 6)))
         exchange(4 * t)
-        ts(V("TT", 0, M), V("A", 0, M), -127.0, AD)
+        act(V("T1", 0, M), V("A0") if t == 0 else N_("W", WA, M), -127.0)
 
     release0(0)
+    dma("g", N_("W", WA + M, 3 * M), ext(T.av[:, M:4 * M]))
+    dma("g", N_("W", WT, M), ext(T.av[:, 4 * M:E]))
     iota(V("JB"), [[0, 16], [1, 16]], 0, 0)
     iota(V("m16"), [[1, 16]], 0, 0)
-    iota(V("t5"), [[0, 16], [1, 5]], 0, 0)
-    iota(V("m5"), [[16, 16], [0, 5]], 0, 0)
+    iota(V("m5"), [[32, 16], [0, 5]], 0, 0)
     iota(V("J512"), [[1, 512]], 0, 0)
     ts(C(3), C(2), 8.0, Op.is_ge)
     ts(C(4), C(2), 8.0, Op.is_lt)
@@ -202,7 +217,10 @@ def build(rank, T, send):
     ts2(V("V1"), V("JmP"), 0.0, EQ, C(3), MU)
     ts2(V("S0"), V("JmP"), 0.0, EQ, C(4), MU)
     ts2(V("S1"), V("JmP"), 8.0, EQ, C(4), MU)
-    ts(N_("D", IX + M, M), V("dpi", 0, M), -float(DO), AD)
+    cp(N_("W", IX + M, M), V("dpi", 0, M))
+    act(N_("W", WA, M), V("A0"))
+    for l in range(4):
+        ts(V("bdW", 6 * l, 6 * l + 6), V("bdi", 6 * l, 6 * l + 6), float(IX + l * M), AD)
 
     def split(plan):
         return sum(x[1] for x in plan if x[0] == "F")
@@ -210,124 +228,109 @@ def build(rank, T, send):
     def parts(l):
         plan = PLAN if l < 4 else PLANT
         ks = [x[1] for x in plan if x[0] == "F"]
-        return [(sum(ks[:i]), k) for i, k in enumerate(ks)] if l == 1 else [(0, sum(ks))]
+        return [(0, ks[0]), (ks[0], sum(ks[1:]))] if l == 1 else [(0, sum(ks))]
 
     def lists(l, par):
         plan, st = (PLAN, 1) if l < 4 else (PLANT, 2)
         c0 = IX + l * M + (par if l == 4 else 0)
-        nf, n, lu, b = split(plan), (M if l < 4 else LN), (l - 1) * M, 2 + l % 2
-        if l < 4 and any(x[0] == "R" for x in plan):
-            ts(N_("DLU", 96 * (l - 1), 96), IND(N_("D", IX + l * M, M), V("bdu", 6 * l, 6 * l + 6)), float(DO), AD)
+        nf, n, lu = split(plan), (M if l < 4 else LN), (l - 1) * M
+        if l < 4:
+            move(LISTQ[l][0], N_("DLU", 96 * (l - 1), 96), IND(N_("W", 0, IX + (l + 1) * M), V("bdW", 6 * l, 6 * l + 6)))
         if n > nf:
-            ts(N_("LU", lu + nf, n - nf), N_("D", c0 + nf * st, n - nf, st), float(DO), AD)
+            move(LISTQ[l][0], N_("LU", lu + nf, n - nf), N_("W", c0 + nf * st, n - nf, st))
         for i, (a, k) in enumerate(parts(l) if nf else []):
-            h, bb = k // 2, b if i % 2 == 0 else 5 - b
+            h, bb = k // 2, ((2, 3), (5,), (6,), (7,))[l - 1][i]
             for j, (a0, a1) in enumerate((("S0", "S1"), ("V0", "V1"))):
-                mm(PS(bb, j * h, h), V(a0), N_("D", c0 + a * st, h, 2 * st), True, False)
-                mm(PS(bb, j * h, h), V(a1), N_("D", c0 + (a + 1) * st, h, 2 * st), False, True)
-            ts(N_("LU", lu + a, k), PS(bb, 0, k), float(DO), AD)
+                total(PS(bb, j * h, h), [(V(a0), N_("W", c0 + a * st, h, 2 * st)), (V(a1), N_("W", c0 + (a + 1) * st, h, 2 * st))])
+            move(LISTQ[l][1], N_("LU", lu + a, k), PS(bb, 0, k))
 
     def own_keys(l, par):
         n, st = (M, 1) if l < 4 else (LN, 2)
-        mm(PS(l % 2, 0, n), V("CW", p1=64), V("one", 0, n, p1=64), True, False)
-        mm(PS(l % 2, 0, n), V("I"), N_("A", l * M + (par if l == 4 else 0), n, st), False, True)
+        total(PS(l % 2, 0, n), [(V("CW", p1=64), V("one", 0, n, p1=64)), (V("I32"), N_("W", acol(l) + (par if l == 4 else 0), n, st))])
 
     lists(1, 0)
-    ts(V("I"), V("JmP"), 0.0, EQ)
+    pick(V("I"), V("one", 0, 128), [[-1, 128]], EQ, 0, 1)
+    pick(V("I32"), V("one", 0, 128), [[-1, 128]], EQ, 0, 1)
     ts2(C(5), C(1), -32.0, MU, 112.0, AD)
     ts(V("P1"), V("JmP"), C(5), EQ)
     ts2(C(6), C(1), 0.0, Op.is_gt, 128.0, MU)
     ts2(C(6), C(1), -32.0, MU, C(6), AD)
     ts(V("P2"), V("JmP"), C(6), EQ)
-    ms(V("CW", p1=64), 0.0); ms(V("CW", p1=1), -128.0); ms(V("CW", p0=32, p1=33), 0.03125)
+    ms(V("CW", p1=64), 0.0); ms(V("CW", p1=1), -128.0); ms(V("CW", p0=32, p1=33), 1.0 / 256)
     own_keys(1, 0)
+    act(N_("W", IX + 2 * M, M), V("dpi", M, 2 * M))
+    fill_g("T0", M, E, 0); fill_g("T0", E + 96, 2960, 128)
 
-    def late_setup(step):
-        if step == 0:
-            ts(N_("D", IX + 2 * M, M), V("dpi", M, 2 * M), -float(DO), AD)
-            fill_g("U", 0, IX + M, 1000); fill_g("U", IX + 4 * M, 2960, 1000)
-            fill_g("D", 0, IX + M, 0); fill_g("D", IX + E, 3216, 0)
-            fill_g("A", E, 2816, 0)
-            fill_g("SD", 0, IX, 0); fill_g("SD", IX + 4 * M, IX + E, 0); fill_g("SD", IX + NONE, 2960, 0)
-            fill_g("CS", 0, 2176, 0); fill_g("H", 0, 168, 0)
-            ts(V("BO"), V("JA"), C(1), EQ)
-            ts(V("BOh"), V("JA"), C(1), EQ)
-            ts2(V("BOw"), V("JA"), C(1), EQ, float(DO + IX), MU)
-            ts(C(7), C(2), 15.0, EQ)
-            ts2(V("S15"), V("JA"), C(1), EQ, C(7), MU)
-            ts(V("G8"), V("JA"), C(0), EQ)
-            ts(V("G8h"), V("JA"), C(0), EQ)
-            ts2(V("G8n"), V("JA"), C(0), EQ, -1.0, MU)
-            ts2(V("NEG"), V("JB"), C(2), NQ, -4096.0, MU)
-            ts2(C(8), C(2), -1.0, MU, 15.0, AD)
-            ts(V("DGr"), V("JB"), C(8), EQ)
-            ts2(V("tri"), V("JB", 0, 16), C(8), Op.is_le, 0.5, MU)
-            ts2(C(9), C(2), -1.0, MU, -24577.0, AD)
-            ts2(C(10), C(2), 0.0625, MU, 0.0625, AD)
-            ts(V("S15k"), V("S15"), 2048.0, MU)
-            ts(V("nIk"), V("I"), -2048.0, MU)
-            ts(V("nI"), V("I"), -1.0, MU)
-            ts(V("n16"), V("I"), -16.0, MU)
-            ms(V("RM"), 0.0); ms(V("RM", 0, None, 16), -8192.0)
-            cp(V("th2"), V("thi"))
-            dma("y", V("thh", p1=8), V("th2"))
-            cp(V("J5h", p1=8), V("J512", p1=8))
-            ts(V("sb2"), V("sbi"), -float(DO), AD)
-            dma("y", V("sbh", p1=8), V("sb2"))
-            mm(PS(5, 0, M), V("G8", p1=8), V("thh", p1=8))
-            act(V("thB"), PS(5, 0, M), -127.0)
-            for j in range(5):
-                n = M if j < 4 else G
-                b = 6 + j % 2
-                mm(PS(b, 0, n), V("G8h", p1=8), V("sbh", j * M, j * M + n, p1=8), True, False)
-                mm(PS(b, 0, n), V("G8n", p1=8), V("J5h", 0, n, p1=8), False, True)
-                nm = j * M if j < 4 else E
-                act(N_("SD", IX + nm, n), PS(b, 0, n), float(DO - nm))
-        if step == 1:
-            ts(N_("D", IX + 3 * M, M), V("dpi", 2 * M, 3 * M), -float(DO), AD)
-            ts(N_("D", IX + 4 * M, M), V("dpi", 3 * M, 4 * M), -float(DO), AD)
-        if step == 2:
-            ts2(V("w1", 0, 16), V("m16"), 16.0, MU, C(2), AD)
-            for par in (0, 1):
-                ts2(N_("E0", 16 * par, 16), V("w1", 0, 16), 2.0, MU, float(4 * M + IX + par), AD)
-            cp(V("E0u"), V("E0"))
-            ts(V("C33", 0, 16), V("w1", 0, 16), float(E), AD)
-            ts(V("C33", 16, 32), V("w1", 0, 16), float(DUM), AD)
-            ts(V("w3", 0, 16), V("C33", 0, 16), float(IX), AD)
-            cp(V("w3", 16, 32), V("C33", 16, 32))
-            ts(V("C34"), V("C33"), 0.5, MU)
-            ms(V("C32", 0, 16), IX + 1023.5); ms(V("C32", 16, 32), float(IX + E))
-            ts2(V("t5"), V("t5"), -1.0, AD, 0.0, MX)
-            ts2(V("t5"), V("t5"), 256.0, MU, C(2), AD)
-            tt(V("CT"), V("t5"), V("m5"), AD)
-            ts2(V("exu"), V("m16"), -1.0, MU, 15.0, AD)
-            ts2(C(11), C(2), 1.0, AD, 8.0, MU)
-            ts2(C(12), C(2), 2.0, AD, C(11), MU)
-            ms(V("enu"), 0)
-            for j in (0, 1):
-                ts(V("enu", j, j + 1), C(12), -1.0, AD)
-            for m in range(16):
-                cp(N_("CS", SEGO[m], 16), V("tri"))
+    def late_setup():
+        cp(N_("W", IX + 3 * M, M), V("dpi", 2 * M, 3 * M))
+        act(N_("W", IX + 4 * M, M), V("dpi", 3 * M, 4 * M))
+        fill_g("U", 0, IX + M, STOP); fill_g("U", IX + 4 * M, WN, STOP)
+        fill_g("SD", 0, IX, 0); fill_g("SD", IX + 4 * M, IX + E, 0); fill_g("SD", IX + NONE, 2960, 0)
+        fill_g("H", 0, 1, 0); fill_g("SPd", 0, 512, -30000); fill_g("RM", 0, LN, 0); fill_g("RM0", 0, LN, 1)
+        iota(V("RM", 0, None, 16), [[0, 16]], -8192, 0)
+        iota(V("RM0", 0, None, 16), [[0, 16]], 0, 0)
+        pick(V("BOa"), V("one", 0, 128), [[-16, 8], [0, 16]], Op.is_ge, 0, 1)
+        pick(V("BO"), V("BOa"), [[16, 8], [0, 16]], Op.is_ge, 15, -1)
+        pick(V("S15"), V("one", 0, 128), [[-16, 8], [0, 16]], EQ, -15, 1)
+        pick(V("G8"), V("one", 0, 128), [[-1, 8], [0, 16]], EQ, 0, 1)
+        ts(V("DG"), V("JB"), C(2), EQ)
+        ts2(V("TRI"), V("JB"), C(2), Op.is_le, -8192.0, MU)
+        ts2(C(7), C(2), -1.0, MU, -1.0, AD)
+        ts(C(8), C(2), -14.0, AD)
+        ts(C(9), C(2), 0.5, AD)
+        ts2(C(10), C(2), 4096.0, MU, -29696.0 - 8192.0, AD)
+        ts(C(11), C(2), 0.0625, MU)
+        for name, src, c in (("nI", "I", -1.0), ("I16", "I", 16.0), ("n16", "I", -16.0), ("n512", "I", -512.0), ("I4k", "I", 4096.0),
+                             ("nI4k", "I", -4096.0), ("BO4k", "BO", 4096.0), ("nBO4k", "BO", -4096.0), ("BOw", "BO", 16384.0),
+                             ("BOp", "BO", C(11)), ("G8n", "G8", -1.0)):
+            ts(V(name), V(src), c, MU)
+        ts2(V("NEG"), V("DG"), 4096.0, MU, -4096.0, AD)
+        ts2(V("POS"), V("DG"), -16384.0, MU, 16384.0, AD)
+        ts2(V("CQ"), V("DG"), 8192.0, MU, C(10), AD)
+        cp(V("th2"), V("thi"))
+        dma("y", V("thh", p1=8), V("th2"))
+        cp(V("J5h", p1=8), V("J512", p1=8))
+        ts(V("sb2"), V("sbi"), -1024.0, AD)
+        dma("y", V("sbh", p1=8), V("sb2"))
+        mm(PS(5, 0, M), V("G8", p1=8), V("thh", p1=8))
+        act(V("thB"), PS(5, 0, M), -127.0)
+        for j in range(5):
+            n = M if j < 4 else G
+            b = 6 + j % 2
+            total(PS(b, 0, n), [(V("G8", p1=8), V("sbh", j * M, j * M + n, p1=8)), (V("G8n", p1=8), V("J5h", 0, n, p1=8))])
+            nm = j * M if j < 4 else E
+            act(N_("SD", IX + nm, n), PS(b, 0, n), float(1024 - nm))
+        ts2(V("lane"), V("m16"), 16.0, MU, C(2), AD)
+        ts2(V("m5"), V("m5"), C(2), AD, C(2), AD)
+        for par in (0, 1):
+            ts2(N_("E0", 16 * par, 16), V("lane"), 2.0, MU, float(4 * M + IX + par), AD)
+            ts(N_("SPd", LN * par, 16, 16), V("lane"), float(WT + M - E - par), AD)
+        ts2(V("T00", 0, 16), V("lane"), 2.0, MU, float(WT - E), AD)
+        ts(V("SP5", 0, 80), V("m5"), float(WS - E), AD)
+        cp(V("E0u"), V("E0"))
+        ts2(V("ex5"), V("m16"), 5.0, MU, 4.0, AD)
+        ts2(V("G1", 0, 6), V("m16", 0, 6), 16.0, MU, C(2), AD)
+        ts2(V("G1", 8, 14), V("G1", 0, 6), 0.2, MU, -0.4, AD)
+        cp(V("r5i"), V("G1", 8, 14))
+        cp(V("rp5"), V("r5i"))
 
     def level(t, l, fill):
         plan, n = (PLAN, M) if l < 4 else (PLANT, LN)
-        nf, lu, win = split(plan), (l - 1) * M, V("TT", 0, NONE + 1)
+        nf, lu, win = split(plan), (l - 1) * M, V(TW(l), 0, NONE + 1)
         fo, so = 0, nf
-        done, tail = {"F": 0, "S": nf}, []
+        done = {"F": 0, "S": nf}
 
         def cols(j):
             a, kk = [x for x in parts(l) if x[0] <= fo][-1]
             return N_("LU", lu + a + j * (kk // 2) + (fo - a) // 2, k // 2)
 
         def finish(c, k, ends):
-            u = N_("U", IX + l * M + c, k) if l < 4 else N_("Ut", c, k)
+            u = N_("U", IX + l * M + c, k) if l < 4 else N_("U", IX + l * M + (t & 1) + 2 * c, k, 2)
             tt(u, ends, PS(l % 2, c, k), MN)
-            if l == 4 or c + k == n:
-                ts(N_("X16", c, k), u, 1536.484375, AD)
-                if l < 4:
-                    tail.append((c, k))
+            if l < 4 and c + k == n:
+                ts(N_(TW(l + 1), l * M + c, k), u, HALF, AD)
             else:
-                ts2(N_("X32", c, k), u, 0.484375, AD, BIG, AD)
+                act(N_(TW(l + 1), l * M + c, k) if l < 4 else N_("Ti", c, k), u, HALF)
 
         for j, (kind, k, fin) in enumerate(plan):
             if kind == "F":
@@ -359,37 +362,27 @@ def build(rank, T, send):
             else:
                 scan(N_("SB", 0, 1536), N_("R0", 0, 1536), N_("GS", 8192, 1536), AD, MN)
                 x = 4 * t + l
-                tt(N_("stg", 96 * x, 96), IND(N_("A", l * M, M), V("bdu", 6 * l, 6 * l + 6)), N_("SB", 15, 96, 16), MN)
+                tt(N_("stg", 96 * x, 96), IND(V("W", E, WA + (l + 1) * M), V("bdW", 6 * l, 6 * l + 6)), N_("SB", 15, 96, 16), MN)
                 exchange(x)
-        if l < 4:
-            c, k = tail[0]
-            act(N_("TT", l * M, c), N_("X32", 0, c), -BIG)
-            ts(N_("TT", l * M + c, k), N_("X16", c, k), -1536.0, AD)
-
-        if l < 4 and not any(x[0] == "R" for x in plan):
-            ts(N_("stg", 96 * (4 * t + l), 96), IND(N_("TT", l * M, M), V("bdu", 6 * l, 6 * l + 6)), 127.0, AD)
-            exchange(4 * t + l)
 
     def odd_tops():
         for a, n in ((0, 1536), (1536, 1536), (3072, 1024)):
-            add("v", lambda g, a=a, n=n: g.vector.tensor_tensor_scan(ap(N_("SB", a, n)), ap(N_("R0", 0, n)), ap(N_("GS", a, n)), 0.0, AD, MN),
-                N_("SB", a, n), [N_("R0", 0, n), N_("GS", a, n), N_("A", 0, 16)])
-        tt(N_("yrs", 1, LN, 2), N_("SB", 15, LN, 16), N_("A", 4 * M + 1, LN, 2), MN)
+            scan(N_("SB", a, n), N_("R0", 0, n), N_("GS", a, n), AD, MN, [N_("W", 0, 16)])
+        tt(N_("yrs", 1, LN, 2), N_("SB", 15, LN, 16), N_("W", WT + 1, LN, 2), MN)
 
     for t in range(NP):
         par, last = t & 1, t == NP - 1
         if t == 0:
-            late_setup(0)
+            late_setup()
+        for l in range(2, 5):
+            lists(l, par)
+        if last:
+            act(V("OLU"), N_("W", IX + 4 * M + 1, LN, 2))
         ghosts(4 * t, 0)
         for l in range(1, 5):
             def fill(l=l):
-                if t == 0 and l < 3:
-                    late_setup(l)
                 if l < 4:
                     own_keys(l + 1, par)
-                    lists(l + 1, par)
-                elif last:
-                    ts(V("OLU"), N_("D", IX + 4 * M + 1, LN, 2), float(DO), AD)
             level(t, l, fill)
             if l < 4:
                 ghosts(4 * t + l, l)
@@ -397,136 +390,112 @@ def build(rank, T, send):
         hs = [(h, h * hn, h * hn // 16, hn // 16) for h in range(HALVES)]
         for h in hs:
             def Hf(name): return N_(name, h[1], hn)
-            ts2(Hf("k2"), Hf("X16"), 16.0, MU, C(9), AD)
-            ts(Hf("Tt"), Hf("X16"), -1536.0, AD)
+            act(Hf("k2"), Hf("Ti"), C(7), 16.0)
             tr(Hf("k2a"), Hf("k2"))
             scan(Hf("k2b"), N_("RM", 0, hn), Hf("k2a"), AD, MX)
             tr(Hf("k2c"), Hf("k2b"))
-            mm(PS(4 + h[0], 0, hn), V("nIk"), Hf("k2"), True, False)
-            mm(PS(4 + h[0], 0, hn), V("I"), Hf("Tt"), False, False)
-            mm(PS(4 + h[0], 0, hn), V("S15k"), Hf("k2c"), False, True)
-            act(Hf("VP"), PS(4 + h[0], 0, hn))
-            act(Hf("d1"), PS(4 + h[0], 0, hn), -256.0, fn=Fn.Relu)
+            total(PS(6 + h[0], 0, hn), [(V("nI"), Hf("k2")), (V("S15"), Hf("k2c"))])
+            act(Hf("DM"), PS(6 + h[0], 0, hn), 16.0, -16.0, RELU)
+            total(PS(6 + h[0], hn, hn), [(V("S15"), Hf("k2c")), (V("BOp"), Hf("DM"))])
+            act(Hf("n1"), PS(6 + h[0], hn, hn), C(8))
         act(N_("H", 1, 16, 5), N_("E0", 16 * par, 16))
         if last:
-            act(V("yrs", 0, M, 2), V("Tt"), 127.0)
+            act(V("yrs", 0, M, 2), V("Ti"), 127.0)
             for j in range(16):
-                act(N_("GS", 256 * j, 256), IND(V("TT", 0, NONE + 1), N_("OLU", 16 * j, 16)), 127.0)
+                act(N_("GS", 256 * j, 256), IND(V(TW(4), 0, NONE + 1), N_("OLU", 16 * j, 16)), 127.0)
 
         def aside(s):
             if s == 1:
-                act(V("d2"), V("Tt"), -111.0, -1.0, fn=Fn.Relu)
-                mm(PS(6, 0, LN), V("I"), V("thB", par, M, 2), True, False)
-                mm(PS(6, 0, LN), V("nI"), V("Tt"), False, False)
-                mm(PS(6, 0, LN), V("nI"), V("d1"), False, True)
-                act(V("d3"), PS(6, 0, LN), fn=Fn.Relu)
+                act(V("Tb"), V("Ti"))
+                act(V("d2"), V("Ti"), -111.0, -1.0, RELU)
+                total(PS(1, 0, LN), [(V("I"), V("thB", par, M, 2)), (V("nI"), V("Tb")), (V("I16"), V("DM"))])
+                act(V("d3"), PS(1, 0, LN), -256.0, 1.0, RELU)
             if s == 2:
-                mm(PS(7, 0, LN), V("nI"), V("d2"), True, False)
-                mm(PS(7, 0, LN), V("nI"), V("d1"), False, False)
-                mm(PS(7, 0, LN), V("n16"), V("d3"), False, True)
-                act(V("d4"), PS(7, 0, LN), 16.0, fn=Fn.Relu)
-                ts(V("w5"), N_("H", 2, 16, 5), 0.0, NQ)
-                mm(PS(6, 0, LN), V("I"), V("NEG"), True, False)
-                mm(PS(6, 0, LN), V("BO"), V("d3"), False, True)
-                scan(V("SW"), V("RM"), PS(6, 0, LN), AD, MX)
-                ts(V("ok"), N_("SW", 15, 16, 16), 0.0, Op.is_gt)
+                total(PS(1, 0, LN), [(V("I"), V("NEG")), (V("BO"), V("d3"))])
+                scan(V("SW"), V("RM0"), PS(1, 0, LN), MU, MX)
+                act(V("nl"), N_("SW", 15, 16, 16), 8192.0 - E - par, -8192.0)
+                total(PS(0, 0, LN), [(V("nI"), V("n1")), (V("BO"), V("X1"))])
+                act(V("mv"), PS(0, 0, LN), C(9), 1.0, RELU)
             if s == 3:
-                mm(PS(6, 0, LN), V("I"), V("d3"), True, False)
-                mm(PS(6, 0, LN), V("nI"), V("d4"), False, True)
-                act(V("dA"), PS(6, 0, LN))
-                tt(V("W", 16, 32), V("w5"), V("ok"), MU)
-                ts2(V("nwd"), V("W", 16, 32), -1.0, MU, 1.0, AD)
+                ts(V("nl"), V("nl"), -float(E + par), MX)
+                total(PS(1, 0, LN), [(V("nI"), V("d2")), (V("n16"), V("d3")), (V("I16"), V("DM"))])
+                act(V("d4"), PS(1, 0, LN), -240.0, 1.0, RELU)
+                total(PS(0, 0, LN), [(V("I"), V("d3")), (V("n512"), V("mv"))])
+                act(V("d5"), PS(0, 0, LN), 0.0, 1.0, RELU)
+            if s == 4:
+                tt(V("G1"), IND(V("nl"), V("rp5", 0, 5)), N_("H", 0, 80), AD)
+                tt(V("G2"), V("G1"), V("SP5", 0, 80), MN)
 
         for s in range(1, 5):
             def lst(h): return N_("E0u", 16 * par + h[2], h[3]) if s == 1 else N_("FL", 16 * (s - 1) + h[2], h[3])
+            xn = "X1" if s == 1 else "X"
+            if s == 4:
+                fill_h = N_("H", 5, 16, 5)
+                if t == 0:
+                    ms(fill_h, 0.0)
+                aside(4)
             for h in hs:
-                if s == 1:
-                    tt(N_("X", h[1], hn), N_("Ut", h[1], hn), N_("VP", h[1], hn), SU)
-                else:
-                    tt(N_("X", h[1], hn), IND(V("U"), lst(h)), N_("VP", h[1], hn), SU)
-                act(N_("X2", h[1], hn), N_("X", h[1], hn), 1.0, fn=Fn.Relu)
-                mm(PS(3 - h[0], 0, hn), V("I"), N_("NEG", 0, hn), True, False)
-                mm(PS(1 - h[0], 0, hn), V("BO"), N_("X2", h[1], hn))
+                def Hf(name): return N_(name, h[1], hn)
+                act(Hf("Dg"), IND(N_("W", 0, 2960), lst(h)), float(IX - 1024))
+                tt(Hf(xn), IND(N_("U", 0, 2960), lst(h)), Hf("DM"), MU)
+                total(PS(2 + h[0], 0, hn), [(V("I4k"), Hf("n1")), (V("I"), Hf("Dg")), (V("nBO4k"), Hf(xn))])
             for h in hs:
-                km = N_("KM", LN * (s - 1) + h[1], hn)
-                ts(km, PS(1 - h[0], 0, hn), C(10), EQ)
-                mm(PS(3 - h[0], 0, hn), V("BOw"), km, False, False)
-                tt(N_("Y", h[1], hn), IND(V("D", 0, DUM), lst(h)), km, MU)
-                mm(PS(3 - h[0], 0, hn), V("BOh"), N_("Y", h[1], hn), False, True)
-            if HALVES == 1:
-                aside(s)
+                def Hf(name): return N_(name, h[1], hn)
+                ts2(Hf("Y"), PS(2 + h[0], 0, hn), -2048.0, MX, 2048.0, MN)
+                total(PS(4 + h[0], 0, hn), [(V("I"), N_("CQ", 0, hn)), (V("nI4k"), Hf("n1")), (V("BO4k"), Hf(xn)), (V("BO"), Hf("Y"))])
             for h in hs:
-                scan(N_("SV", h[1], hn), N_("RM", 0, hn), PS(3 - h[0], 0, hn), AD, MX)
+                scan(N_("SV", h[1], hn), N_("RM0", 0, hn), PS(4 + h[0], 0, hn), MU, MX)
                 ends = N_("SV", h[1] + 15, h[3], 16)
                 if s < 4:
-                    cp(N_("FL", 16 * s + h[2], h[3]), ends)
+                    act(N_("FL", 16 * s + h[2], h[3]), ends)
                     act(N_("H", 1 + s + 5 * h[2], h[3], 5), ends)
             if s == 4:
                 cp(N_("H", 5, 16, 5), N_("SV", 15, 16, 16))
-            if HALVES > 1:
+            else:
                 aside(s)
-            if last and s == 1:
-                for a in range(IX + M, IX + E, M):
-                    act(N_("YD", a, M), N_("D", a, M), float(DO))
-                act(V("YD", 0, IX + M), V("D", 0, IX + M))
-                act(V("YD", IX + E), V("D", IX + E))
-        ts(V("MV"), N_("H", 1, 80), 0.0, NQ)
-        ts(N_("Z", 0, 80), N_("H", 1, 80), 0.0, EQ)
-        tt(N_("H", 81, 80), N_("H", 0, 80), V("MV"), MU)
-        ts(N_("Z", 80, 80), N_("H", 1, 80), 0.0, EQ)
-        scan(V("FQ"), V("Z"), N_("H", 1, 160), MU, AD)
-        fq = N_("FQ", 4, 32, 5)
-        ts(V("own"), N_("FQ", 4, 16, 5), float(E + IX), Op.is_lt)
-        tt(V("w1"), fq, V("C32"), SU)
-        tt(V("W", 0, 16), V("own"), V("nwd"), MU)
-        tt(V("w2"), V("w1"), V("W"), MU)
-        tt(V("idl"), V("w2", 0, 16), V("w2", 16, 32), AD)
-        tt(V("XI"), IND(V("idl"), V("exu")), V("DGr"), MU)
-        mm(PS(7, 0, LN), V("BOh"), V("XI"))
-        mm(PS(6, 0, LN), V("BOh"), V("XI"))
-        dw = V("YD") if last else V("D")
-        tt(V("w6"), fq, V("w3"), SU)
-        tt(V("w7"), V("w6"), V("W"), MU)
-        tt(V("w4"), V("w7"), V("C33"), AD)
-        cp(V("tg"), V("w4"))
-        tt(V("KO"), V("MV"), V("CT"), MU)
-        cp(V("fu"), N_("FQ", 4, 16, 5))
-        scan(V("KQ"), V("Z", 0, 80), V("KO"), MU, AD)
-        cp(V("kou"), N_("KQ", 4, 16, 5))
-        for m in range(NVSEG, 16):
-            act(N_("NE", SEGO[m], SEG[m]), PS(7, LN - SEG[m], SEG[m]), V("idl", m, m + 1), -1.0, fn=Fn.Abs)
-            chain.append(len(ops) - 1)
-        act(V("oA"), IND(V("A"), V("tg", 0, 16)))
-        act(V("oD"), IND(dw, V("tg", 16, 32)))
-        act(V("KL"), IND(V("KM"), V("kou")))
-        for m in range(NVSEG):
-            ts(N_("NE", SEGO[m], SEG[m]), PS(6, LN - SEG[m], SEG[m]), V("idl", m, m + 1), NQ)
-        for a, b in zip(CUTS, CUTS[1:]):
-            add("v", lambda g, a=a, b=b: g.vector.tensor_tensor_scan(ap(V("NS", SEGO[a], SEGO[b])), ap(V("NE", SEGO[a], SEGO[b])),
-                ap(V("CS", SEGO[a], SEGO[b])), 0.0, MN, MX), V("NS", SEGO[a], SEGO[b]), [V("NE", SEGO[a], SEGO[b]), V("CS", SEGO[a], SEGO[b])])
-        tt(V("w1"), IND(V("NS"), V("enu", 0, 2)), V("w7"), MU)
-        tt(V("w2"), V("w1"), V("C34"), AD)
-        ts(V("off"), V("w2"), 2.0, MU)
-
-        def write_a():
-            tt(IND(V("A"), V("off", 0, 16)), V("oA"), V("dA"), AD)
-
-        def write_d():
-            tt(IND(dw, V("off", 16, 32)), V("oD"), V("ZD"), AD)
-
+        hh = N_("H", 1, 80)
+        act(V("MV"), hh, 0.0, 1.0, Fn.Sign)
+        act(V("Z"), hh, 1.0, -1.0, RELU)
+        if par:
+            ts(V("Hd"), hh, -1.0, AD)
+        tt(V("CC"), V("Hd") if par else hh, V("G2"), MN)
+        act(N_("CC", 0, 16, 5), V("T00", 0, 16))
+        tt(V("CM"), V("CC"), V("MV"), MU)
+        scan(V("FT"), V("Z"), V("CM"), MU, AD)
+        tt(V("XI"), IND(V("FT"), V("ex5")), V("DG"), MU)
+        act(V("tg"), N_("FT", 4, 16, 5), float(E + par))
+        act(V("AE"), IND(V("FT"), V("ex5")))
+        mm(PS(3, 0, LN), V("BO"), V("XI"))
+        total(PS(2, 0, LN), [(V("I"), V("TRI")), (V("BO"), V("XI"))])
+        scan(V("FF"), V("Z"), hh, MU, AD)
+        act(V("fu"), N_("FF", 4, 16, 5))
+        tt(V("XL"), IND(V("U"), V("tg")), V("DM"), MU)
+        act(V("oW"), IND(V("W"), V("tg")))
+        total(PS(5, 0, LN), [(V("nI"), V("n1")), (V("BO"), V("XL"))])
+        total(PS(6, 0, LN), [(V("I"), V("d5")), (V("nI"), V("d4")), (V("I32"), V("oW"))])
+        act(V("ab"), PS(5, 0, LN), 0.0, 1.0, Fn.Abs)
+        act(V("KL"), V("ab"), 1.0, -1.0, RELU)
+        act(V("oW2"), PS(6, 0, LN))
+        mm(PS(4, 0, LN), V("I"), V("POS"), True, False)
+        mm(PS(4, 0, LN), V("BO"), V("XI"), False, False)
+        nd = 16 // BLOCKS
+        for d in list(range(1, nd)) + [0]:
+            n = LN - 16 * d
+            tt(N_("EQ", LN * d, n), N_("AE", 0, n), PS(3 if d else 2, 16 * d, n), EQ)
+            mm(PS(4, 16 * d, n), V("BOw"), N_("EQ", LN * d, n), False, d == 0)
+        tt(V("ZD"), IND(V("SD"), V("fu")), V("KL"), MU)
+        scan(V("OF"), N_("SPd", LN * par, LN), PS(4, 0, LN), MX, MN)
+        ts(V("off"), N_("OF", 15, 16, 16), float(E + par), AD)
+        for b in range(BLOCKS - 1, -1, -1):
+            tt(IND(V("W"), N_("off", nd * b, nd)), N_("oW2", 16 * nd * b, 16 * nd), N_("ZD", 16 * nd * b, 16 * nd), AD)
         if not last:
-            tt(V("ZD"), IND(V("SD"), V("fu")), V("KL"), MU)
-            write_a()
             release0(t + 1)
-            write_d()
-            own_keys(1, 0)
             lists(1, 0)
+            own_keys(1, 0)
         else:
-            tt(V("ZD"), IND(V("SD"), V("fu")), V("KL"), MU)
-            write_d()
-            dma("y", ext(T.yd[:, :]), N_("YD", IX + M, 4 * M))
-            write_a()
-            dma("y", ext(T.ya[:, :]), V("A", 0, E))
+            dma("y", ext(T.yd[:, :]), N_("W", IX + M, 4 * M))
+            dma("g", ext(T.ya[:, 0:4 * M]), N_("W", WA, 4 * M))
+            dma("g", ext(T.ya[:, 4 * M:E]), N_("W", WT, M))
             odd_tops()
             dma("y", ext(T.yr[:, :]), V("yrs"))
     return ops, chain
@@ -587,7 +556,11 @@ def emit(g, T, steps, landed, sent):
             for x in views:
                 psum = x[0].startswith("ps")
                 for (j, lo, hi, p0, p1, jw) in seen.get(x[0], []):
-                    meet = lo < x[2] and x[1] < hi and p0 < x[5] and x[4] < p1
+                    a, b = x[1], x[2]
+                    if w and jw and (kind == "d") != (ops[j][4] == "d"):
+                        e = 16 // SIZE[BUF[x[0]][0]]
+                        a, b = a // e * e, -(-b // e) * e
+                    meet = lo < b and a < hi and p0 < x[5] and x[4] < p1
                     if (meet and (w or jw)) or (psum and (ops[j][0] != q or q == "p")):
                         d.add(j)
         for views, w in ((rd, False), (wr, True)):

@@ -5,39 +5,45 @@ M, E, G, NONE, LN, NP = 512, 2560, 384, 2944, 256, 3
 IX = 1
 WA, WS, WT, WN = IX + E, IX + E + 4 * M + 1, IX + E + 5 * M + 1, 5896
 STOP = -1000
-HALVES = 2
+HN = LN // 2
+JOIN = (1, 1, 1)
+NW, NV = 10, 3
 BLOCKS = 4
-PLAN = [("F", 112, 0), ("F", 112, 0), ("R", 96, 0), ("V", 64, 0), ("F", 112, 1), ("S", 48, 1), ("S", 40, 0), ("S", 24, 0)]
-PLANT = [("F", 64, 0), ("F", 64, 1), ("F", 64, 0), ("S", 32, 0), ("V", 32, 0)]
+PLAN = [("W", 72, 0), ("F", 112, 1), ("F", 128, 1), ("R", 96, 1), ("F", 96, 2), ("S", 56, 1), ("S", 32, 1), ("S", 16, 2)]
+PLANT = [("W", 16, 0), ("F", 48, 1), ("F", 64, 2), ("F", 32, 2), ("S", 32, 1), ("S", 32, 1), ("S", 32, 2)]
 LISTQ = {1: "vv", 2: "ss", 3: "vs", 4: "sv"}
+DATEQ, NEXTQ = "vv", "ss"
+RN = 1536
 
 S_, P_ = "sbuf", "psum"
 f32, bf, f16, i32, u16 = "float32", "bfloat16", "float16", "int32", "uint16"
 BUF = {
-    "W": (f32, WN), "U": (f32, WN), "T0": (i32, 2960), "T1": (i32, 2960), "SD": (f32, 2960), "A0": (bf, M),
-    "dpi": (i32, 2048), "sbi": (i32, 152), "sb2": (f16, 152), "sbh": (f16, 2432), "thi": (i32, 32), "th2": (bf, 32), "thh": (bf, 512), "thB": (bf, 512),
+    "W": (f32, WN), "U": (f32, 5640), "T0": (i32, 2960), "T1": (i32, 2960), "SD": (f32, 3088), "A0": (bf, M),
+    "sbi": (i32, 152), "sb2": (f16, 152), "sbh": (f16, 2432), "thi": (i32, 32), "th2": (bf, 32), "thh": (bf, 512), "thB": (bf, 512),
     "bdi": (i32, 24), "bd0": (u16, 6), "bdW": (u16, 24),
     "GS": (bf, 9728), "SO": (f16, 8192), "SB": (bf, 4096), "PF": (f32, 4096), "PR": (f16, 4096),
     "LU": (u16, 2048), "DLU": (u16, 288), "OLU": (u16, 256),
-    "R16": (bf, 1024), "R8": (bf, 1024), "R0": (bf, 1536), "RM": (bf, 256), "RM0": (bf, 256),
-    "stg": (bf, 12 * 96), "land": (bf, 12 * 96), "yrs": (bf, 512),
+    "R16": (bf, RN), "R8": (bf, RN), "R0": (bf, 1536), "RM": (bf, 256), "RM0": (bf, 256),
+    "stg": (bf, 12 * 96), "land": (bf, 12 * 96), "yrs": (bf, 512), "Ao": (bf, 256),
     "Ti": (i32, 256), "Tb": (bf, 256), "k2": (f16, 256), "k2a": (f16, 256), "k2b": (f16, 256), "k2c": (f16, 256), "DM": (bf, 256), "n1": (f16, 256),
     "X": (f16, 256), "X1": (f16, 256), "Dg": (f16, 256), "Y": (f16, 256), "SV": (f32, 256), "SW": (f32, 256), "FL": (u16, 64),
-    "H": (f32, 96), "Hd": (f32, 80), "Z": (f32, 80), "MV": (f32, 80), "G1": (f32, 80), "G2": (f32, 80), "CC": (f32, 80), "CM": (f32, 80),
-    "FT": (f32, 80), "FF": (f32, 80), "nl": (f32, 16), "lane": (f32, 16), "E0": (f32, 32), "E0u": (u16, 32), "T00": (f32, 32), "SP5": (f32, 160),
-    "SPd": (f32, 512), "m5": (f32, 80), "ex5": (u16, 16), "rp5": (u16, 6), "r5i": (i32, 6), "tg": (u16, 16), "fu": (u16, 16), "off": (u16, 16),
+    "H": (f32, 112), "Hd": (f32, 96), "Z": (f32, 96), "MV": (f32, 96), "G1": (f32, 96), "G2": (f32, 96), "CC": (f32, 96), "CM": (f32, 96),
+    "FT": (f32, 96), "FF": (f32, 96), "nl": (f32, 16), "lane": (f32, 16), "E0u": (u16, 32), "two": (f32, 144),
+    "SPd": (f32, 512), "m6": (f32, 144), "ex6": (u16, 16), "rp6": (u16, 6), "r6i": (i32, 6), "r6f": (f32, 6), "tg": (u16, 16), "fu": (u16, 16), "off": (u16, 16),
     "XI": (f16, 256), "AE": (f32, 256), "EQ": (bf, 1024), "OF": (f32, 256), "XL": (f16, 256), "ab": (bf, 256), "KL": (bf, 256),
-    "d2": (bf, 256), "d3": (bf, 256), "d4": (bf, 256), "d5": (bf, 256), "mv": (bf, 256), "oW": (f32, 256), "oW2": (f32, 256), "ZD": (f32, 256),
-    "pi": (i32, 4), "col": (f32, 16), "JmP": (f32, 128), "JB": (f32, 256), "J512": (f32, 512), "J5h": (f16, 512), "m16": (f32, 16),
+    "d2": (bf, 256), "d3": (bf, 256), "d4": (bf, 256), "d5": (bf, 256), "mv": (bf, 256), "oW": (f16, 256), "oW2": (f32, 256), "ZD": (f32, 256),
+    "pi": (i32, 4), "col": (f32, 16), "JmP": (f32, 128), "JB": (f32, 256), "Jlo": (bf, 512), "Jhi": (bf, 512), "m16": (f32, 16), "cst": (bf, 128),
     "I": (bf, 128), "I32": (f32, 128), "nI": (bf, 128), "I16": (bf, 128), "n16": (bf, 128), "n512": (bf, 128), "I4k": (bf, 128), "nI4k": (bf, 128),
     "BO": (bf, 128), "BOa": (bf, 128), "BO4k": (bf, 128), "nBO4k": (bf, 128), "BOw": (bf, 128), "BOp": (bf, 128), "S15": (bf, 128),
     "P1": (bf, 128), "P2": (bf, 128), "V0": (f32, 128), "V1": (f32, 128), "S0": (f32, 128), "S1": (f32, 128), "G8": (bf, 128), "G8n": (bf, 128),
-    "CW": (bf, 128), "one": (bf, 512), "DG": (bf, 256), "NEG": (bf, 256), "POS": (bf, 256), "TRI": (bf, 256), "CQ": (bf, 256),
+    "CW": (bf, 128), "one": (bf, 512), "DG": (bf, 256), "NEG": (bf, 256), "POS": (bf, 256), "TRI": (bf, 256), "CQ": (bf, 128),
+    "C14": (bf, 128), "S4k": (bf, 128), "BOp4k": (bf, 128),
 }
 SIZE = {f32: 4, i32: 4, bf: 2, f16: 2, u16: 2}
-GAT, FAR, WAKE, HOLD, GAP, PE = 1.56, 3500.0, 60.0, 0.5, 300.0, 0.7
+GAT, FAR, NEAR, WAKE, HOLD, GAP, PE, AHEAD = 1.8, 3500.0, 2000.0, 60.0, 0.4, 300.0, 0.65, 500.0
+UPPER = []
 HALF = 0.498
-LENGTH = [0.0]
+ORDER, LENGTH, ROUNDS = [], [0.0], 4
 HOME, _fill = {}, {}
 for _k, (_d, _n) in BUF.items():
     if _n <= 128 and _k not in ("bdi", "thi", "th2"):
@@ -48,7 +54,7 @@ for _d, _n in _fill.items():
     SCRATCH["sm_" + _d] = (S_, [128, _n], _d)
 for _b in range(8):
     SCRATCH["ps%d" % _b] = (P_, [128, 512], f32)
-NDMA = 40
+NDMA = 48
 SEMAPHORES = ["sv", "ss", "sp", "sg", "sent"] + ["dm%d" % k for k in range(NDMA)] + ["ar%d" % k for k in range(12)]
 ESEM = {"v": "sv", "s": "ss", "p": "sp", "g": "sg"}
 
@@ -82,10 +88,10 @@ def build(rank, T, send):
         if kind == "x":
             return (0.0, 0.0)
         if kind == "r":
-            return (300.0, 300.0 + FAR)
+            return (300.0, 300.0 + two)
         if kind == "d":
             x = out if out[0] != "@" else ins[0]
-            return (60.0 if q != "g" else 600.0, 2000.0 + (x[5] - x[4]) * (x[2] - x[1]) * SIZE[BUF[x[0]][0]] / 250.0)
+            return (60.0 if q != "g" else 600.0, 2000.0 + (x[5] - x[4]) * (x[2] - x[1]) * SIZE[BUF[x[0]][0]] / 450.0)
         vs = [x for x in [out] + ins if isinstance(x, tuple)]
         ind = [x for x in vs if x[0] == "*"]
         if ind:
@@ -97,12 +103,12 @@ def build(rank, T, send):
             if q == "p":
                 c = 30.0 + PE * max(64, n) * (4 if BUF[ins[0][0]][0] == f32 else 1)
             elif q == "g":
-                c = 150.0 + 2 * n
+                c = 1.5 * (150.0 + 2 * n)
             elif q == "s":
-                c = 65.0 + max(64, n)
+                c = 190.0 + max(64, n)
             else:
                 half = 0.5 if not ps and all(SIZE[BUF[x[0]][0]] == 2 for x in big) else 1.0
-                c = 50.0 + max(64, n * half * (2 if two and not ps else 1))
+                c = 105.0 + max(64, n * half * (2 if two and not ps else 1))
         return (c, c)
 
     def add(q, call, out, ins, kind="c", two=False):
@@ -127,9 +133,17 @@ def build(rank, T, send):
     def tr(o, a): add("v", lambda g: g.vector.transpose(ap(o), ap(a)), o, [a])
     def scan(o, a, b, op0, op1, also=()):
         add("v", lambda g: g.vector.tensor_tensor_scan(ap(o), ap(a), ap(b), 0.0, op0, op1), o, [a, b] + list(also))
-    def act(o, a, bias=0.0, scale=1.0, fn=Fn.Identity):
-        add("s", lambda g: g.scalar.activation(ap(o), ap(a), fn, bias=ap(bias), scale=ap(scale)), o, [a, bias, scale])
-    def move(q, o, a): cp(o, a) if q == "v" else act(o, a)
+    def act(o, a, bias=0.0, scale=1.0, fn=Fn.Identity, also=()):
+        add("s", lambda g: g.scalar.activation(ap(o), ap(a), fn, bias=ap(bias), scale=ap(scale)), o, [a, bias, scale] + list(also))
+    def move(q, o, a, c=0.0, scale=1.0):
+        if q == "s":
+            act(o, a, c, scale)
+        elif scale != 1.0:
+            ts2(o, a, scale, MU, c, AD)
+        elif c != 0.0:
+            ts(o, a, c, AD)
+        else:
+            cp(o, a)
     def mm(o, l, r, st=True, en=True): add("p", lambda g: g.tensor.matmul(ap(o), ap(l), ap(r), st, en), o, [l, r])
     def total(o, terms):
         for j, (l, r) in enumerate(terms):
@@ -140,21 +154,21 @@ def build(rank, T, send):
         else:
             add("g", lambda g: g.iota(ap(o), pat, base, ch, allow_small_or_imprecise_dtypes=True), o, [])
     def pick(o, a, pat, op, base, ch): add("g", lambda g: g.affine_select(ap(o), ap(a), pat, op, 0.0, base, ch), o, [a])
-    def dma(q, o, a):
-        add(q, lambda g: {"y": g.sync, "s": g.scalar, "g": g}[q].dma_start(ap(o), ap(a)), o, [a], "d")
+    def dma(q, o, a, also=()):
+        add(q, lambda g: {"y": g.sync, "s": g.scalar, "g": g}[q].dma_start(ap(o), ap(a)), o, [a] + list(also), "d")
     def PS(b, lo, n, st=1): return ("ps%d" % b, lo, lo + (n - 1) * st + 1, st, 0, 128)
     def C(j): return V("col", j, j + 1)
     def ext(x): return ("@", x)
     def TW(l): return "T%d" % (l % 2)
     def acol(l): return WA + l * M if l < 4 else WT
-    AD, SU, MU, MX, MN, EQ, NQ = Op.add, Op.subtract, Op.mult, Op.max, Op.min, Op.is_equal, Op.not_equal
+    AD, SU, MU, MX, MN, EQ = Op.add, Op.subtract, Op.mult, Op.max, Op.min, Op.is_equal
     RELU = Fn.Relu
 
     dma("y", V("A0"), ext(T.av[:, 0:M]))
     dma("s", V("bdi"), ext(T.bd[:, :]))
-    dma("y", V("dpi", 0, M), ext(T.dp[:, 0:M]))
-    dma("y", V("dpi", M, 2 * M), ext(T.dp[:, M:2 * M]))
-    dma("y", V("dpi", 2 * M, 4 * M), ext(T.dp[:, 2 * M:4 * M]))
+    dma("y", V("T1", M, 2 * M), ext(T.dp[:, 0:M]))
+    dma("y", V("T1", 2 * M, 3 * M), ext(T.dp[:, M:2 * M]))
+    dma("y", V("T1", 3 * M, E), ext(T.dp[:, 2 * M:4 * M]))
     dma("y", V("thi"), ext(T.th[:, :]))
     dma("y", V("sbi"), ext(T.sb[:, :]))
 
@@ -171,22 +185,28 @@ def build(rank, T, send):
     ms(V("one"), 1.0)
     iota(V("pi", 0, 1), [[0, 1]], 0, 1)
     iota(V("JmP"), [[1, 128]], 0, -1)
-    ms(V("T1", M, 3 * M), 0); fill_s("T1", 3 * M, E, 0.0); ms(V("T1", E, 2960), 128)
-    fill_s("R8", 0, 1024, -0.0625); ms(V("R8", 0, None, 8), 512.0)
-    fill_s("R0", 0, 1536, 0.0); ms(V("R0", 0, None, 16), 512.0)
-    fill_s("R16", 0, 1024, -0.0625); ms(V("R16", 0, None, 16), 512.0)
+    fill_s("T1", E, 2960, 128.0)
+    for name, st in (("R8", 8), ("R16", 16)):
+        ms(V(name, 0, M), -0.0625); ms(V(name, 0, M, st), 512.0)
+        for a in range(M, RN, M):
+            dma("y", N_(name, a, M), V(name, 0, M))
     ts(V("pi", 1, 2), V("pi", 0, 1), 4, Op.arith_shift_right)
     ts(V("pi", 2, 3), V("pi", 0, 1), 15, Op.bitwise_and)
     cp(V("col", 0, 3), V("pi", 0, 3))
     cp(V("bd0"), V("bdi", 0, 6))
-    fill_g("W", 0, IX + M, 0); fill_g("W", WS - 1, WT, 0); fill_g("W", WT + M, WN, 0)
+    fill_g("W", M, IX + M, 0); fill_g("W", E, E + 4, 0); fill_g("W", WS - 2, WS + 2, 0)
+    fill_g("W", WT - 2, WT + 2, 0); fill_g("W", WT + M - 2, WT + M + 2, 0)
+    fill_g("R0", 0, M, 0)
+    iota(V("R0", 0, M, 16), [[0, 32]], 512, 0)
+    for a in (M, 2 * M):
+        dma("y", N_("R0", a, M), V("R0", 0, M))
 
     def exchange(k):
-        add("g", send(k), None, [N_("stg", 96 * k, 96)], "r")
+        add("g", send(k), None, [N_("stg", 96 * k, 96)], "r", FAR if k % 4 else NEAR)
 
     def mirror(l):
         for a, n in ((l * M, M), (E + 96 * l, 96)):
-            dma("y", N_(TW(l), a, n), N_(TW(l + 1), a, n))
+            dma("y", N_(TW(l), a, n), N_(TW(l + 1), a, n), [N_(TW(l + 1), E + 96 * l, 96)])
 
     def ghosts(k, l):
         add("x", k, N_("land", 96 * k, 96), [], "x")
@@ -205,48 +225,58 @@ def build(rank, T, send):
         act(V("T1", 0, M), V("A0") if t == 0 else N_("W", WA, M), -127.0)
 
     release0(0)
-    dma("g", N_("W", WA + M, 3 * M), ext(T.av[:, M:4 * M]))
+    dma("g", N_("W", WA, 4 * M), ext(T.av[:, 0:4 * M]), [N_("stg", 0, 96)])
     dma("g", N_("W", WT, M), ext(T.av[:, 4 * M:E]))
     iota(V("JB"), [[0, 16], [1, 16]], 0, 0)
     iota(V("m16"), [[1, 16]], 0, 0)
-    iota(V("m5"), [[32, 16], [0, 5]], 0, 0)
-    iota(V("J512"), [[1, 512]], 0, 0)
+    iota(V("m6", 0, 96), [[32, 16], [0, 6]], WS - E, 0)
+    iota(V("m6", 96, 128), [[1, 2], [32, 16]], 4 * M + IX, 0)
+    iota(V("m6", 128, 144), [[32, 16]], WT - E, 0)
+    iota(V("Jlo", p1=32), [[0, 2], [1, 256]], 0, 0)
+    iota(V("Jhi", p1=32), [[256, 2], [0, 256]], 0, 0)
     ts(C(3), C(2), 8.0, Op.is_ge)
     ts(C(4), C(2), 8.0, Op.is_lt)
     ts2(V("V0"), V("JmP"), -8.0, EQ, C(3), MU)
     ts2(V("V1"), V("JmP"), 0.0, EQ, C(3), MU)
     ts2(V("S0"), V("JmP"), 0.0, EQ, C(4), MU)
     ts2(V("S1"), V("JmP"), 8.0, EQ, C(4), MU)
-    cp(N_("W", IX + M, M), V("dpi", 0, M))
-    act(N_("W", WA, M), V("A0"))
-    for l in range(4):
-        ts(V("bdW", 6 * l, 6 * l + 6), V("bdi", 6 * l, 6 * l + 6), float(IX + l * M), AD)
+    act(N_("W", IX + M, M), N_("T1", M, M))
+    ts(V("bdW"), V("bdi"), float(IX), AD)
 
     def split(plan):
-        return sum(x[1] for x in plan if x[0] == "F")
+        return sum(x[1] for x in plan if x[0] in "FW")
 
     def parts(l):
-        plan = PLAN if l < 4 else PLANT
-        ks = [x[1] for x in plan if x[0] == "F"]
-        return [(0, ks[0]), (ks[0], sum(ks[1:]))] if l == 1 else [(0, sum(ks))]
+        ks = [x[1] for x in (PLAN if l < 4 else PLANT) if x[0] in "FW"]
+        if l == 1:
+            return [(0, ks[0] + ks[1]), (ks[0] + ks[1], sum(ks[2:]))]
+        return [(0, sum(ks))] if l < 4 or sum(ks) <= HN else [(0, HN), (HN, sum(ks) - HN)]
+
+    def place(l, c):
+        return c if l < 4 else (c + HN) % LN
+
+    def runs(l, c, k):
+        return [(c, k)] if l < 4 or c >= HN or c + k <= HN else [(c, HN - c), (HN, c + k - HN)]
 
     def lists(l, par):
         plan, st = (PLAN, 1) if l < 4 else (PLANT, 2)
         c0 = IX + l * M + (par if l == 4 else 0)
         nf, n, lu = split(plan), (M if l < 4 else LN), (l - 1) * M
         if l < 4:
-            move(LISTQ[l][0], N_("DLU", 96 * (l - 1), 96), IND(N_("W", 0, IX + (l + 1) * M), V("bdW", 6 * l, 6 * l + 6)))
-        if n > nf:
-            move(LISTQ[l][0], N_("LU", lu + nf, n - nf), N_("W", c0 + nf * st, n - nf, st))
+            move(LISTQ[l][0], N_("DLU", 96 * (l - 1), 96), IND(N_("W", l * M, IX + M), V("bdW", 6 * l, 6 * l + 6)))
+        for a, k in (runs(l, nf, n - nf) if n > nf else []):
+            move(LISTQ[l][0], N_("LU", lu + a, k), N_("W", c0 + place(l, a) * st, k, st))
         for i, (a, k) in enumerate(parts(l) if nf else []):
-            h, bb = k // 2, ((2, 3), (5,), (6,), (7,))[l - 1][i]
+            h, bb, c = k // 2, ((2, 3), (5,), (6,), (7, 2))[l - 1][i], c0 + place(l, a) * st
             for j, (a0, a1) in enumerate((("S0", "S1"), ("V0", "V1"))):
-                total(PS(bb, j * h, h), [(V(a0), N_("W", c0 + a * st, h, 2 * st)), (V(a1), N_("W", c0 + (a + 1) * st, h, 2 * st))])
+                total(PS(bb, j * h, h), [(V(a0), N_("W", c, h, 2 * st)), (V(a1), N_("W", c + st, h, 2 * st))])
             move(LISTQ[l][1], N_("LU", lu + a, k), PS(bb, 0, k))
 
     def own_keys(l, par):
         n, st = (M, 1) if l < 4 else (LN, 2)
-        total(PS(l % 2, 0, n), [(V("CW", p1=64), V("one", 0, n, p1=64)), (V("I32"), N_("W", acol(l) + (par if l == 4 else 0), n, st))])
+        for a in range(0, n, HN):
+            total(PS(l % 2, a, HN), [(V("CW", p1=64), V("one", 0, HN, p1=64)),
+                                     (V("I32"), N_("W", acol(l) + (par if l == 4 else 0) + a * st, HN, st))])
 
     lists(1, 0)
     pick(V("I"), V("one", 0, 128), [[-1, 128]], EQ, 0, 1)
@@ -258,21 +288,33 @@ def build(rank, T, send):
     ts(V("P2"), V("JmP"), C(6), EQ)
     ms(V("CW", p1=64), 0.0); ms(V("CW", p1=1), -128.0); ms(V("CW", p0=32, p1=33), 1.0 / 256)
     own_keys(1, 0)
-    act(N_("W", IX + 2 * M, M), V("dpi", M, 2 * M))
-    fill_g("T0", M, E, 0); fill_g("T0", E + 96, 2960, 128)
+    for l in (2, 3, 4):
+        act(N_("W", IX + l * M, M), N_("T1", l * M, M))
+    fill_g("T0", 2 * M, E, 0); fill_g("T0", E + 96, 2960, 128)
 
     def late_setup():
-        cp(N_("W", IX + 3 * M, M), V("dpi", 2 * M, 3 * M))
-        act(N_("W", IX + 4 * M, M), V("dpi", 3 * M, 4 * M))
-        fill_g("U", 0, IX + M, STOP); fill_g("U", IX + 4 * M, WN, STOP)
-        fill_g("SD", 0, IX, 0); fill_g("SD", IX + 4 * M, IX + E, 0); fill_g("SD", IX + NONE, 2960, 0)
-        fill_g("H", 0, 1, 0); fill_g("SPd", 0, 512, -30000); fill_g("RM", 0, LN, 0); fill_g("RM0", 0, LN, 1)
-        iota(V("RM", 0, None, 16), [[0, 16]], -8192, 0)
-        iota(V("RM0", 0, None, 16), [[0, 16]], 0, 0)
-        pick(V("BOa"), V("one", 0, 128), [[-16, 8], [0, 16]], Op.is_ge, 0, 1)
-        pick(V("BO"), V("BOa"), [[16, 8], [0, 16]], Op.is_ge, 15, -1)
+        fill_g("W", 0, M, 0); fill_g("W", WS + 2, WT - 2, 0); fill_g("W", WT + M + 2, WN, 0)
+        fill_g("U", 0, IX + M, STOP); fill_g("U", IX + 4 * M, 5640, STOP)
+        fill_g("SD", 0, IX, 0); fill_g("SD", IX + 4 * M, IX + E, 0); fill_g("SD", IX + NONE, 3088, 0)
+        fill_g("H", 0, 112, 0); fill_g("SPd", 0, 512, -30000); fill_g("RM", 0, HN, 0); fill_g("RM0", 0, LN, 1)
+        iota(V("RM", 0, HN, 16), [[0, 8]], -8192, 0)
+        iota(V("RM0", 0, LN, 16), [[0, 16]], 0, 0)
         pick(V("S15"), V("one", 0, 128), [[-16, 8], [0, 16]], EQ, -15, 1)
         pick(V("G8"), V("one", 0, 128), [[-1, 8], [0, 16]], EQ, 0, 1)
+        pick(V("BOa"), V("one", 0, 128), [[-16, 8], [0, 16]], Op.is_ge, 0, 1)
+        pick(V("BO"), V("BOa"), [[16, 8], [0, 16]], Op.is_ge, 15, -1)
+        for c, eye, block in ((-1, "nI", None), (16, "I16", None), (-16, "n16", None), (-512, "n512", None),
+                              (4096, "I4k", "BO4k"), (-4096, "nI4k", "nBO4k"), (16384, None, "BOw")):
+            fill_g("cst", 0, 128, c)
+            if eye:
+                pick(V(eye), V("cst"), [[-1, 128]], EQ, 0, 1)
+            if block:
+                pick(V("BOa"), V("cst"), [[-16, 8], [0, 16]], Op.is_ge, 0, 1)
+                pick(V(block), V("BOa"), [[16, 8], [0, 16]], Op.is_ge, 15, -1)
+            if c == -1:
+                pick(V("G8n"), V("cst"), [[-1, 8], [0, 16]], EQ, 0, 1)
+            if c == 4096:
+                pick(V("S4k"), V("cst"), [[-16, 8], [0, 16]], EQ, -15, 1)
         ts(V("DG"), V("JB"), C(2), EQ)
         ts2(V("TRI"), V("JB"), C(2), Op.is_le, -8192.0, MU)
         ts2(C(7), C(2), -1.0, MU, -1.0, AD)
@@ -280,104 +322,219 @@ def build(rank, T, send):
         ts(C(9), C(2), 0.5, AD)
         ts2(C(10), C(2), 4096.0, MU, -29696.0 - 8192.0, AD)
         ts(C(11), C(2), 0.0625, MU)
-        for name, src, c in (("nI", "I", -1.0), ("I16", "I", 16.0), ("n16", "I", -16.0), ("n512", "I", -512.0), ("I4k", "I", 4096.0),
-                             ("nI4k", "I", -4096.0), ("BO4k", "BO", 4096.0), ("nBO4k", "BO", -4096.0), ("BOw", "BO", 16384.0),
-                             ("BOp", "BO", C(11)), ("G8n", "G8", -1.0)):
-            ts(V(name), V(src), c, MU)
+        ts(V("BOp"), V("BO"), C(11), MU)
+        ts(V("BOp4k"), V("BOp"), 4096.0, MU)
+        ts2(V("C14"), V("one", 0, HN), C(8), MU, 4096.0, MU)
         ts2(V("NEG"), V("DG"), 4096.0, MU, -4096.0, AD)
         ts2(V("POS"), V("DG"), -16384.0, MU, 16384.0, AD)
-        ts2(V("CQ"), V("DG"), 8192.0, MU, C(10), AD)
+        ts2(V("CQ"), V("DG", 0, HN), 8192.0, MU, C(10), AD)
         cp(V("th2"), V("thi"))
         dma("y", V("thh", p1=8), V("th2"))
-        cp(V("J5h", p1=8), V("J512", p1=8))
         ts(V("sb2"), V("sbi"), -1024.0, AD)
         dma("y", V("sbh", p1=8), V("sb2"))
-        mm(PS(5, 0, M), V("G8", p1=8), V("thh", p1=8))
-        act(V("thB"), PS(5, 0, M), -127.0)
-        for j in range(5):
-            n = M if j < 4 else G
-            b = 6 + j % 2
-            total(PS(b, 0, n), [(V("G8", p1=8), V("sbh", j * M, j * M + n, p1=8)), (V("G8n", p1=8), V("J5h", 0, n, p1=8))])
-            nm = j * M if j < 4 else E
-            act(N_("SD", IX + nm, n), PS(b, 0, n), float(1024 - nm))
         ts2(V("lane"), V("m16"), 16.0, MU, C(2), AD)
-        ts2(V("m5"), V("m5"), C(2), AD, C(2), AD)
+        ts2(V("two"), V("m6"), C(2), AD, C(2), AD)
         for par in (0, 1):
-            ts2(N_("E0", 16 * par, 16), V("lane"), 2.0, MU, float(4 * M + IX + par), AD)
             ts(N_("SPd", LN * par, 16, 16), V("lane"), float(WT + M - E - par), AD)
-        ts2(V("T00", 0, 16), V("lane"), 2.0, MU, float(WT - E), AD)
-        ts(V("SP5", 0, 80), V("m5"), float(WS - E), AD)
-        cp(V("E0u"), V("E0"))
-        ts2(V("ex5"), V("m16"), 5.0, MU, 4.0, AD)
-        ts2(V("G1", 0, 6), V("m16", 0, 6), 16.0, MU, C(2), AD)
-        ts2(V("G1", 8, 14), V("G1", 0, 6), 0.2, MU, -0.4, AD)
-        cp(V("r5i"), V("G1", 8, 14))
-        cp(V("rp5"), V("r5i"))
+        cp(V("E0u"), V("two", 96, 128))
+        ts2(V("ex6"), V("m16"), 6.0, MU, 4.0, AD)
+        ts2(V("r6f"), V("lane", 0, 6), 1.0 / 6, MU, -5.0 / 12, AD)
+        cp(V("r6i"), V("r6f"))
+        cp(V("rp6"), V("r6i"))
+
+    def spread():
+        for j in (5, 0, 1, 2, 3, 4):
+            if j == 5:
+                mm(PS(5, 0, M), V("G8", p1=8), V("thh", p1=8))
+                act(V("thB"), PS(5, 0, M), -127.0)
+            else:
+                n, nm, b = (M, j * M, 6 + j % 2) if j < 4 else (G, E, 6)
+                total(PS(b, 0, n), [(V("G8", p1=8), V("sbh", j * M, j * M + n, p1=8)), (V("G8n", p1=8), V("Jlo", 0, n, p1=8)),
+                                    (V("G8n", p1=8), V("Jhi", 0, n, p1=8))])
+                act(N_("SD", IX + nm, n), PS(b, 0, n), float(1024 - nm))
 
     def level(t, l, fill):
         plan, n = (PLAN, M) if l < 4 else (PLANT, LN)
         nf, lu, win = split(plan), (l - 1) * M, V(TW(l), 0, NONE + 1)
-        fo, so = 0, nf
-        done = {"F": 0, "S": nf}
+        at, scanned, done = {"F": 0, "S": nf, "R": 0}, {"F": 0, "S": nf}, {"F": 0, "S": nf}
 
         def cols(j):
-            a, kk = [x for x in parts(l) if x[0] <= fo][-1]
-            return N_("LU", lu + a + j * (kk // 2) + (fo - a) // 2, k // 2)
+            a, kk = [x for x in parts(l) if x[0] <= at["F"]][-1]
+            return N_("LU", lu + a + j * (kk // 2) + (at["F"] - a) // 2, k // 2)
 
-        def finish(c, k, ends):
-            u = N_("U", IX + l * M + c, k) if l < 4 else N_("U", IX + l * M + (t & 1) + 2 * c, k, 2)
-            tt(u, ends, PS(l % 2, c, k), MN)
-            if l < 4 and c + k == n:
-                ts(N_(TW(l + 1), l * M + c, k), u, HALF, AD)
-            else:
-                act(N_(TW(l + 1), l * M + c, k) if l < 4 else N_("Ti", c, k), u, HALF)
+        def finish(c0, k0, w):
+            for c, k in runs(l, c0, k0):
+                e = place(l, c)
+                u = N_("U", IX + l * M + c, k) if l < 4 else N_("U", IX + l * M + (t & 1) + 2 * e, k, 2)
+                tt(u, N_("SO", w * c + w - 1, k, w), PS(l % 2, e, k), MN)
+                if l < 4:
+                    move("v" if j == len(plan) - 1 else "s", N_(TW(l + 1), l * M + c, k), u, HALF)
+                else:
+                    move(DATEQ[c // HN], N_("Ti", e, k), u, HALF)
 
         for j, (kind, k, fin) in enumerate(plan):
-            if kind == "F":
-                e0, e = 8 * fo, 8 * k
-                act(N_("PF", e0, e), IND(win, cols(0)), -0.5)
+            if kind in "FW":
+                e0, e = 8 * at["F"], 8 * k
+                move("s" if kind == "F" else "v", N_("PF", e0, e), IND(win, cols(0)), -0.5)
             elif kind == "S":
-                act(N_("GS", 16 * so, 16 * k), IND(win, N_("LU", lu + so, k)))
+                act(N_("GS", 16 * at["S"], 16 * k), IND(win, N_("LU", lu + at["S"], k)))
             elif kind == "R":
-                act(N_("GS", 8192, 1536), IND(win, N_("DLU", 96 * (l - 1), 96)), 127.0)
-            if kind != "V":
+                act(N_("GS", 8192 + 16 * at["R"], 16 * k), IND(win, N_("DLU", 96 * (l - 1) + at["R"], k)), 127.0)
+                at["R"] += k
+            if kind not in "VW":
                 chain.append(len(ops) - 1)
             if j == 0:
                 fill()
-            if kind == "F":
-                tt(N_("PR", e0, e), IND(win, cols(1)), N_("PF", e0, e), MN)
-                scan(N_("SO", e0, e), N_("R8", 0, e), N_("PR", e0, e), AD, MN)
-                fo += k
-                if fin or fo == nf:
-                    finish(done["F"], fo - done["F"], N_("SO", 8 * done["F"] + 7, fo - done["F"], 8))
-                    done["F"] = fo
-            elif kind in "SV":
-                if kind == "V":
-                    cp(N_("GS", 16 * so, 16 * k), IND(win, N_("LU", lu + so, k)))
-                scan(N_("SO", 16 * so, 16 * k), N_("R16", 0, 16 * k), N_("GS", 16 * so, 16 * k), AD, MN)
-                so += k
-                if fin or so == n:
-                    finish(done["S"], so - done["S"], N_("SO", 16 * done["S"] + 15, so - done["S"], 16))
-                    done["S"] = so
-            else:
+            if kind == "R" and at["R"] < 96:
+                continue
+            if kind == "R":
                 scan(N_("SB", 0, 1536), N_("R0", 0, 1536), N_("GS", 8192, 1536), AD, MN)
                 x = 4 * t + l
-                tt(N_("stg", 96 * x, 96), IND(V("W", E, WA + (l + 1) * M), V("bdW", 6 * l, 6 * l + 6)), N_("SB", 15, 96, 16), MN)
+                tt(N_("stg", 96 * x, 96), IND(N_("W", E + l * M, IX + M), V("bdW", 6 * l, 6 * l + 6)), N_("SB", 15, 96, 16), MN)
                 exchange(x)
+                continue
+            if kind in "FW":
+                tt(N_("PR", e0, e), IND(win, cols(1)), N_("PF", e0, e), MN)
+            if kind == "V":
+                cp(N_("GS", 16 * at["S"], 16 * k), IND(win, N_("LU", lu + at["S"], k)))
+            z, w, src, step = ("F", 8, "PR", "R8") if kind in "FW" else ("S", 16, "GS", "R16")
+            at[z] += k
+            if fin:
+                a, e = w * scanned[z], w * (at[z] - scanned[z])
+                scan(N_("SO", a, e), N_(step, 0, e), N_(src, a, e), AD, MN)
+                scanned[z] = at[z]
+            if fin == 2:
+                finish(done[z], at[z] - done[z], w)
+                done[z] = at[z]
+
+    def odd_gathers(js):
+        for j in js:
+            move("v" if NW <= j < NW + NV else "s", N_("GS", 256 * j, 256), IND(V(TW(4), 0, NONE + 1), N_("OLU", 16 * j, 16)), 127.0)
 
     def odd_tops():
-        for a, n in ((0, 1536), (1536, 1536), (3072, 1024)):
-            scan(N_("SB", a, n), N_("R0", 0, n), N_("GS", a, n), AD, MN, [N_("W", 0, 16)])
-        tt(N_("yrs", 1, LN, 2), N_("SB", 15, LN, 16), N_("W", WT + 1, LN, 2), MN)
+        act(N_("OLU", 16 * NW, LN - 16 * NW), N_("W", IX + 4 * M + 1 + 32 * NW, LN - 16 * NW, 2))
+        odd_gathers(range(NW, 16))
+        for a, n in ((0, 96), (96, 96), (192, 48), (240, 16)):
+            scan(N_("SB", 16 * a, 16 * n), N_("R0", 0, 16 * n), N_("GS", 16 * a, 16 * n), AD, MN)
+            tt(N_("yrs", 1 + 2 * a, n, 2), N_("SB", 16 * a + 15, n, 16), N_("Ao", a, n), MN)
+
+    def views(h, nh):
+        def Hf(name): return N_(name, HN * h, HN * nh)
+        def L(name, at=0): return N_(name, at + 8 * h, 8 * nh)
+        def Six(name, at=0): return N_(name, at + 48 * h, 48 * nh)
+        def Slot(name, s): return N_(name, s + 48 * h, 8 * nh, 6)
+        def Ends(name): return N_(name, HN * h + 15, 8 * nh, 16)
+        def K(name): return N_(name, 0, HN * nh)
+        def B(k, j=0): return PS(((7, 3, 5, 0), (6, 2, 4, 1))[h][k], HN * nh * j, HN * nh)
+        return Hf, L, Six, Slot, Ends, K, B
+
+    def caps(h, nh, par):
+        Hf, L, Six, Slot, Ends, K, B = views(h, nh)
+        act(Six("Hd"), Six("H"), -float(E + par))
+        tt(Six("G1"), IND(L("nl"), V("rp6", 0, 3 * nh)), Six("Hd"), AD)
+        tt(Six("G2"), Six("G1"), Six("two"), MN)
+
+    def lanes(h, par):
+        Hf, L, Six, Slot, Ends, K, B = views(h, 1)
+        move(DATEQ[1 - h], Hf("k2"), Hf("Ti"), C(7), 16.0)
+        tr(Hf("k2a"), Hf("k2"))
+        scan(Hf("k2b"), N_("RM", 0, HN), Hf("k2a"), AD, MX)
+        tr(Hf("k2c"), Hf("k2b"))
+        total(B(0), [(V("nI"), Hf("k2")), (V("S15"), Hf("k2c"))])
+        act(Hf("DM"), B(0), 16.0, -16.0, RELU)
+        total(B(0, 1), [(V("S15"), Hf("k2c")), (V("BOp"), Hf("DM"))])
+        act(Hf("n1"), B(0, 1), C(8))
+        act(Slot("H", 1), L("two", 96 + 16 * par))
+
+        def aside(s):
+            if s == 1:
+                act(Hf("Tb"), Hf("Ti"))
+                act(Hf("d2"), Hf("Ti"), -111.0, -1.0, RELU)
+                total(B(3, 2), [(V("I"), N_("thB", par + LN * h, HN, 2)), (V("nI"), Hf("Tb")), (V("I16"), Hf("DM"))])
+                act(Hf("d3"), B(3, 2), -256.0, 1.0, RELU)
+            if s == 2:
+                total(B(3, 3), [(V("I"), K("NEG")), (V("BO"), Hf("d3"))])
+                scan(Hf("SW"), K("RM0"), B(3, 3), MU, MX)
+                act(L("nl"), Ends("SW"), 8192.0, -8192.0, RELU)
+                total(B(0), [(V("nI"), Hf("n1")), (V("BO"), Hf("X1"))])
+                act(Hf("mv"), B(0), C(9), 1.0, RELU)
+            if s == 3:
+                total(B(3, 2), [(V("nI"), Hf("d2")), (V("n16"), Hf("d3")), (V("I16"), Hf("DM"))])
+                act(Hf("d4"), B(3, 2), -240.0, 1.0, RELU)
+                total(B(0), [(V("I"), Hf("d3")), (V("n512"), Hf("mv"))])
+                act(Hf("d5"), B(0), 0.0, 1.0, RELU)
+                if JOIN[0] == 1 or h == 0:
+                    caps(h, JOIN[0], par)
+
+        for s in range(1, 5):
+            lst = L("E0u", 16 * par) if s == 1 else L("FL", 16 * (s - 1))
+            x = Hf("X1" if s == 1 else "X")
+            act(Hf("Dg"), IND(N_("W", 0, 2960), lst), float(IX - 1024))
+            tt(x, IND(N_("U", 0, 2960), lst), Hf("DM"), MU)
+            own = [(V("I4k"), Hf("n1"))] if s > 1 else [(V("I"), V("C14")), (V("S4k"), Hf("k2c")), (V("BOp4k"), Hf("DM"))]
+            total(B(1), own + [(V("I"), Hf("Dg")), (V("nBO4k"), x)])
+            ts2(Hf("Y"), B(1), -2048.0, MX, 2048.0, MN)
+            total(B(2), [(V("I"), V("CQ")), (V("nI4k"), Hf("n1")), (V("BO4k"), x), (V("BO"), Hf("Y"))])
+            scan(Hf("SV"), N_("RM0", 0, HN), B(2), MU, MX)
+            ends = N_("SV", HN * h + 15, 8, 16)
+            if s < 4:
+                move(NEXTQ[1 - h], L("FL", 16 * s), ends)
+                act(Slot("H", 1 + s), ends)
+                aside(s)
+            else:
+                cp(Slot("H", 5), ends)
+
+    def targets(h, nh, par):
+        Hf, L, Six, Slot, Ends, K, B = views(h, nh)
+        hh = Six("H", 1)
+        act(Six("MV"), hh, 0.0, 1.0, Fn.Sign)
+        act(Six("Z"), hh, 1.0, -1.0, RELU)
+        if par:
+            ts(Six("Hd"), hh, -1.0, AD)
+        tt(Six("CC"), Six("Hd") if par else hh, Six("G2"), MN)
+        act(Slot("CC", 0), L("two", 128))
+        tt(Six("CM"), Six("CC"), Six("MV"), MU)
+        scan(Six("FT"), Six("Z"), Six("CM"), MU, AD)
+        act(L("tg"), Slot("FT", 4), float(E + par))
+        scan(Six("FF"), Six("Z"), hh, MU, AD)
+        act(L("fu"), Slot("FF", 4))
+
+    def contest(h, nh, par):
+        Hf, L, Six, Slot, Ends, K, B = views(h, nh)
+        wide, ids = HN * nh, IND(Six("FT"), V("ex6", 0, 8 * nh))
+        tt(Hf("XI"), ids, K("DG"), MU)
+        act(Hf("AE"), ids)
+        mm(B(1), V("BO"), Hf("XI"))
+        total(B(1, 1), [(V("I"), K("TRI")), (V("BO"), Hf("XI"))])
+        tt(Hf("XL"), IND(V("U"), L("tg")), Hf("DM"), MU)
+        act(Hf("oW"), IND(V("W"), L("tg")), -1024.0)
+        total(B(0), [(V("nI"), Hf("n1")), (V("BO"), Hf("XL"))])
+        total(B(3, 2), [(V("I"), Hf("d5")), (V("nI"), Hf("d4")), (V("I"), Hf("oW"))])
+        act(Hf("ab"), B(0), 0.0, 1.0, Fn.Abs)
+        act(Hf("KL"), Hf("ab"), 1.0, -1.0, RELU)
+        act(Hf("oW2"), B(3, 2), 1024.0)
+        x2, b0 = B(2), B(1)
+        mm(x2, V("I"), K("POS"), True, False)
+        mm(x2, V("BO"), Hf("XI"), False, False)
+        for d in list(range(1, 16 // BLOCKS)) + [0]:
+            n = wide - 16 * d
+            eq = N_("EQ", LN * d + HN * h, n)
+            tt(eq, N_("AE", HN * h, n), (b0[0], 16 * d, wide, 1, 0, 128) if d else B(1, 1), EQ)
+            mm((x2[0], 16 * d, wide, 1, 0, 128), V("BOw"), eq, False, d == 0)
+        tt(Hf("ZD"), IND(V("SD"), L("fu")), Hf("KL"), MU)
+        scan(Hf("OF"), N_("SPd", LN * par + HN * h, wide), x2, MX, MN)
+        ts(L("off"), Ends("OF"), float(E + par), AD)
 
     for t in range(NP):
         par, last = t & 1, t == NP - 1
         if t == 0:
             late_setup()
+            spread()
         for l in range(2, 5):
             lists(l, par)
         if last:
-            act(V("OLU"), N_("W", IX + 4 * M + 1, LN, 2))
+            act(N_("OLU", 0, 16 * NW), N_("W", IX + 4 * M + 1, 16 * NW, 2))
+            act(V("Ao"), N_("W", WT + 1, LN, 2))
         ghosts(4 * t, 0)
         for l in range(1, 5):
             def fill(l=l):
@@ -386,106 +543,18 @@ def build(rank, T, send):
             level(t, l, fill)
             if l < 4:
                 ghosts(4 * t + l, l)
-        hn = LN // HALVES
-        hs = [(h, h * hn, h * hn // 16, hn // 16) for h in range(HALVES)]
-        for h in hs:
-            def Hf(name): return N_(name, h[1], hn)
-            act(Hf("k2"), Hf("Ti"), C(7), 16.0)
-            tr(Hf("k2a"), Hf("k2"))
-            scan(Hf("k2b"), N_("RM", 0, hn), Hf("k2a"), AD, MX)
-            tr(Hf("k2c"), Hf("k2b"))
-            total(PS(6 + h[0], 0, hn), [(V("nI"), Hf("k2")), (V("S15"), Hf("k2c"))])
-            act(Hf("DM"), PS(6 + h[0], 0, hn), 16.0, -16.0, RELU)
-            total(PS(6 + h[0], hn, hn), [(V("S15"), Hf("k2c")), (V("BOp"), Hf("DM"))])
-            act(Hf("n1"), PS(6 + h[0], hn, hn), C(8))
-        act(N_("H", 1, 16, 5), N_("E0", 16 * par, 16))
+        first = len(ops)
+        lanes(1, par)
+        targets(1, 1, par)
+        contest(1, 1, par)
+        UPPER.extend(range(first, len(ops)))
+        lanes(0, par)
+        targets(0, 1, par)
+        contest(0, 1, par)
         if last:
             act(V("yrs", 0, M, 2), V("Ti"), 127.0)
-            for j in range(16):
-                act(N_("GS", 256 * j, 256), IND(V(TW(4), 0, NONE + 1), N_("OLU", 16 * j, 16)), 127.0)
-
-        def aside(s):
-            if s == 1:
-                act(V("Tb"), V("Ti"))
-                act(V("d2"), V("Ti"), -111.0, -1.0, RELU)
-                total(PS(1, 0, LN), [(V("I"), V("thB", par, M, 2)), (V("nI"), V("Tb")), (V("I16"), V("DM"))])
-                act(V("d3"), PS(1, 0, LN), -256.0, 1.0, RELU)
-            if s == 2:
-                total(PS(1, 0, LN), [(V("I"), V("NEG")), (V("BO"), V("d3"))])
-                scan(V("SW"), V("RM0"), PS(1, 0, LN), MU, MX)
-                act(V("nl"), N_("SW", 15, 16, 16), 8192.0 - E - par, -8192.0)
-                total(PS(0, 0, LN), [(V("nI"), V("n1")), (V("BO"), V("X1"))])
-                act(V("mv"), PS(0, 0, LN), C(9), 1.0, RELU)
-            if s == 3:
-                ts(V("nl"), V("nl"), -float(E + par), MX)
-                total(PS(1, 0, LN), [(V("nI"), V("d2")), (V("n16"), V("d3")), (V("I16"), V("DM"))])
-                act(V("d4"), PS(1, 0, LN), -240.0, 1.0, RELU)
-                total(PS(0, 0, LN), [(V("I"), V("d3")), (V("n512"), V("mv"))])
-                act(V("d5"), PS(0, 0, LN), 0.0, 1.0, RELU)
-            if s == 4:
-                tt(V("G1"), IND(V("nl"), V("rp5", 0, 5)), N_("H", 0, 80), AD)
-                tt(V("G2"), V("G1"), V("SP5", 0, 80), MN)
-
-        for s in range(1, 5):
-            def lst(h): return N_("E0u", 16 * par + h[2], h[3]) if s == 1 else N_("FL", 16 * (s - 1) + h[2], h[3])
-            xn = "X1" if s == 1 else "X"
-            if s == 4:
-                fill_h = N_("H", 5, 16, 5)
-                if t == 0:
-                    ms(fill_h, 0.0)
-                aside(4)
-            for h in hs:
-                def Hf(name): return N_(name, h[1], hn)
-                act(Hf("Dg"), IND(N_("W", 0, 2960), lst(h)), float(IX - 1024))
-                tt(Hf(xn), IND(N_("U", 0, 2960), lst(h)), Hf("DM"), MU)
-                total(PS(2 + h[0], 0, hn), [(V("I4k"), Hf("n1")), (V("I"), Hf("Dg")), (V("nBO4k"), Hf(xn))])
-            for h in hs:
-                def Hf(name): return N_(name, h[1], hn)
-                ts2(Hf("Y"), PS(2 + h[0], 0, hn), -2048.0, MX, 2048.0, MN)
-                total(PS(4 + h[0], 0, hn), [(V("I"), N_("CQ", 0, hn)), (V("nI4k"), Hf("n1")), (V("BO4k"), Hf(xn)), (V("BO"), Hf("Y"))])
-            for h in hs:
-                scan(N_("SV", h[1], hn), N_("RM0", 0, hn), PS(4 + h[0], 0, hn), MU, MX)
-                ends = N_("SV", h[1] + 15, h[3], 16)
-                if s < 4:
-                    act(N_("FL", 16 * s + h[2], h[3]), ends)
-                    act(N_("H", 1 + s + 5 * h[2], h[3], 5), ends)
-            if s == 4:
-                cp(N_("H", 5, 16, 5), N_("SV", 15, 16, 16))
-            else:
-                aside(s)
-        hh = N_("H", 1, 80)
-        act(V("MV"), hh, 0.0, 1.0, Fn.Sign)
-        act(V("Z"), hh, 1.0, -1.0, RELU)
-        if par:
-            ts(V("Hd"), hh, -1.0, AD)
-        tt(V("CC"), V("Hd") if par else hh, V("G2"), MN)
-        act(N_("CC", 0, 16, 5), V("T00", 0, 16))
-        tt(V("CM"), V("CC"), V("MV"), MU)
-        scan(V("FT"), V("Z"), V("CM"), MU, AD)
-        tt(V("XI"), IND(V("FT"), V("ex5")), V("DG"), MU)
-        act(V("tg"), N_("FT", 4, 16, 5), float(E + par))
-        act(V("AE"), IND(V("FT"), V("ex5")))
-        mm(PS(3, 0, LN), V("BO"), V("XI"))
-        total(PS(2, 0, LN), [(V("I"), V("TRI")), (V("BO"), V("XI"))])
-        scan(V("FF"), V("Z"), hh, MU, AD)
-        act(V("fu"), N_("FF", 4, 16, 5))
-        tt(V("XL"), IND(V("U"), V("tg")), V("DM"), MU)
-        act(V("oW"), IND(V("W"), V("tg")))
-        total(PS(5, 0, LN), [(V("nI"), V("n1")), (V("BO"), V("XL"))])
-        total(PS(6, 0, LN), [(V("I"), V("d5")), (V("nI"), V("d4")), (V("I32"), V("oW"))])
-        act(V("ab"), PS(5, 0, LN), 0.0, 1.0, Fn.Abs)
-        act(V("KL"), V("ab"), 1.0, -1.0, RELU)
-        act(V("oW2"), PS(6, 0, LN))
-        mm(PS(4, 0, LN), V("I"), V("POS"), True, False)
-        mm(PS(4, 0, LN), V("BO"), V("XI"), False, False)
+            odd_gathers(range(NW))
         nd = 16 // BLOCKS
-        for d in list(range(1, nd)) + [0]:
-            n = LN - 16 * d
-            tt(N_("EQ", LN * d, n), N_("AE", 0, n), PS(3 if d else 2, 16 * d, n), EQ)
-            mm(PS(4, 16 * d, n), V("BOw"), N_("EQ", LN * d, n), False, d == 0)
-        tt(V("ZD"), IND(V("SD"), V("fu")), V("KL"), MU)
-        scan(V("OF"), N_("SPd", LN * par, LN), PS(4, 0, LN), MX, MN)
-        ts(V("off"), N_("OF", 15, 16, 16), float(E + par), AD)
         for b in range(BLOCKS - 1, -1, -1):
             tt(IND(V("W"), N_("off", nd * b, nd)), N_("oW2", 16 * nd * b, 16 * nd), N_("ZD", 16 * nd * b, 16 * nd), AD)
         if not last:
@@ -509,37 +578,54 @@ def arrange(ops, deps, chain):
     for i in range(n):
         for j in deps[i]:
             after[j].append(i)
+    busy = [x[5][0] for x in ops]
+
+    def lag(a, b):
+        return ops[a][5][1] - busy[a] + (0.0 if (ops[a][0] == "p" and ops[b][0] == "p") or soft.get(b) == a else WAKE)
+
+    def run(prio, before, behind, back):
+        left, ready, end = [len(d) for d in before], [ops[i][5][1] - busy[i] if back else 0.0 for i in range(n)], [0.0] * n
+        free = {q: 0.0 for q in "vspgyx"}
+        open_ = {q: [i for i in range(n) if ops[i][0] == q and not before[i]] for q in free}
+        order = []
+        while len(order) < n:
+            pick = None
+            for q, cand in open_.items():
+                if not cand:
+                    continue
+                t = max(free[q], min(ready[i] for i in cand))
+                b = max((i for i in cand if ready[i] <= t), key=lambda i: (prio[i], -i))
+                for h in cand:
+                    if t < ready[h] < t + HOLD * busy[b] and prio[h] > prio[b] + GAP:
+                        b = h
+                s = max(free[q], ready[b])
+                if pick is None or s < pick[0]:
+                    pick = (s, q, b)
+            s, q, b = pick
+            open_[q].remove(b)
+            order.append(b)
+            free[q] = end[b] = s + busy[b]
+            for k in behind[b]:
+                ready[k] = max(ready[k], end[b] + (lag(k, b) if back else lag(b, k)))
+                left[k] -= 1
+                if not left[k]:
+                    open_[ops[k][0]].append(k)
+        return order, end
+
     prio = [0.0] * n
     for i in range(n - 1, -1, -1):
         prio[i] = ops[i][5][1] + max([prio[k] + WAKE for k in after[i]], default=0.0)
-    left, ready = [len(d) for d in deps], [0.0] * n
-    free = {q: 0.0 for q in "vspgyx"}
-    open_ = {q: [i for i in range(n) if ops[i][0] == q and not deps[i]] for q in free}
-    order = []
-    while len(order) < n:
-        pick = None
-        for q, cand in open_.items():
-            if not cand:
-                continue
-            t = max(free[q], min(ready[i] for i in cand))
-            b = max((i for i in cand if ready[i] <= t), key=lambda i: (prio[i], -i))
-            for h in cand:
-                if t < ready[h] < t + HOLD * ops[b][5][0] and prio[h] > prio[b] + GAP:
-                    b = h
-            s = max(free[q], ready[b])
-            if pick is None or s < pick[0]:
-                pick = (s, q, b)
-        s, q, b = pick
-        open_[q].remove(b)
-        order.append(b)
-        free[q] = s + ops[b][5][0]
-        for k in after[b]:
-            ready[k] = max(ready[k], s + ops[b][5][1] + (0.0 if (q == "p" and ops[k][0] == "p") or soft.get(k) == b else WAKE))
-            left[k] -= 1
-            if not left[k]:
-                open_[ops[k][0]].append(k)
-        LENGTH[0] = s + ops[b][5][1]
-    return order
+    best = None
+    for _ in range(ROUNDS):
+        for i in UPPER:
+            prio[i] += AHEAD
+        order, end = run(prio, deps, after, False)
+        length = max(end[i] + ops[i][5][1] - busy[i] for i in range(n))
+        if best is None or length < best[0]:
+            best = (length, order)
+        prio = run(end, after, deps, True)[1]
+    LENGTH[0] = best[0]
+    return best[1]
 
 
 def emit(g, T, steps, landed, sent):
@@ -571,9 +657,11 @@ def emit(g, T, steps, landed, sent):
                 seen[x[0]] = old + [(i, x[1], x[2], x[4], x[5], w)]
         d.discard(i)
         deps.append(d)
-    order = arrange(ops, deps, chain)
+    if not ORDER:
+        ORDER.extend(arrange(ops, deps, chain))
+    order = ORDER
     place = {i: k for k, i in enumerate(order)}
-    upto, need, marked = {}, {}, set()
+    upto, known, need, marked = {q: {} for q in "vspgyx"}, {}, {}, set()
     for i in order:
         q, kind = ops[i][0], ops[i][4]
         best = {}
@@ -583,12 +671,15 @@ def emit(g, T, steps, landed, sent):
                 best[key] = j
         w = []
         if kind != "x":
-            for key, j in best.items():
-                if ops[j][4] != "r" and not (q == "p" and key == "p") and upto.get((q, key), -1) < place[j]:
-                    upto[(q, key)] = place[j]
+            for key, j in sorted(best.items(), key=lambda x: -place[x[1]]):
+                if ops[j][4] != "r" and not (q == "p" and key == "p") and upto[q].get(key, -1) < place[j]:
+                    upto[q][key] = place[j]
+                    for k, at in known[j].items():
+                        upto[q][k] = max(upto[q].get(k, -1), at)
                     w.append(j)
                     marked.add(j)
         need[i] = w
+        known[i] = dict(upto[q]) if kind != "x" else {}
     queue = {"v": g.vector, "s": g.scalar, "p": g.tensor, "g": g, "y": g.sync}
     token, count, nd = {}, {k: 0 for k in ESEM}, 0
     for i in order:

@@ -3,50 +3,58 @@ from concourse.mybir import AluOpType as Op, ActivationFunctionType as Fn
 
 M, E, G, NONE, LN, NP = 512, 2560, 384, 2944, 256, 3
 IX = 1
-WA, WS, WT, WN = IX + E, IX + E + 4 * M + 1, IX + E + 5 * M + 1, 5896
+WA, WN = IX + E, 5520
 STOP = -1000
 HN = LN // 2
-JOIN = (1, 1, 1)
+JOIN = 2
+STEP, OFF, LO, HI = 7168.0, -987.0, -5020.0, 2148.0
+BIG, LOW = 16384, -30000
 NW, NV = 10, 3
 BLOCKS = 4
 PLAN = [("W", 72, 0), ("F", 112, 1), ("F", 128, 1), ("R", 96, 1), ("F", 96, 2), ("S", 56, 1), ("S", 32, 1), ("S", 16, 2)]
 PLANT = [("W", 16, 0), ("F", 48, 1), ("F", 64, 2), ("F", 32, 2), ("S", 32, 1), ("S", 32, 1), ("S", 32, 2)]
 LISTQ = {1: "vv", 2: "ss", 3: "vs", 4: "sv"}
-DATEQ, NEXTQ = "vv", "ss"
+DATEQ, FIRSTQ, NEXTQ, LINKQ, OFFQ = "ss", "ss", "vv", "vs", "sv"
 RN = 1536
 
 S_, P_ = "sbuf", "psum"
 f32, bf, f16, i32, u16 = "float32", "bfloat16", "float16", "int32", "uint16"
+PFN = 8 * sum(x[1] for x in PLAN if x[0] in "FW")
+SD0 = 400
 BUF = {
-    "W": (f32, WN), "U": (f32, 5640), "T0": (i32, 2960), "T1": (i32, 2960), "SD": (f32, 3088), "A0": (bf, M),
-    "sbi": (i32, 152), "sb2": (f16, 152), "sbh": (f16, 2432), "thi": (i32, 32), "th2": (bf, 32), "thh": (bf, 512), "thB": (bf, 512),
+    "W": (f32, WN), "U": (f32, WN), "T0": (i32, SD0 + WN), "T1": (i32, 2960), "A0": (bf, M), "thB": (f16, 512),
     "bdi": (i32, 24), "bd0": (u16, 6), "bdW": (u16, 24),
-    "GS": (bf, 9728), "SO": (f16, 8192), "SB": (bf, 4096), "PF": (f32, 4096), "PR": (f16, 4096),
+    "GS": (bf, 9728), "SO": (f16, 8192), "SB": (bf, 4096), "PF": (f32, PFN), "PR": (f16, 4096),
     "LU": (u16, 2048), "DLU": (u16, 288), "OLU": (u16, 256),
-    "R16": (bf, RN), "R8": (bf, RN), "R0": (bf, 1536), "RM": (bf, 256), "RM0": (bf, 256),
+    "R16": (bf, RN), "R8": (bf, RN), "RM": (bf, 128), "RM0": (bf, 256),
     "stg": (bf, 12 * 96), "land": (bf, 12 * 96), "yrs": (bf, 512), "Ao": (bf, 256),
-    "Ti": (i32, 256), "Tb": (bf, 256), "k2": (f16, 256), "k2a": (f16, 256), "k2b": (f16, 256), "k2c": (f16, 256), "DM": (bf, 256), "n1": (f16, 256),
-    "X": (f16, 256), "X1": (f16, 256), "Dg": (f16, 256), "Y": (f16, 256), "SV": (f32, 256), "SW": (f32, 256), "FL": (u16, 64),
-    "H": (f32, 112), "Hd": (f32, 96), "Z": (f32, 96), "MV": (f32, 96), "G1": (f32, 96), "G2": (f32, 96), "CC": (f32, 96), "CM": (f32, 96),
-    "FT": (f32, 96), "FF": (f32, 96), "nl": (f32, 16), "lane": (f32, 16), "E0u": (u16, 32), "two": (f32, 144),
-    "SPd": (f32, 512), "m6": (f32, 144), "ex6": (u16, 16), "rp6": (u16, 6), "r6i": (i32, 6), "r6f": (f32, 6), "tg": (u16, 16), "fu": (u16, 16), "off": (u16, 16),
-    "XI": (f16, 256), "AE": (f32, 256), "EQ": (bf, 1024), "OF": (f32, 256), "XL": (f16, 256), "ab": (bf, 256), "KL": (bf, 256),
-    "d2": (bf, 256), "d3": (bf, 256), "d4": (bf, 256), "d5": (bf, 256), "mv": (bf, 256), "oW": (f16, 256), "oW2": (f32, 256), "ZD": (f32, 256),
-    "pi": (i32, 4), "col": (f32, 16), "JmP": (f32, 128), "JB": (f32, 256), "Jlo": (bf, 512), "Jhi": (bf, 512), "m16": (f32, 16), "cst": (bf, 128),
-    "I": (bf, 128), "I32": (f32, 128), "nI": (bf, 128), "I16": (bf, 128), "n16": (bf, 128), "n512": (bf, 128), "I4k": (bf, 128), "nI4k": (bf, 128),
-    "BO": (bf, 128), "BOa": (bf, 128), "BO4k": (bf, 128), "nBO4k": (bf, 128), "BOw": (bf, 128), "BOp": (bf, 128), "S15": (bf, 128),
-    "P1": (bf, 128), "P2": (bf, 128), "V0": (f32, 128), "V1": (f32, 128), "S0": (f32, 128), "S1": (f32, 128), "G8": (bf, 128), "G8n": (bf, 128),
-    "CW": (bf, 128), "one": (bf, 512), "DG": (bf, 256), "NEG": (bf, 256), "POS": (bf, 256), "TRI": (bf, 256), "CQ": (bf, 128),
-    "C14": (bf, 128), "S4k": (bf, 128), "BOp4k": (bf, 128),
+    "Ti": (i32, 256), "k2": (f16, 256), "k2a": (f16, 256), "k2b": (f16, 256), "k2c": (f16, 256), "DM": (bf, 256), "n1": (f16, 256),
+    "X": (f16, 256), "X1": (f16, 256), "Dg": (f16, 256), "Y": (f16, 256), "SW": (f32, 256), "FL": (u16, 64),
+    "H0": (f32, 9 * HN), "H1": (f32, 9 * HN), "nl": (f32, 128), "GG": (f32, 256), "CC": (f32, 256), "Z": (f32, 256), "FT": (f32, 256),
+    "sp": (f32, 32), "msp": (f32, 32), "two": (f32, 32), "SPd": (f32, 512), "m2": (f32, 32), "m8": (f32, 8), "exi": (i32, 8),
+    "ex": (u16, 8), "LC": (u16, 8), "rp": (u16, 4), "tf": (u16, 32), "off": (u16, 16),
+    "XI": (f16, 256), "AE": (f16, 256), "EQ": (bf, 1024), "OF": (f32, 256), "XL": (f16, 256), "ab": (bf, 256), "KL": (bf, 256),
+    "ok": (bf, 256), "old": (f16, 256), "sub": (f16, 256), "oW": (f32, 256), "ZD": (f32, 256),
+    "pi": (i32, 5), "col": (f32, 24), "JmP": (f32, 128), "JB": (f32, 256),
+    "cj": (f32, 64), "cp": (f32, 64), "cn": (f32, 64), "c16": (f32, 64), "n16": (f32, 64),
+    "nil": (bf, 128), "I": (bf, 128), "I32": (f32, 128), "I16f": (f32, 128), "nI": (bf, 128), "nI16": (bf, 128), "I31": (bf, 128),
+    "I8": (bf, 128), "I16th": (bf, 128), "nI4k": (bf, 128), "IS": (bf, 128), "nIS": (bf, 128),
+    "BO": (bf, 128), "BOa": (bf, 128), "BOS": (bf, 128), "nBOS": (bf, 128), "BOw": (bf, 128), "BOp": (bf, 128), "S15": (bf, 128), "S32": (bf, 128),
+    "P1": (bf, 128), "P2": (bf, 128), "V0": (f32, 128), "V1": (f32, 128), "S0": (f32, 128), "S1": (f32, 128),
+    "CW": (bf, 128), "CB": (bf, 128), "one": (bf, 512), "DG": (bf, 256), "NEG": (bf, 256), "N16": (bf, 128), "TRI": (bf, 128),
+    "cq": (bf, 128), "c2": (bf, 128),
 }
 SIZE = {f32: 4, i32: 4, bf: 2, f16: 2, u16: 2}
-GAT, FAR, NEAR, WAKE, HOLD, GAP, PE, AHEAD = 1.8, 3500.0, 2000.0, 60.0, 0.4, 300.0, 0.65, 500.0
+GAT, FAR, NEAR, FIRST, WAKE, HOLD, GAP, PE, AHEAD = 1.8, 3500.0, 2500.0, 600.0, 80.0, 0.4, 300.0, 0.65, 0.0
+VFIX, SFIX, CYC, DMA, RATE, SOON = 105.0, 190.0, 1.0, 2400.0, 420.0, 5000.0
+EARLY = []
+TURN = []
 UPPER = []
 HALF = 0.498
 ORDER, LENGTH, ROUNDS = [], [0.0], 4
 HOME, _fill = {}, {}
 for _k, (_d, _n) in BUF.items():
-    if _n <= 128 and _k not in ("bdi", "thi", "th2"):
+    if _n <= 128 and _k != "bdi":
         HOME[_k] = ("sm_" + _d, _fill.get(_d, 0))
         _fill[_d] = _fill.get(_d, 0) + -(-_n // 16) * 16
 SCRATCH = {k: (S_, [128, n], d) for k, (d, n) in BUF.items() if k not in HOME}
@@ -72,7 +80,7 @@ def IND(win, off):
 
 
 def build(rank, T, send):
-    ops, chain = [], []
+    ops, chain, loaded = [], [], [0.0]
 
     def ap(x):
         if not isinstance(x, tuple):
@@ -82,16 +90,18 @@ def build(rank, T, send):
         if x[0] == "@":
             return x[1]
         name, o = HOME.get(x[0], (x[0], 0))
+        if len(x) > 6:
+            return T[name][x[4]:x[5]:x[6], x[1]:x[2]]
         return T[name][x[4]:x[5], o + x[1]:o + x[2]:x[3]] if x[3] != 1 else T[name][x[4]:x[5], o + x[1]:o + x[2]]
 
     def span(q, out, ins, kind, two):
         if kind == "x":
             return (0.0, 0.0)
         if kind == "r":
-            return (300.0, 300.0 + two)
+            return (300.0 + two[0], 300.0 + two[0] + two[1])
         if kind == "d":
             x = out if out[0] != "@" else ins[0]
-            return (60.0 if q != "g" else 600.0, 2000.0 + (x[5] - x[4]) * (x[2] - x[1]) * SIZE[BUF[x[0]][0]] / 450.0)
+            return (60.0 if q != "g" else 600.0, DMA + len(range(*x[4:])) * (x[2] - x[1]) * SIZE[BUF[x[0]][0]] / RATE)
         vs = [x for x in [out] + ins if isinstance(x, tuple)]
         ind = [x for x in vs if x[0] == "*"]
         if ind:
@@ -105,10 +115,10 @@ def build(rank, T, send):
             elif q == "g":
                 c = 1.5 * (150.0 + 2 * n)
             elif q == "s":
-                c = 190.0 + max(64, n)
+                c = SFIX + CYC * max(64, n)
             else:
                 half = 0.5 if not ps and all(SIZE[BUF[x[0]][0]] == 2 for x in big) else 1.0
-                c = 105.0 + max(64, n * half * (2 if two and not ps else 1))
+                c = VFIX + CYC * max(64, n * half * (2 if two and not ps else 1))
         return (c, c)
 
     def add(q, call, out, ins, kind="c", two=False):
@@ -144,6 +154,11 @@ def build(rank, T, send):
             ts(o, a, c, AD)
         else:
             cp(o, a)
+    def above(q, o, a, c):
+        if q == "s":
+            act(o, a, c, 1.0, RELU)
+        else:
+            ts2(o, a, c, AD, 0.0, MX)
     def mm(o, l, r, st=True, en=True): add("p", lambda g: g.tensor.matmul(ap(o), ap(l), ap(r), st, en), o, [l, r])
     def total(o, terms):
         for j, (l, r) in enumerate(terms):
@@ -153,24 +168,27 @@ def build(rank, T, send):
             add("g", lambda g: g.iota(ap(o), pat, base, ch), o, [])
         else:
             add("g", lambda g: g.iota(ap(o), pat, base, ch, allow_small_or_imprecise_dtypes=True), o, [])
-    def pick(o, a, pat, op, base, ch): add("g", lambda g: g.affine_select(ap(o), ap(a), pat, op, 0.0, base, ch), o, [a])
+    def pick(o, a, pat, op, base, ch, c=0.0): add("g", lambda g: g.affine_select(ap(o), ap(a), pat, op, c, base, ch), o, [a])
+    def eye(name, c, pat=((-1, 128),), base=0): pick(V(name), V("nil"), [list(x) for x in pat], Op.not_equal, base, 1, c)
+    def const(o, c):
+        n = len(range(o[1], o[2], o[3]))
+        pick(o, V("nil", 0, n, p0=o[4], p1=o[5]), [[0, n]], Op.is_gt, 0, 0, c)
     def dma(q, o, a, also=()):
         add(q, lambda g: {"y": g.sync, "s": g.scalar, "g": g}[q].dma_start(ap(o), ap(a)), o, [a] + list(also), "d")
     def PS(b, lo, n, st=1): return ("ps%d" % b, lo, lo + (n - 1) * st + 1, st, 0, 128)
     def C(j): return V("col", j, j + 1)
+    def R(name, j): return V(name, 32 + j, 33 + j)
     def ext(x): return ("@", x)
     def TW(l): return "T%d" % (l % 2)
-    def acol(l): return WA + l * M if l < 4 else WT
+    def acol(l): return WA + l * M
     AD, SU, MU, MX, MN, EQ = Op.add, Op.subtract, Op.mult, Op.max, Op.min, Op.is_equal
     RELU = Fn.Relu
 
     dma("y", V("A0"), ext(T.av[:, 0:M]))
     dma("s", V("bdi"), ext(T.bd[:, :]))
     dma("y", V("T1", M, 2 * M), ext(T.dp[:, 0:M]))
-    dma("y", V("T1", 2 * M, 3 * M), ext(T.dp[:, M:2 * M]))
-    dma("y", V("T1", 3 * M, E), ext(T.dp[:, 2 * M:4 * M]))
-    dma("y", V("thi"), ext(T.th[:, :]))
-    dma("y", V("sbi"), ext(T.sb[:, :]))
+    for l in (2, 3, 4):
+        dma("y", N_("T1", l * M, M), ext(T.dp[:, (l - 1) * M:l * M]))
 
     def fill_s(name, lo, hi, c):
         for a in range(lo, hi, M):
@@ -187,22 +205,17 @@ def build(rank, T, send):
     iota(V("JmP"), [[1, 128]], 0, -1)
     fill_s("T1", E, 2960, 128.0)
     for name, st in (("R8", 8), ("R16", 16)):
-        ms(V(name, 0, M), -0.0625); ms(V(name, 0, M, st), 512.0)
+        fill_s(name, 0, M, -0.0625); ms(V(name, 0, M, st), 512.0)
         for a in range(M, RN, M):
             dma("y", N_(name, a, M), V(name, 0, M))
     ts(V("pi", 1, 2), V("pi", 0, 1), 4, Op.arith_shift_right)
     ts(V("pi", 2, 3), V("pi", 0, 1), 15, Op.bitwise_and)
     cp(V("col", 0, 3), V("pi", 0, 3))
+    iota(V("nil"), [[0, 128]], 0, 0)
     cp(V("bd0"), V("bdi", 0, 6))
-    fill_g("W", M, IX + M, 0); fill_g("W", E, E + 4, 0); fill_g("W", WS - 2, WS + 2, 0)
-    fill_g("W", WT - 2, WT + 2, 0); fill_g("W", WT + M - 2, WT + M + 2, 0)
-    fill_g("R0", 0, M, 0)
-    iota(V("R0", 0, M, 16), [[0, 32]], 512, 0)
-    for a in (M, 2 * M):
-        dma("y", N_("R0", a, M), V("R0", 0, M))
 
     def exchange(k):
-        add("g", send(k), None, [N_("stg", 96 * k, 96)], "r", FAR if k % 4 else NEAR)
+        add("g", send(k), None, [N_("stg", 96 * k, 96)], "r", (0.0 if k else FIRST, FAR if k % 4 else NEAR))
 
     def mirror(l):
         for a, n in ((l * M, M), (E + 96 * l, 96)):
@@ -225,22 +238,21 @@ def build(rank, T, send):
         act(V("T1", 0, M), V("A0") if t == 0 else N_("W", WA, M), -127.0)
 
     release0(0)
-    dma("g", N_("W", WA, 4 * M), ext(T.av[:, 0:4 * M]), [N_("stg", 0, 96)])
-    dma("g", N_("W", WT, M), ext(T.av[:, 4 * M:E]))
+    dma("g", N_("W", WA, 2 * M), ext(T.av[:, 0:2 * M]), [N_("stg", 0, 96)])
+    dma("g", N_("W", WA + 2 * M, 3 * M), ext(T.av[:, 2 * M:E]), [N_("stg", 0, 96)])
     iota(V("JB"), [[0, 16], [1, 16]], 0, 0)
-    iota(V("m16"), [[1, 16]], 0, 0)
-    iota(V("m6", 0, 96), [[32, 16], [0, 6]], WS - E, 0)
-    iota(V("m6", 96, 128), [[1, 2], [32, 16]], 4 * M + IX, 0)
-    iota(V("m6", 128, 144), [[32, 16]], WT - E, 0)
-    iota(V("Jlo", p1=32), [[0, 2], [1, 256]], 0, 0)
-    iota(V("Jhi", p1=32), [[256, 2], [0, 256]], 0, 0)
+    iota(V("msp"), [[1, 2], [-16, 16]], LN - WA, 0)
+    iota(V("cj"), [[1, 64]], -32, 0)
+    iota(V("m2"), [[1, 2], [32, 16]], WA + 4 * M, 0)
+    iota(V("m8"), [[0, 2], [32, 4]], 15, 0)
+    iota(V("exi"), [[8, 8]], 8, 0)
     ts(C(3), C(2), 8.0, Op.is_ge)
     ts(C(4), C(2), 8.0, Op.is_lt)
     ts2(V("V0"), V("JmP"), -8.0, EQ, C(3), MU)
     ts2(V("V1"), V("JmP"), 0.0, EQ, C(3), MU)
     ts2(V("S0"), V("JmP"), 0.0, EQ, C(4), MU)
     ts2(V("S1"), V("JmP"), 8.0, EQ, C(4), MU)
-    act(N_("W", IX + M, M), N_("T1", M, M))
+    act(N_("W", M, IX + M), N_("T1", M - IX, IX + M))
     ts(V("bdW"), V("bdi"), float(IX), AD)
 
     def split(plan):
@@ -275,83 +287,78 @@ def build(rank, T, send):
     def own_keys(l, par):
         n, st = (M, 1) if l < 4 else (LN, 2)
         for a in range(0, n, HN):
-            total(PS(l % 2, a, HN), [(V("CW", p1=64), V("one", 0, HN, p1=64)),
+            total(PS(l % 2, a, HN), [(V("CW", p1=2), V("one", 0, HN, p1=2)),
                                      (V("I32"), N_("W", acol(l) + (par if l == 4 else 0) + a * st, HN, st))])
 
     lists(1, 0)
-    pick(V("I"), V("one", 0, 128), [[-1, 128]], EQ, 0, 1)
-    pick(V("I32"), V("one", 0, 128), [[-1, 128]], EQ, 0, 1)
+    eye("I", 1.0)
+    eye("I32", 1.0)
     ts2(C(5), C(1), -32.0, MU, 112.0, AD)
     ts(V("P1"), V("JmP"), C(5), EQ)
     ts2(C(6), C(1), 0.0, Op.is_gt, 128.0, MU)
     ts2(C(6), C(1), -32.0, MU, C(6), AD)
     ts(V("P2"), V("JmP"), C(6), EQ)
-    ms(V("CW", p1=64), 0.0); ms(V("CW", p1=1), -128.0); ms(V("CW", p0=32, p1=33), 1.0 / 256)
+    eye("CW", -128.0, ((0, 128),))
+    pick(V("CW"), V("CW"), [[0, 128]], Op.not_equal, -1, 1, 1.0 / 256)
     own_keys(1, 0)
     for l in (2, 3, 4):
         act(N_("W", IX + l * M, M), N_("T1", l * M, M))
     fill_g("T0", 2 * M, E, 0); fill_g("T0", E + 96, 2960, 128)
+    fill_g("T0", 2960, SD0 + WA, 0); fill_g("T0", SD0 + WA + NONE, SD0 + WN, 0)
+    EARLY.extend([len(ops) - 2, len(ops) - 1])
 
     def late_setup():
-        fill_g("W", 0, M, 0); fill_g("W", WS + 2, WT - 2, 0); fill_g("W", WT + M + 2, WN, 0)
-        fill_g("U", 0, IX + M, STOP); fill_g("U", IX + 4 * M, 5640, STOP)
-        fill_g("SD", 0, IX, 0); fill_g("SD", IX + 4 * M, IX + E, 0); fill_g("SD", IX + NONE, 3088, 0)
-        fill_g("H", 0, 112, 0); fill_g("SPd", 0, 512, -30000); fill_g("RM", 0, HN, 0); fill_g("RM0", 0, LN, 1)
+        fill_g("W", 0, M, 0); fill_g("W", WA + E, WN, 0)
+        fill_g("U", 0, IX + M, STOP); fill_g("U", IX + 4 * M, WN, STOP)
+        for h in (0, 1):
+            fill_g("H%d" % h, 0, HN, LOW); fill_g("H%d" % h, HN, 5 * HN, BIG); fill_g("GG", HN * h + 64, HN * h + HN, BIG)
+            iota(N_("GG", HN * h + 64, 8, 8), [[0, 8]], LOW, 0)
+        fill_g("SPd", 0, 512, -LOW); fill_g("RM", 0, HN, 0); fill_g("RM0", 0, LN, 1)
         iota(V("RM", 0, HN, 16), [[0, 8]], -8192, 0)
         iota(V("RM0", 0, LN, 16), [[0, 16]], 0, 0)
-        pick(V("S15"), V("one", 0, 128), [[-16, 8], [0, 16]], EQ, -15, 1)
-        pick(V("G8"), V("one", 0, 128), [[-1, 8], [0, 16]], EQ, 0, 1)
-        pick(V("BOa"), V("one", 0, 128), [[-16, 8], [0, 16]], Op.is_ge, 0, 1)
-        pick(V("BO"), V("BOa"), [[16, 8], [0, 16]], Op.is_ge, 15, -1)
-        for c, eye, block in ((-1, "nI", None), (16, "I16", None), (-16, "n16", None), (-512, "n512", None),
-                              (4096, "I4k", "BO4k"), (-4096, "nI4k", "nBO4k"), (16384, None, "BOw")):
-            fill_g("cst", 0, 128, c)
-            if eye:
-                pick(V(eye), V("cst"), [[-1, 128]], EQ, 0, 1)
-            if block:
-                pick(V("BOa"), V("cst"), [[-16, 8], [0, 16]], Op.is_ge, 0, 1)
-                pick(V(block), V("BOa"), [[16, 8], [0, 16]], Op.is_ge, 15, -1)
-            if c == -1:
-                pick(V("G8n"), V("cst"), [[-1, 8], [0, 16]], EQ, 0, 1)
-            if c == 4096:
-                pick(V("S4k"), V("cst"), [[-16, 8], [0, 16]], EQ, -15, 1)
+        for name, c in (("nI", -1.0), ("nI16", -16.0), ("I16f", 16.0), ("I31", 31.0), ("I8", 8.0), ("I16th", 0.0625),
+                        ("nI4k", -4096.0), ("IS", STEP), ("nIS", -STEP)):
+            eye(name, c)
+        iota(V("CB"), [[0, 8], [int(STEP), 16]], 17 * int(STEP), 0)
+        for row, c in ((1, -1024.0), (2, OFF + 1024.0)):
+            pick(V("CB"), V("CB"), [[0, 128]], Op.not_equal, -row, 1, c)
+        for name, c in (("S15", 1.0), ("S32", -32.0)):
+            eye(name, c, ((-16, 8), (0, 16)), -15)
+        for name, c in (("BO", 1.0), ("BOS", STEP), ("nBOS", -STEP), ("BOw", -float(BIG))):
+            pick(V("BOa"), V("nil"), [[16, 8], [0, 16]], Op.is_gt, 0, -1, c)
+            pick(V(name), V("BOa"), [[16, 8], [0, 16]], Op.is_ge, 15, -1)
         ts(V("DG"), V("JB"), C(2), EQ)
-        ts2(V("TRI"), V("JB"), C(2), Op.is_le, -8192.0, MU)
-        ts2(C(7), C(2), -1.0, MU, -1.0, AD)
-        ts(C(8), C(2), -14.0, AD)
-        ts(C(9), C(2), 0.5, AD)
-        ts2(C(10), C(2), 4096.0, MU, -29696.0 - 8192.0, AD)
-        ts(C(11), C(2), 0.0625, MU)
-        ts(V("BOp"), V("BO"), C(11), MU)
-        ts(V("BOp4k"), V("BOp"), 4096.0, MU)
-        ts2(V("C14"), V("one", 0, HN), C(8), MU, 4096.0, MU)
-        ts2(V("NEG"), V("DG"), 4096.0, MU, -4096.0, AD)
-        ts2(V("POS"), V("DG"), -16384.0, MU, 16384.0, AD)
-        ts2(V("CQ"), V("DG", 0, HN), 8192.0, MU, C(10), AD)
-        cp(V("th2"), V("thi"))
-        dma("y", V("thh", p1=8), V("th2"))
-        ts(V("sb2"), V("sbi"), -1024.0, AD)
-        dma("y", V("sbh", p1=8), V("sb2"))
-        ts2(V("lane"), V("m16"), 16.0, MU, C(2), AD)
-        ts2(V("two"), V("m6"), C(2), AD, C(2), AD)
-        for par in (0, 1):
-            ts(N_("SPd", LN * par, 16, 16), V("lane"), float(WT + M - E - par), AD)
-        cp(V("E0u"), V("two", 96, 128))
-        ts2(V("ex6"), V("m16"), 6.0, MU, 4.0, AD)
-        ts2(V("r6f"), V("lane", 0, 6), 1.0 / 6, MU, -5.0 / 12, AD)
-        cp(V("r6i"), V("r6f"))
-        cp(V("rp6"), V("r6i"))
+        pick(V("TRI"), V("BOw"), [[1, 128]], Op.is_gt, 0, -1)
+        act(V("cp"), V("cj"), C(2))
+        for name, c in (("cn", -1.0), ("c16", 0.0625), ("n16", -0.0625)):
+            act(V(name), V("cp"), 0.0, c)
+        act(C(20), C(2), -8.875, 0.125)
+        ts(V("BOp"), V("BO"), R("c16", 0), MU)
+        ts(V("c2"), V("DG", 0, HN), -22.0, AD)
+        ts(V("cq"), V("DG", 0, HN), R("cp", -5), AD)
+        ts2(V("NEG"), V("DG"), 4096.0, MU, -4064.0, AD)
+        ts2(V("N16"), V("DG", 0, HN), float(BIG), MU, -float(BIG), AD)
+        ts2(V("two"), V("m2"), C(2), AD, C(2), AD)
+        ts(V("sp"), V("msp"), R("cn", 0), AD)
+        pick(N_("SPd", 0, 32, 16), V("sp"), [[0, 32]], Op.is_ge, 0, 0)
+        ts(V("pi", 3, 4), V("pi", 0, 1), 7, Op.bitwise_and)
+        ts(V("pi", 4, 5), V("pi", 0, 1), 8, Op.bitwise_and)
+        cp(V("col", 16, 18), V("pi", 3, 5))
+        ts(C(18), C(17), 2.0, MU)
+        ts2(C(19), C(16), float(HN), MU, C(18), AD)
+        ts(V("rp"), V("m8", 0, 4), C(18), AD)
+        ts(V("LC"), V("m8"), C(19), AD)
+        cp(V("ex"), V("exi"))
 
     def spread():
-        for j in (5, 0, 1, 2, 3, 4):
-            if j == 5:
-                mm(PS(5, 0, M), V("G8", p1=8), V("thh", p1=8))
-                act(V("thB"), PS(5, 0, M), -127.0)
-            else:
-                n, nm, b = (M, j * M, 6 + j % 2) if j < 4 else (G, E, 6)
-                total(PS(b, 0, n), [(V("G8", p1=8), V("sbh", j * M, j * M + n, p1=8)), (V("G8n", p1=8), V("Jlo", 0, n, p1=8)),
-                                    (V("G8n", p1=8), V("Jhi", 0, n, p1=8))])
-                act(N_("SD", IX + nm, n), PS(b, 0, n), float(1024 - nm))
+        def row(r, lo, n, st=16): return N_("T0", SD0 + WA + lo, n)[:4] + (r, 128, st)
+        after = [N_("land", 0, 96)]
+        dma("y", row(0, 0, 4 * M), ext(T.sb[:, 0:4 * M]), after)
+        dma("y", row(0, 4 * M, M), ext(T.th[:, :]), after)
+        dma("y", row(0, E, G), ext(T.sb[:, 4 * M:4 * M + G]), after)
+        for s in (8, 4, 2, 1):
+            dma("y", row(s, 0, NONE, 2 * s), row(0, 0, NONE, 2 * s), [N_("land", 96, 96)] if s == 2 else [])
+        act(V("thB"), N_("T0", SD0 + acol(4), M), 127.0 + 256.0, -1.0)
 
     def level(t, l, fill):
         plan, n = (PLAN, M) if l < 4 else (PLANT, LN)
@@ -388,7 +395,7 @@ def build(rank, T, send):
             if kind == "R" and at["R"] < 96:
                 continue
             if kind == "R":
-                scan(N_("SB", 0, 1536), N_("R0", 0, 1536), N_("GS", 8192, 1536), AD, MN)
+                scan(N_("SB", 0, 1536), N_("R16", 0, 1536), N_("GS", 8192, 1536), MX, MN)
                 x = 4 * t + l
                 tt(N_("stg", 96 * x, 96), IND(N_("W", E + l * M, IX + M), V("bdW", 6 * l, 6 * l + 6)), N_("SB", 15, 96, 16), MN)
                 exchange(x)
@@ -412,129 +419,116 @@ def build(rank, T, send):
             move("v" if NW <= j < NW + NV else "s", N_("GS", 256 * j, 256), IND(V(TW(4), 0, NONE + 1), N_("OLU", 16 * j, 16)), 127.0)
 
     def odd_tops():
-        act(N_("OLU", 16 * NW, LN - 16 * NW), N_("W", IX + 4 * M + 1 + 32 * NW, LN - 16 * NW, 2))
+        if NW < 16:
+            act(N_("OLU", 16 * NW, LN - 16 * NW), N_("W", IX + 4 * M + 1 + 32 * NW, LN - 16 * NW, 2))
         odd_gathers(range(NW, 16))
         for a, n in ((0, 96), (96, 96), (192, 48), (240, 16)):
-            scan(N_("SB", 16 * a, 16 * n), N_("R0", 0, 16 * n), N_("GS", 16 * a, 16 * n), AD, MN)
+            scan(N_("SB", 16 * a, 16 * n), N_("R16", 0, 16 * n), N_("GS", 16 * a, 16 * n), MX, MN)
             tt(N_("yrs", 1 + 2 * a, n, 2), N_("SB", 16 * a + 15, n, 16), N_("Ao", a, n), MN)
 
-    def views(h, nh):
+    def views(h, nh=1):
         def Hf(name): return N_(name, HN * h, HN * nh)
+        def Tops(name, at): return N_(name, at + LN * h, HN * nh, 2)
         def L(name, at=0): return N_(name, at + 8 * h, 8 * nh)
-        def Six(name, at=0): return N_(name, at + 48 * h, 48 * nh)
-        def Slot(name, s): return N_(name, s + 48 * h, 8 * nh, 6)
-        def Ends(name): return N_(name, HN * h + 15, 8 * nh, 16)
-        def K(name): return N_(name, 0, HN * nh)
-        def B(k, j=0): return PS(((7, 3, 5, 0), (6, 2, 4, 1))[h][k], HN * nh * j, HN * nh)
-        return Hf, L, Six, Slot, Ends, K, B
+        def B(k, j=0): return PS(((7, 3, 5), (6, 2, 4))[h][k], HN * j, HN)
+        return Hf, Tops, L, B
 
-    def caps(h, nh, par):
-        Hf, L, Six, Slot, Ends, K, B = views(h, nh)
-        act(Six("Hd"), Six("H"), -float(E + par))
-        tt(Six("G1"), IND(L("nl"), V("rp6", 0, 3 * nh)), Six("Hd"), AD)
-        tt(Six("G2"), Six("G1"), Six("two"), MN)
+    def aside(h, nh, par):
+        Hf, Tops, L, B = views(h, nh)
+        a, b = PS(1 - h if nh == 1 else 1, LN, HN * nh), PS(1 - h if nh == 1 else 1, LN + HN if nh == 1 else 0, HN * nh)
+        total(a, [(V("I"), Tops("thB", par)), (V("I16th"), Hf("k2")), (V("nI16"), Hf("DM"))])
+        act(Hf("ok"), a, R("n16", 9), -1.0, Fn.Sign)
+        total(b, [(V("I"), N_("NEG", 0, HN * nh)), (V("BO"), Hf("ok"))])
+        scan(Hf("SW"), N_("RM0", 0, HN * nh), b, MU, MX)
+        total(a, [(V("I16th"), Hf("k2")), (V("I8"), Hf("ok"))])
+        act(Tops("U", acol(4) + par), a, C(20))
+        for k in range(h, h + nh):
+            act(N_("nl", 64 * k, 64), IND(N_("SW", HN * k, HN), V("rp")), 94208.0, -5376.0)
 
     def lanes(h, par):
-        Hf, L, Six, Slot, Ends, K, B = views(h, 1)
-        move(DATEQ[1 - h], Hf("k2"), Hf("Ti"), C(7), 16.0)
+        Hf, Tops, L, B = views(h)
+        H = "H%d" % h
+        const(N_(H, HN + 15, 8, 16), (WA - par - 0.25) / 8)
+        pick(N_(H, 4 * HN + 15, 8, 16), L("two", 16 * par), [[0, 8]], Op.is_ge, 0, 0)
+        move(DATEQ[1 - h], Hf("k2"), Hf("Ti"), R("cn", 1), 16.0)
         tr(Hf("k2a"), Hf("k2"))
-        scan(Hf("k2b"), N_("RM", 0, HN), Hf("k2a"), AD, MX)
+        scan(Hf("k2b"), V("RM"), Hf("k2a"), AD, MX)
         tr(Hf("k2c"), Hf("k2b"))
+        total(B(2), [(V("I16f"), Tops("U", IX + 4 * M + par)), (V("I31"), Hf("k2")), (V("S32"), Hf("k2c"))])
+        above(FIRSTQ[1 - h], Hf("X1"), B(2), R("cn", -31))
         total(B(0), [(V("nI"), Hf("k2")), (V("S15"), Hf("k2c"))])
         act(Hf("DM"), B(0), 16.0, -16.0, RELU)
         total(B(0, 1), [(V("S15"), Hf("k2c")), (V("BOp"), Hf("DM"))])
-        act(Hf("n1"), B(0, 1), C(8))
-        act(Slot("H", 1), L("two", 96 + 16 * par))
-
-        def aside(s):
-            if s == 1:
-                act(Hf("Tb"), Hf("Ti"))
-                act(Hf("d2"), Hf("Ti"), -111.0, -1.0, RELU)
-                total(B(3, 2), [(V("I"), N_("thB", par + LN * h, HN, 2)), (V("nI"), Hf("Tb")), (V("I16"), Hf("DM"))])
-                act(Hf("d3"), B(3, 2), -256.0, 1.0, RELU)
-            if s == 2:
-                total(B(3, 3), [(V("I"), K("NEG")), (V("BO"), Hf("d3"))])
-                scan(Hf("SW"), K("RM0"), B(3, 3), MU, MX)
-                act(L("nl"), Ends("SW"), 8192.0, -8192.0, RELU)
-                total(B(0), [(V("nI"), Hf("n1")), (V("BO"), Hf("X1"))])
-                act(Hf("mv"), B(0), C(9), 1.0, RELU)
-            if s == 3:
-                total(B(3, 2), [(V("nI"), Hf("d2")), (V("n16"), Hf("d3")), (V("I16"), Hf("DM"))])
-                act(Hf("d4"), B(3, 2), -240.0, 1.0, RELU)
-                total(B(0), [(V("I"), Hf("d3")), (V("n512"), Hf("mv"))])
-                act(Hf("d5"), B(0), 0.0, 1.0, RELU)
-                if JOIN[0] == 1 or h == 0:
-                    caps(h, JOIN[0], par)
-
+        act(Hf("n1"), B(0, 1), R("cp", -14))
+        if JOIN == 1 or h == 0:
+            aside(h, JOIN, par)
         for s in range(1, 5):
-            lst = L("E0u", 16 * par) if s == 1 else L("FL", 16 * (s - 1))
-            x = Hf("X1" if s == 1 else "X")
-            act(Hf("Dg"), IND(N_("W", 0, 2960), lst), float(IX - 1024))
-            tt(x, IND(N_("U", 0, 2960), lst), Hf("DM"), MU)
-            own = [(V("I4k"), Hf("n1"))] if s > 1 else [(V("I"), V("C14")), (V("S4k"), Hf("k2c")), (V("BOp4k"), Hf("DM"))]
-            total(B(1), own + [(V("I"), Hf("Dg")), (V("nBO4k"), x)])
-            ts2(Hf("Y"), B(1), -2048.0, MX, 2048.0, MN)
-            total(B(2), [(V("I"), V("CQ")), (V("nI4k"), Hf("n1")), (V("BO4k"), x), (V("BO"), Hf("Y"))])
-            scan(Hf("SV"), N_("RM0", 0, HN), B(2), MU, MX)
-            ends = N_("SV", HN * h + 15, 8, 16)
-            if s < 4:
-                move(NEXTQ[1 - h], L("FL", 16 * s), ends)
-                act(Slot("H", 1 + s), ends)
-                aside(s)
+            if s == 1:
+                x = Hf("X1")
+                own = [(V("CB", p1=3), V("one", 0, HN, p1=3)), (V("I32"), Tops("W", IX + 4 * M + par))]
+                back = [(V("IS"), V("c2"))]
             else:
-                cp(Slot("H", 5), ends)
+                x, lst = Hf("X"), L("FL", 16 * (s - 1))
+                act(Hf("Dg"), IND(N_("W", 0, 2960), lst), OFF)
+                tt(x, IND(N_("U", 0, 2960), lst), Hf("DM"), MU)
+                own = [(V("IS"), Hf("n1")), (V("I"), Hf("Dg"))]
+                back = [(V("IS"), V("cq")), (V("nIS"), Hf("n1"))]
+            total(B(1), own + [(V("nBOS"), x)])
+            ts2(Hf("Y"), B(1), LO, MX, HI, MN)
+            total(B(2), back + [(V("BOS"), x), (V("BO"), Hf("Y"))])
+            scan(N_(H, (4 + s) * HN, HN), N_("RM0", 0, HN), B(2), MU, MX)
+            if s < 4:
+                above(NEXTQ[1 - h], L("FL", 16 * s), N_(H, (4 + s) * HN + 15, 8, 16), -float(E))
 
-    def targets(h, nh, par):
-        Hf, L, Six, Slot, Ends, K, B = views(h, nh)
-        hh = Six("H", 1)
-        act(Six("MV"), hh, 0.0, 1.0, Fn.Sign)
-        act(Six("Z"), hh, 1.0, -1.0, RELU)
-        if par:
-            ts(Six("Hd"), hh, -1.0, AD)
-        tt(Six("CC"), Six("Hd") if par else hh, Six("G2"), MN)
-        act(Slot("CC", 0), L("two", 128))
-        tt(Six("CM"), Six("CC"), Six("MV"), MU)
-        scan(Six("FT"), Six("Z"), Six("CM"), MU, AD)
-        act(L("tg"), Slot("FT", 4), float(E + par))
-        scan(Six("FF"), Six("Z"), hh, MU, AD)
-        act(L("fu"), Slot("FF", 4))
-
-    def contest(h, nh, par):
-        Hf, L, Six, Slot, Ends, K, B = views(h, nh)
-        wide, ids = HN * nh, IND(Six("FT"), V("ex6", 0, 8 * nh))
-        tt(Hf("XI"), ids, K("DG"), MU)
+    def writes(h, par):
+        Hf, Tops, L, B = views(h)
+        H, tg, fu = "H%d" % h, N_("tf", 16 * h, 8), N_("tf", 16 * h + 8, 8)
+        tt(N_("GG", HN * h, 64), IND(N_(H, 0, 8 * HN), V("LC", 0, 4)), N_("nl", 64 * h, 64), AD)
+        walk = IND(N_(H, HN, 8 * HN), V("LC"))
+        tt(Hf("CC"), walk, Hf("GG"), MN)
+        act(Hf("Z"), walk, 0.0, -8.0)
+        scan(Hf("FT"), Hf("Z"), Hf("CC"), AD, MX)
+        act(N_("tf", 16 * h, 16), N_("FT", HN * h + 7, 16, 8))
+        ids = IND(Hf("FT"), V("ex"))
+        tt(Hf("XI"), ids, V("DG", 0, HN), MU)
         act(Hf("AE"), ids)
         mm(B(1), V("BO"), Hf("XI"))
-        total(B(1, 1), [(V("I"), K("TRI")), (V("BO"), Hf("XI"))])
-        tt(Hf("XL"), IND(V("U"), L("tg")), Hf("DM"), MU)
-        act(Hf("oW"), IND(V("W"), L("tg")), -1024.0)
+        tt(Hf("XL"), IND(V("U"), tg), Hf("DM"), MU)
         total(B(0), [(V("nI"), Hf("n1")), (V("BO"), Hf("XL"))])
-        total(B(3, 2), [(V("I"), Hf("d5")), (V("nI"), Hf("d4")), (V("I"), Hf("oW"))])
         act(Hf("ab"), B(0), 0.0, 1.0, Fn.Abs)
         act(Hf("KL"), Hf("ab"), 1.0, -1.0, RELU)
-        act(Hf("oW2"), B(3, 2), 1024.0)
+        act(Hf("old"), IND(V("W"), tg), -1024.0)
+        a, b, new = PS(1 - h, LN, HN), B(0, 1), IND(N_("T0", SD0, WN), fu)
+        if LINKQ[1 - h] == "s":
+            act(Hf("sub"), new, -1024.0)
+            total(b, [(V("I"), Hf("sub")), (V("nI4k"), Hf("ab"))])
+            act(Hf("ZD"), b, 1024.0, 1.0, RELU)
+        else:
+            tt(Hf("ZD"), new, Hf("KL"), MU)
+        total(a, [(V("nI"), Hf("DM")), (V("I8"), Hf("ok")), (V("I"), Hf("old")), (V("nI4k"), Hf("KL"))])
+        act(Hf("oW"), a, 1024.0 + 8.0, 1.0, RELU)
         x2, b0 = B(2), B(1)
-        mm(x2, V("I"), K("POS"), True, False)
+        mm(x2, V("I"), V("N16"), True, False)
         mm(x2, V("BO"), Hf("XI"), False, False)
         for d in list(range(1, 16 // BLOCKS)) + [0]:
-            n = wide - 16 * d
+            n = HN - 16 * d
             eq = N_("EQ", LN * d + HN * h, n)
-            tt(eq, N_("AE", HN * h, n), (b0[0], 16 * d, wide, 1, 0, 128) if d else B(1, 1), EQ)
-            mm((x2[0], 16 * d, wide, 1, 0, 128), V("BOw"), eq, False, d == 0)
-        tt(Hf("ZD"), IND(V("SD"), L("fu")), Hf("KL"), MU)
-        scan(Hf("OF"), N_("SPd", LN * par + HN * h, wide), x2, MX, MN)
-        ts(L("off"), Ends("OF"), float(E + par), AD)
+            tt(eq, N_("AE", HN * h, n), (b0[0], 16 * d, HN, 1, 0, 128), EQ)
+            mm((x2[0], 16 * d, HN, 1, 0, 128), V("BOw" if d else "TRI"), eq, False, d == 0)
+        scan(Hf("OF"), N_("SPd", LN * par + HN * h, HN), x2, MN, MX)
+        move(OFFQ[1 - h], L("off"), N_("OF", HN * h + 15, 8, 16), WA - par - 0.2)
 
     for t in range(NP):
         par, last = t & 1, t == NP - 1
         if t == 0:
+            first = len(ops)
             late_setup()
-            spread()
+            EARLY.extend(i for i in range(first, len(ops)) if ops[i][0] in "vs")
         for l in range(2, 5):
             lists(l, par)
         if last:
             act(N_("OLU", 0, 16 * NW), N_("W", IX + 4 * M + 1, 16 * NW, 2))
-            act(V("Ao"), N_("W", WT + 1, LN, 2))
+            act(V("Ao"), N_("W", acol(4) + 1, LN, 2))
         ghosts(4 * t, 0)
         for l in range(1, 5):
             def fill(l=l):
@@ -543,28 +537,29 @@ def build(rank, T, send):
             level(t, l, fill)
             if l < 4:
                 ghosts(4 * t + l, l)
+            if t == 0 and l == 1:
+                spread()
         first = len(ops)
         lanes(1, par)
-        targets(1, 1, par)
-        contest(1, 1, par)
         UPPER.extend(range(first, len(ops)))
         lanes(0, par)
-        targets(0, 1, par)
-        contest(0, 1, par)
+        first = len(ops)
+        writes(1, par)
+        UPPER.extend(range(first, len(ops)))
+        writes(0, par)
         if last:
             act(V("yrs", 0, M, 2), V("Ti"), 127.0)
             odd_gathers(range(NW))
         nd = 16 // BLOCKS
         for b in range(BLOCKS - 1, -1, -1):
-            tt(IND(V("W"), N_("off", nd * b, nd)), N_("oW2", 16 * nd * b, 16 * nd), N_("ZD", 16 * nd * b, 16 * nd), AD)
+            tt(IND(V("W"), N_("off", nd * b, nd)), N_("oW", 16 * nd * b, 16 * nd), N_("ZD", 16 * nd * b, 16 * nd), AD)
         if not last:
             release0(t + 1)
             lists(1, 0)
             own_keys(1, 0)
         else:
             dma("y", ext(T.yd[:, :]), N_("W", IX + M, 4 * M))
-            dma("g", ext(T.ya[:, 0:4 * M]), N_("W", WA, 4 * M))
-            dma("g", ext(T.ya[:, 4 * M:E]), N_("W", WT, M))
+            dma("g", ext(T.ya[:, :]), N_("W", WA, E))
             odd_tops()
             dma("y", ext(T.yr[:, :]), V("yrs"))
     return ops, chain
@@ -573,6 +568,7 @@ def build(rank, T, send):
 def arrange(ops, deps, chain):
     n = len(ops)
     soft = {b: a for a, b in zip(chain, chain[1:]) if a not in deps[b]}
+    soft.update((b, a) for a, b in TURN)
     deps = [d | {soft[i]} if i in soft else d for i, d in enumerate(deps)]
     after = [[] for _ in range(n)]
     for i in range(n):
@@ -581,13 +577,13 @@ def arrange(ops, deps, chain):
     busy = [x[5][0] for x in ops]
 
     def lag(a, b):
-        return ops[a][5][1] - busy[a] + (0.0 if (ops[a][0] == "p" and ops[b][0] == "p") or soft.get(b) == a else WAKE)
+        return ops[a][5][1] - busy[a] + (0.0 if (ops[a][0] == "p" and ops[b][0] == "p") else WAKE) if soft.get(b) != a else 0.0
 
     def run(prio, before, behind, back):
         left, ready, end = [len(d) for d in before], [ops[i][5][1] - busy[i] if back else 0.0 for i in range(n)], [0.0] * n
         free = {q: 0.0 for q in "vspgyx"}
         open_ = {q: [i for i in range(n) if ops[i][0] == q and not before[i]] for q in free}
-        order = []
+        order, engines = [], 0.0
         while len(order) < n:
             pick = None
             for q, cand in open_.items():
@@ -605,8 +601,12 @@ def arrange(ops, deps, chain):
             open_[q].remove(b)
             order.append(b)
             free[q] = end[b] = s + busy[b]
+            late = 0.0
+            if ops[b][4] == "d" and not back:
+                late = max(0.0, engines - s - DMA)
+                engines = s + late + ops[b][5][1]
             for k in behind[b]:
-                ready[k] = max(ready[k], end[b] + (lag(k, b) if back else lag(b, k)))
+                ready[k] = max(ready[k], end[b] + (late if soft.get(k) != b else 0.0) + (lag(k, b) if back else lag(b, k)))
                 left[k] -= 1
                 if not left[k]:
                     open_[ops[k][0]].append(k)
@@ -619,6 +619,11 @@ def arrange(ops, deps, chain):
     for _ in range(ROUNDS):
         for i in UPPER:
             prio[i] += AHEAD
+        early = set(EARLY)
+        for i in range(chain[0] - 1, -1, -1):
+            if i in early or any(k in early for k in after[i]):
+                early.add(i)
+                prio[i] = max([prio[i], prio[chain[0]] - SOON] + [prio[k] + ops[i][5][1] for k in after[i] if k in early])
         order, end = run(prio, deps, after, False)
         length = max(end[i] + ops[i][5][1] - busy[i] for i in range(n))
         if best is None or length < best[0]:
@@ -641,20 +646,20 @@ def emit(g, T, steps, landed, sent):
         for views, w in ((rd, False), (wr, True)):
             for x in views:
                 psum = x[0].startswith("ps")
-                for (j, lo, hi, p0, p1, jw) in seen.get(x[0], []):
+                for (j, lo, hi, rows, jw) in seen.get(x[0], []):
                     a, b = x[1], x[2]
                     if w and jw and (kind == "d") != (ops[j][4] == "d"):
                         e = 16 // SIZE[BUF[x[0]][0]]
                         a, b = a // e * e, -(-b // e) * e
-                    meet = lo < b and a < hi and p0 < x[5] and x[4] < p1
+                    meet = lo < b and a < hi and rows & set(range(*x[4:]))
                     if (meet and (w or jw)) or (psum and (ops[j][0] != q or q == "p")):
                         d.add(j)
         for views, w in ((rd, False), (wr, True)):
             for x in views:
                 old = seen.get(x[0], [])
                 if w:
-                    old = [a for a in old if not (x[3] == 1 and x[1] <= a[1] and a[2] <= x[2] and x[4] <= a[3] and a[4] <= x[5] and a[0] in d)]
-                seen[x[0]] = old + [(i, x[1], x[2], x[4], x[5], w)]
+                    old = [a for a in old if not (x[3] == 1 and x[1] <= a[1] and a[2] <= x[2] and a[3] <= set(range(*x[4:])) and a[0] in d)]
+                seen[x[0]] = old + [(i, x[1], x[2], set(range(*x[4:])), w)]
         d.discard(i)
         deps.append(d)
     if not ORDER:
@@ -717,7 +722,7 @@ def rank_program(g, core, T, topo):
             for j, d in enumerate(group):
                 free = [e for e in topo.engines(src, dsts[d]) if e not in used]
                 n = 1
-                while 2 * n <= len(free) // (len(group) - j):
+                while 2 * n <= min([len(free) // (len(group) - j)] + [len(x) for x in out.values()]):
                     n *= 2
                 out[d] = free[:n]
                 used.update(out[d])

@@ -2,56 +2,67 @@ from concourse.bass import DstId, RemoteDMATransfer
 from concourse.mybir import AluOpType as Op, ActivationFunctionType as Fn
 
 M, E, G, NONE, LN, NP = 512, 2560, 384, 2944, 256, 3
-IX = 1
+IX = 4
 WA, WN = IX + E, 5520
 STOP = -1000
 HN = LN // 2
 JOIN = 2
-STEP, OFF, LO, HI = 7168.0, -987.0, -5020.0, 2148.0
+STEP, OFF, LO, HI = 7168.0, -984.0, -5020.0, 2148.0
 BIG, LOW = 16384, -30000
+TOP = 24560
 NW, NV = 10, 3
 BLOCKS = 4
-PLAN = [("W", 72, 0), ("F", 112, 1), ("F", 128, 1), ("R", 96, 1), ("F", 96, 2), ("S", 56, 1), ("S", 32, 1), ("S", 16, 2)]
-PLANT = [("W", 16, 0), ("F", 48, 1), ("F", 64, 2), ("F", 32, 2), ("S", 32, 1), ("S", 32, 1), ("S", 32, 2)]
-LISTQ = {1: "vv", 2: "ss", 3: "vs", 4: "sv"}
-DATEQ, FIRSTQ, NEXTQ, LINKQ, OFFQ = "ss", "ss", "vv", "vs", "sv"
+PLAN = [("W", 88, 0), ("F", 104, 1), ("F", 72, 2), ("R", 96, 1), ("F", 132, 2), ("S", 76, 1), ("S", 24, 1), ("S", 16, 2)]
+SHORT = 160
+PLANT = [("W", 24, 0), ("F", 40, 1), ("F", 64, 2), ("S", 48, 1), ("F", 32, 2), ("S", 32, 1), ("S", 16, 2)]
+RELQ = "vsv"
+LINKS0Q = "ggg"
+DATEQ, FIRSTQ, NEXTQ, LINKQ, OFFQ = "vv", "vv", "vv", "vs", "vv"
+MASKQ, BASEQ, AIMQ, PLACEQ, OLDQ = "vv", "ss", "vv", "sv", "ss"
 RN = 1536
 
 S_, P_ = "sbuf", "psum"
 f32, bf, f16, i32, u16 = "float32", "bfloat16", "float16", "int32", "uint16"
 PFN = 8 * sum(x[1] for x in PLAN if x[0] in "FW")
+PAIRS = [sum(x[1] for x in p if x[0] in "FW") // 2 for p in (PLAN, PLAN, PLANT)]
+HP = sum(PAIRS)
 SD0 = 400
 BUF = {
-    "W": (f32, WN), "U": (f32, WN), "T0": (i32, SD0 + WN), "T1": (i32, 2960), "A0": (bf, M), "thB": (f16, 512),
+    "W": (f32, WN), "U": (f32, WN), "T0": (i32, SD0 + WN), "T1": (i32, 2960), "A0": (bf, M), "thB": (bf, 512),
     "bdi": (i32, 24), "bd0": (u16, 6), "bdW": (u16, 24),
     "GS": (bf, 9728), "SO": (f16, 8192), "SB": (bf, 4096), "PF": (f32, PFN), "PR": (f16, 4096),
-    "LU": (u16, 2048), "DLU": (u16, 288), "OLU": (u16, 256),
+    "LU": (u16, 2048), "LP": (u16, 2 * HP), "LT": (u16, 2 * HP), "DLU": (u16, 288), "OLU": (u16, 256),
     "R16": (bf, RN), "R8": (bf, RN), "RM": (bf, 128), "RM0": (bf, 256),
     "stg": (bf, 12 * 96), "land": (bf, 12 * 96), "yrs": (bf, 512), "Ao": (bf, 256),
-    "Ti": (i32, 256), "k2": (f16, 256), "k2a": (f16, 256), "k2b": (f16, 256), "k2c": (f16, 256), "DM": (bf, 256), "n1": (f16, 256),
+    "k2": (f16, 256), "k2a": (f16, 256), "k2b": (f16, 256), "k2c": (f16, 256), "DM": (bf, 256), "n1": (f16, 256),
     "X": (f16, 256), "X1": (f16, 256), "Dg": (f16, 256), "Y": (f16, 256), "SW": (f32, 256), "FL": (u16, 64),
     "H0": (f32, 9 * HN), "H1": (f32, 9 * HN), "nl": (f32, 128), "GG": (f32, 256), "CC": (f32, 256), "Z": (f32, 256), "FT": (f32, 256),
     "sp": (f32, 32), "msp": (f32, 32), "two": (f32, 32), "SPd": (f32, 512), "m2": (f32, 32), "m8": (f32, 8), "exi": (i32, 8),
     "ex": (u16, 8), "LC": (u16, 8), "rp": (u16, 4), "tf": (u16, 32), "off": (u16, 16),
     "XI": (f16, 256), "AE": (f16, 256), "EQ": (bf, 1024), "OF": (f32, 256), "XL": (f16, 256), "ab": (bf, 256), "KL": (bf, 256),
     "ok": (bf, 256), "old": (f16, 256), "sub": (f16, 256), "oW": (f32, 256), "ZD": (f32, 256),
-    "pi": (i32, 5), "col": (f32, 24), "JmP": (f32, 128), "JB": (f32, 256),
-    "cj": (f32, 64), "cp": (f32, 64), "cn": (f32, 64), "c16": (f32, 64), "n16": (f32, 64),
-    "nil": (bf, 128), "I": (bf, 128), "I32": (f32, 128), "I16f": (f32, 128), "nI": (bf, 128), "nI16": (bf, 128), "I31": (bf, 128),
+    "pi": (i32, 5), "col": (f32, 28), "JB": (bf, 128),
+    "nil": (bf, 128), "I": (bf, 128), "I32": (f32, 128), "nI256": (bf, 128), "nI": (bf, 128), "nI16": (bf, 128), "I31": (bf, 128),
     "I8": (bf, 128), "I16th": (bf, 128), "nI4k": (bf, 128), "IS": (bf, 128), "nIS": (bf, 128),
-    "BO": (bf, 128), "BOa": (bf, 128), "BOS": (bf, 128), "nBOS": (bf, 128), "BOw": (bf, 128), "BOp": (bf, 128), "S15": (bf, 128), "S32": (bf, 128),
+    "BO": (bf, 128), "BOa": (bf, 128), "BO16": (bf, 128), "BOS": (bf, 128), "nBOS": (bf, 128), "BOw": (bf, 128), "BOp": (bf, 128), "S15": (bf, 128), "S32": (bf, 128),
     "P1": (bf, 128), "P2": (bf, 128), "V0": (f32, 128), "V1": (f32, 128), "S0": (f32, 128), "S1": (f32, 128),
     "CW": (bf, 128), "CB": (bf, 128), "one": (bf, 512), "DG": (bf, 256), "NEG": (bf, 256), "N16": (bf, 128), "TRI": (bf, 128),
     "cq": (bf, 128), "c2": (bf, 128),
 }
 SIZE = {f32: 4, i32: 4, bf: 2, f16: 2, u16: 2}
-GAT, FAR, NEAR, FIRST, WAKE, HOLD, GAP, PE, AHEAD = 1.8, 3500.0, 2500.0, 600.0, 80.0, 0.4, 300.0, 0.65, 0.0
-VFIX, SFIX, CYC, DMA, RATE, SOON = 105.0, 190.0, 1.0, 2400.0, 420.0, 5000.0
+COST = dict(GAT=1.6, FAR=2500.0, NEAR=2100.0, WAKE=160.0, PE=0.5, VFIX=48.0, SFIX=250.0, CYC=1.0, DMA=1900.0, GP=1.8)
+COSTS = [dict(GAT=0.83 * f * x, FAR=2300.0, NEAR=1900.0, WAKE=160.0, PE=0.42 * f, VFIX=40.0 * f, SFIX=210.0 * f, CYC=0.83 * f,
+              DMA=1600.0, GP=0.84 * f) for f, x in ((1.0, 1.56), (1.15, 1.15), (1.2, 1.85), (1.45, 2.05))]
+FIRST, HOLD, GAP, RATE, SOON = 600.0, 0.4, 300.0, 550.0, 5000.0
 EARLY = []
+OPENING = [("pi", 0), ("W", M), ("S0", 0), ("S1", 0), ("V0", 0), ("V1", 0), ("stg", 0), ("W", WA), ("P1", 0), ("P2", 16), ("P2", 0),
+           ("I", 0), ("nil", 0), ("CW", 0), ("I32", 0), ("JB", 0), ("m8", 0), ("m2", 0), ("msp", 0)]
 TURN = []
-UPPER = []
 HALF = 0.498
-ORDER, LENGTH, ROUNDS = [], [0.0], 4
+ORDER, ROUNDS = [], 4
+REACH, AFTER = 30, 50
+SWEEPS = [(100, 8000, 150.0), (70, 6000, 40.0)]
+LOOSE = set()
 HOME, _fill = {}, {}
 for _k, (_d, _n) in BUF.items():
     if _n <= 128 and _k != "bdi":
@@ -62,7 +73,7 @@ for _d, _n in _fill.items():
     SCRATCH["sm_" + _d] = (S_, [128, _n], _d)
 for _b in range(8):
     SCRATCH["ps%d" % _b] = (P_, [128, 512], f32)
-NDMA = 48
+NDMA = 56
 SEMAPHORES = ["sv", "ss", "sp", "sg", "sent"] + ["dm%d" % k for k in range(NDMA)] + ["ar%d" % k for k in range(12)]
 ESEM = {"v": "sv", "s": "ss", "p": "sp", "g": "sg"}
 
@@ -79,8 +90,38 @@ def IND(win, off):
     return ("*", win, off)
 
 
+def span(c, q, out, ins, kind, two):
+    if kind == "x":
+        return (0.0, 0.0)
+    if kind == "r":
+        hold = 300.0 + (0.0 if two else FIRST)
+        return (hold, hold + c["FAR" if two % 4 else "NEAR"])
+    if kind == "d":
+        x, n = (out if out[0] != "@" else ins[0]), max(1, two)
+        size = n * len(range(*x[4:])) * (x[2] - x[1]) * (2 if q == "g" and out[0] == "@" else SIZE[BUF[x[0]][0]])
+        return (60.0 * n if q != "g" else 600.0, c["DMA"] + 60.0 * (n - 1) + size / RATE)
+    vs = [x for x in [out] + ins if isinstance(x, tuple)]
+    ind = [x for x in vs if x[0] == "*"]
+    if ind:
+        t = 50.0 + 16 * (ind[0][2][2] - ind[0][2][1]) * (3.8 if out[0] == "*" else c["GAT"])
+    else:
+        n = len(range(out[1], out[2], out[3]))
+        big = [x for x in vs if x[2] - x[1] > 1 or n == 1]
+        ps = any(x[0].startswith("ps") for x in big)
+        if q == "p":
+            t = 30.0 + c["PE"] * max(64, n) * (4 if BUF[ins[0][0]][0] == f32 else 1)
+        elif q == "g":
+            t = c["GP" if n > 16 else "CYC"] * (170.0 + 2 * n)
+        elif q == "s":
+            t = c["SFIX"] + c["CYC"] * max(64, n)
+        else:
+            half = 0.5 if not ps and all(SIZE[BUF[x[0]][0]] == 2 for x in big) else 1.0
+            t = c["VFIX"] + c["CYC"] * max(64, n * half * (2 if two and not ps else 1))
+    return (t, t)
+
+
 def build(rank, T, send):
-    ops, chain, loaded = [], [], [0.0]
+    ops, chain, sent = [], [], []
 
     def ap(x):
         if not isinstance(x, tuple):
@@ -94,33 +135,6 @@ def build(rank, T, send):
             return T[name][x[4]:x[5]:x[6], x[1]:x[2]]
         return T[name][x[4]:x[5], o + x[1]:o + x[2]:x[3]] if x[3] != 1 else T[name][x[4]:x[5], o + x[1]:o + x[2]]
 
-    def span(q, out, ins, kind, two):
-        if kind == "x":
-            return (0.0, 0.0)
-        if kind == "r":
-            return (300.0 + two[0], 300.0 + two[0] + two[1])
-        if kind == "d":
-            x = out if out[0] != "@" else ins[0]
-            return (60.0 if q != "g" else 600.0, DMA + len(range(*x[4:])) * (x[2] - x[1]) * SIZE[BUF[x[0]][0]] / RATE)
-        vs = [x for x in [out] + ins if isinstance(x, tuple)]
-        ind = [x for x in vs if x[0] == "*"]
-        if ind:
-            c = 50.0 + 16 * (ind[0][2][2] - ind[0][2][1]) * (3.8 if out[0] == "*" else GAT)
-        else:
-            n = len(range(out[1], out[2], out[3]))
-            big = [x for x in vs if x[2] - x[1] > 1 or n == 1]
-            ps = any(x[0].startswith("ps") for x in big)
-            if q == "p":
-                c = 30.0 + PE * max(64, n) * (4 if BUF[ins[0][0]][0] == f32 else 1)
-            elif q == "g":
-                c = 1.5 * (150.0 + 2 * n)
-            elif q == "s":
-                c = SFIX + CYC * max(64, n)
-            else:
-                half = 0.5 if not ps and all(SIZE[BUF[x[0]][0]] == 2 for x in big) else 1.0
-                c = VFIX + CYC * max(64, n * half * (2 if two and not ps else 1))
-        return (c, c)
-
     def add(q, call, out, ins, kind="c", two=False):
         rd, wr = [], []
         for x in ins:
@@ -129,11 +143,11 @@ def build(rank, T, send):
             elif isinstance(x, tuple) and x[0] != "@":
                 rd.append(x)
         if out is not None and out[0] == "*":
-            rd += [out[1], out[2]]
+            rd.append(out[2])
             wr.append(out[1])
         elif out is not None and out[0] != "@":
             wr.append(out)
-        ops.append((q, call, rd, wr, kind, span(q, out, ins, kind, two)))
+        ops.append((q, call, rd, wr, kind, (q, out, ins, kind, two)))
 
     def tt(o, a, b, op): add("v", lambda g: g.vector.tensor_tensor(ap(o), ap(a), ap(b), op), o, [a, b], two=True)
     def ts(o, a, s1, op0): add("v", lambda g: g.vector.tensor_scalar(ap(o), ap(a), ap(s1), None, op0), o, [a, s1])
@@ -146,7 +160,10 @@ def build(rank, T, send):
     def act(o, a, bias=0.0, scale=1.0, fn=Fn.Identity, also=()):
         add("s", lambda g: g.scalar.activation(ap(o), ap(a), fn, bias=ap(bias), scale=ap(scale)), o, [a, bias, scale] + list(also))
     def move(q, o, a, c=0.0, scale=1.0):
-        if q == "s":
+        if q == "g":
+            pick(o, a, [[0, len(range(o[1], o[2], o[3]))]], Op.is_ge, 0, 0)
+            ops[-1][2].extend(sent[-1:])
+        elif q == "s":
             act(o, a, c, scale)
         elif scale != 1.0:
             ts2(o, a, scale, MU, c, AD)
@@ -170,14 +187,18 @@ def build(rank, T, send):
             add("g", lambda g: g.iota(ap(o), pat, base, ch, allow_small_or_imprecise_dtypes=True), o, [])
     def pick(o, a, pat, op, base, ch, c=0.0): add("g", lambda g: g.affine_select(ap(o), ap(a), pat, op, c, base, ch), o, [a])
     def eye(name, c, pat=((-1, 128),), base=0): pick(V(name), V("nil"), [list(x) for x in pat], Op.not_equal, base, 1, c)
+    def unit(o, pat, base):
+        pick(o, V("one", 0, o[2] - o[1], p1=o[5]), pat, Op.is_equal, base, 1)
     def const(o, c):
         n = len(range(o[1], o[2], o[3]))
         pick(o, V("nil", 0, n, p0=o[4], p1=o[5]), [[0, n]], Op.is_gt, 0, 0, c)
-    def dma(q, o, a, also=()):
-        add(q, lambda g: {"y": g.sync, "s": g.scalar, "g": g}[q].dma_start(ap(o), ap(a)), o, [a] + list(also), "d")
+    def dmas(q, pairs, also=()):
+        add(q, lambda g: [{"y": g.sync, "s": g.scalar, "g": g}[q].dma_start(ap(o), ap(a)) for o, a in pairs], pairs[0][0],
+            [a for o, a in pairs] + list(also), "d", len(pairs))
+        ops[-1][3].extend(o for o, a in pairs[1:])
+    def dma(q, o, a, also=()): dmas(q, [(o, a)], also)
     def PS(b, lo, n, st=1): return ("ps%d" % b, lo, lo + (n - 1) * st + 1, st, 0, 128)
     def C(j): return V("col", j, j + 1)
-    def R(name, j): return V(name, 32 + j, 33 + j)
     def ext(x): return ("@", x)
     def TW(l): return "T%d" % (l % 2)
     def acol(l): return WA + l * M
@@ -196,38 +217,35 @@ def build(rank, T, send):
             act(N_(name, a, n), N_("one", 0, n), 0.0, c)
 
     def fill_g(name, lo, hi, c):
-        for a in range(lo, hi, 256):
-            n = min(256, hi - a)
+        for a in range(lo, hi, 260):
+            n = min(260, hi - a)
             iota(N_(name, a, n), [[0, n]], c, 0)
 
     ms(V("one"), 1.0)
     iota(V("pi", 0, 1), [[0, 1]], 0, 1)
-    iota(V("JmP"), [[1, 128]], 0, -1)
+    for name, far, base in (("S0", -999, 0), ("S1", 999, -999), ("V0", -999, -8), ("V1", 999, -999 - 8)):
+        unit(V(name), [[-16, 8], [far, 2], [-1, 8]], base)
     fill_s("T1", E, 2960, 128.0)
     for name, st in (("R8", 8), ("R16", 16)):
-        fill_s(name, 0, M, -0.0625); ms(V(name, 0, M, st), 512.0)
-        for a in range(M, RN, M):
-            dma("y", N_(name, a, M), V(name, 0, M))
-    ts(V("pi", 1, 2), V("pi", 0, 1), 4, Op.arith_shift_right)
-    ts(V("pi", 2, 3), V("pi", 0, 1), 15, Op.bitwise_and)
-    cp(V("col", 0, 3), V("pi", 0, 3))
+        ms(V(name, 0, M), -0.0625); ms(V(name, 0, M, st), 512.0)
+        dmas("y", [(N_(name, a, M), V(name, 0, M)) for a in range(M, RN, M)])
     iota(V("nil"), [[0, 128]], 0, 0)
     cp(V("bd0"), V("bdi", 0, 6))
 
     def exchange(k):
-        add("g", send(k), None, [N_("stg", 96 * k, 96)], "r", (0.0 if k else FIRST, FAR if k % 4 else NEAR))
+        sent.append(N_("stg", 96 * k, 96))
+        add("g", send(k), None, [N_("stg", 96 * k, 96)], "r", k)
 
-    def mirror(l):
-        for a, n in ((l * M, M), (E + 96 * l, 96)):
-            dma("y", N_(TW(l), a, n), N_(TW(l + 1), a, n), [N_(TW(l + 1), E + 96 * l, 96)])
+    def mirror(l, first):
+        dmas("y", [(N_(TW(l), a, n), N_(TW(l + 1), a, n)) for a, n in ((l * M, M), (E + 96 * l, 2960 - E if first else 96))])
 
     def ghosts(k, l):
         add("x", k, N_("land", 96 * k, 96), [], "x")
         for d, P in ((1, "P1"), (2, "P2"), (3, "I")):
             mm(PS(4, 32 * (d - 1), 32), V(P), N_("land", 96 * k + 32 * (d - 1), 32))
-        act(N_(TW(l + 1), E + 96 * l, 96), PS(4, 0, 96), -127.0)
+        move("s" if l else "v", N_(TW(l + 1), E + 96 * l, 96), PS(4, 0, 96), -127.0)
         if l < 3:
-            mirror(l)
+            mirror(l, k == 0)
 
     def release0(t):
         if t == 0:
@@ -239,30 +257,16 @@ def build(rank, T, send):
 
     release0(0)
     dma("g", N_("W", WA, 2 * M), ext(T.av[:, 0:2 * M]), [N_("stg", 0, 96)])
-    dma("g", N_("W", WA + 2 * M, 3 * M), ext(T.av[:, 2 * M:E]), [N_("stg", 0, 96)])
-    iota(V("JB"), [[0, 16], [1, 16]], 0, 0)
-    iota(V("msp"), [[1, 2], [-16, 16]], LN - WA, 0)
-    iota(V("cj"), [[1, 64]], -32, 0)
-    iota(V("m2"), [[1, 2], [32, 16]], WA + 4 * M, 0)
-    iota(V("m8"), [[0, 2], [32, 4]], 15, 0)
-    iota(V("exi"), [[8, 8]], 8, 0)
-    ts(C(3), C(2), 8.0, Op.is_ge)
-    ts(C(4), C(2), 8.0, Op.is_lt)
-    ts2(V("V0"), V("JmP"), -8.0, EQ, C(3), MU)
-    ts2(V("V1"), V("JmP"), 0.0, EQ, C(3), MU)
-    ts2(V("S0"), V("JmP"), 0.0, EQ, C(4), MU)
-    ts2(V("S1"), V("JmP"), 8.0, EQ, C(4), MU)
-    act(N_("W", M, IX + M), N_("T1", M - IX, IX + M))
+    act(N_("W", IX + M, M), N_("T1", M, M))
+    iota(N_("W", M, IX), [[0, IX]], 0, 0)
     ts(V("bdW"), V("bdi"), float(IX), AD)
 
     def split(plan):
         return sum(x[1] for x in plan if x[0] in "FW")
 
-    def parts(l):
-        ks = [x[1] for x in (PLAN if l < 4 else PLANT) if x[0] in "FW"]
-        if l == 1:
-            return [(0, ks[0] + ks[1]), (ks[0] + ks[1], sum(ks[2:]))]
-        return [(0, sum(ks))] if l < 4 or sum(ks) <= HN else [(0, HN), (HN, sum(ks) - HN)]
+    def parts():
+        ks = [x[1] for x in PLAN if x[0] in "FW"]
+        return [(0, ks[0] + ks[1]), (ks[0] + ks[1], sum(ks[2:]))]
 
     def place(l, c):
         return c if l < 4 else (c + HN) % LN
@@ -270,95 +274,129 @@ def build(rank, T, send):
     def runs(l, c, k):
         return [(c, k)] if l < 4 or c >= HN or c + k <= HN else [(c, HN - c), (HN, c + k - HN)]
 
-    def lists(l, par):
-        plan, st = (PLAN, 1) if l < 4 else (PLANT, 2)
-        c0 = IX + l * M + (par if l == 4 else 0)
-        nf, n, lu = split(plan), (M if l < 4 else LN), (l - 1) * M
-        if l < 4:
-            move(LISTQ[l][0], N_("DLU", 96 * (l - 1), 96), IND(N_("W", l * M, IX + M), V("bdW", 6 * l, 6 * l + 6)))
-        for a, k in (runs(l, nf, n - nf) if n > nf else []):
-            move(LISTQ[l][0], N_("LU", lu + a, k), N_("W", c0 + place(l, a) * st, k, st))
-        for i, (a, k) in enumerate(parts(l) if nf else []):
-            h, bb, c = k // 2, ((2, 3), (5,), (6,), (7, 2))[l - 1][i], c0 + place(l, a) * st
+    def released(l):
+        move(RELQ[l - 1], N_("DLU", 96 * (l - 1), 96), IND(N_("W", l * M, IX + M), V("bdW", 6 * l, 6 * l + 6)))
+
+    def lists1():
+        nf, c0 = split(PLAN), IX + M
+        released(1)
+        cp(N_("LU", nf, M - nf), N_("W", c0 + nf, M - nf))
+        for (a, k), bank in zip(parts(), (2, 3)):
             for j, (a0, a1) in enumerate((("S0", "S1"), ("V0", "V1"))):
-                total(PS(bb, j * h, h), [(V(a0), N_("W", c, h, 2 * st)), (V(a1), N_("W", c + st, h, 2 * st))])
-            move(LISTQ[l][1], N_("LU", lu + a, k), PS(bb, 0, k))
+                total(PS(bank, j * k // 2, k // 2), [(V(a0), N_("W", c0 + a, k // 2, 2)), (V(a1), N_("W", c0 + a + 1, k // 2, 2))])
+            cp(N_("LU", a, k), PS(bank, 0, k))
+
+    def lists(t):
+        src, ix = ("W", IX) if t else ("T1", 0)
+        for paired in (True, False):
+            for l in (2, 3, 4):
+                nf, n, st = (split(PLAN), M, 1) if l < 4 else (split(PLANT), LN, 2)
+                c0 = ix + l * M + (t & 1 if l == 4 else 0)
+                for a, k in runs(l, 0, nf) if paired else []:
+                    for j in (0, 1):
+                        move("g" if t else "vs"[j], N_("LP", j * HP + sum(PAIRS[:l - 2]) + a // 2, k // 2), N_(src, c0 + (place(l, a) + j) * st, k // 2, 2 * st))
+                for a, k in runs(l, nf, n - nf) if not paired else []:
+                    move("g", N_("LU", (l - 1) * M + a, k), N_(src, c0 + place(l, a) * st, k, st))
+            if paired:
+                dma("y", V("LT"), V("LP"))
+                dmas("y", [(V("LP", HP * (1 - j), HP * (2 - j), 1, 16 * x + 8 * j, 16 * x + 8 * j + 8),
+                            V("LT", HP * j, HP * (j + 1), 1, 16 * x + 8 - 8 * j, 16 * x + 16 - 8 * j)) for j in (1, 0) for x in range(8)])
 
     def own_keys(l, par):
         n, st = (M, 1) if l < 4 else (LN, 2)
-        for a in range(0, n, HN):
-            total(PS(l % 2, a, HN), [(V("CW", p1=2), V("one", 0, HN, p1=2)),
-                                     (V("I32"), N_("W", acol(l) + (par if l == 4 else 0) + a * st, HN, st))])
+        for a in range(0, n, LN):
+            total(PS(l % 2, a, LN), [(V("CW", p1=2), V("one", 0, LN, p1=2)),
+                                     (V("I32"), N_("W", acol(l) + (par if l == 4 else 0) + a * st, LN, st))])
 
-    lists(1, 0)
-    eye("I", 1.0)
-    eye("I32", 1.0)
-    ts2(C(5), C(1), -32.0, MU, 112.0, AD)
-    ts(V("P1"), V("JmP"), C(5), EQ)
-    ts2(C(6), C(1), 0.0, Op.is_gt, 128.0, MU)
-    ts2(C(6), C(1), -32.0, MU, C(6), AD)
-    ts(V("P2"), V("JmP"), C(6), EQ)
+    lists1()
+    unit(V("I"), [[-1, 128]], 0)
+    unit(V("P1"), [[16, 8], [-1, 16]], -112)
+    unit(V("P2", 0, 16), [[-1, 16]], 0)
+    unit(V("P2", 16, 128), [[16, 7], [-1, 16]], -112)
+    unit(V("I32"), [[-1, 128]], 0)
     eye("CW", -128.0, ((0, 128),))
     pick(V("CW"), V("CW"), [[0, 128]], Op.not_equal, -1, 1, 1.0 / 256)
     own_keys(1, 0)
     for l in (2, 3, 4):
-        act(N_("W", IX + l * M, M), N_("T1", l * M, M))
-    fill_g("T0", 2 * M, E, 0); fill_g("T0", E + 96, 2960, 128)
+        move(LINKS0Q[l - 2], N_("W", IX + l * M, M), N_("T1", l * M, M))
     fill_g("T0", 2960, SD0 + WA, 0); fill_g("T0", SD0 + WA + NONE, SD0 + WN, 0)
-    EARLY.extend([len(ops) - 2, len(ops) - 1])
 
     def late_setup():
-        fill_g("W", 0, M, 0); fill_g("W", WA + E, WN, 0)
-        fill_g("U", 0, IX + M, STOP); fill_g("U", IX + 4 * M, WN, STOP)
+        first = len(ops)
+        for j, x in ((2, 15), (3, 7), (4, 8)):
+            ts(V("pi", j, j + 1), V("pi", 0, 1), x, Op.bitwise_and)
+        cp(V("col", 2, 5), V("pi", 2, 5))
+        move("v", C(5), C(2), -31.0 * TOP / 16, -2.0)
+        move("v", C(6), C(2), -14.0)
+        ts(C(7), C(4), 2.0, MU)
+        ts2(C(8), C(3), float(HN), MU, C(7), AD)
+        iota(V("msp"), [[1, 2], [-16, 16]], LN - WA, 0)
+        iota(V("m2"), [[1, 2], [32, 16]], WA + 4 * M, 0)
+        iota(V("m8"), [[0, 2], [32, 4]], 15, 0)
+        iota(V("exi"), [[8, 8]], 8, 0)
+        fill_g("U", 0, IX + M, STOP)
         for h in (0, 1):
-            fill_g("H%d" % h, 0, HN, LOW); fill_g("H%d" % h, HN, 5 * HN, BIG); fill_g("GG", HN * h + 64, HN * h + HN, BIG)
+            fill_g("GG", HN * h + 64, HN * h + HN, BIG)
             iota(N_("GG", HN * h + 64, 8, 8), [[0, 8]], LOW, 0)
-        fill_g("SPd", 0, 512, -LOW); fill_g("RM", 0, HN, 0); fill_g("RM0", 0, LN, 1)
-        iota(V("RM", 0, HN, 16), [[0, 8]], -8192, 0)
+            fill_g("SPd", LN * h, LN * h + LN, -LOW)
+        fill_g("RM", 0, HN, 1); fill_g("RM0", 0, LN, 1)
+        iota(V("RM", 15, HN, 16), [[0, 8]], -TOP - 16, 0)
         iota(V("RM0", 0, LN, 16), [[0, 16]], 0, 0)
-        for name, c in (("nI", -1.0), ("nI16", -16.0), ("I16f", 16.0), ("I31", 31.0), ("I8", 8.0), ("I16th", 0.0625),
+        for name, c in (("nI", -1.0), ("nI16", -16.0), ("nI256", -256.0), ("I31", 31.0 / 16), ("I8", 8.0), ("I16th", 0.0625),
                         ("nI4k", -4096.0), ("IS", STEP), ("nIS", -STEP)):
             eye(name, c)
         iota(V("CB"), [[0, 8], [int(STEP), 16]], 17 * int(STEP), 0)
         for row, c in ((1, -1024.0), (2, OFF + 1024.0)):
             pick(V("CB"), V("CB"), [[0, 128]], Op.not_equal, -row, 1, c)
-        for name, c in (("S15", 1.0), ("S32", -32.0)):
+        for name, c in (("S15", 1.0), ("S32", -2.0)):
             eye(name, c, ((-16, 8), (0, 16)), -15)
-        for name, c in (("BO", 1.0), ("BOS", STEP), ("nBOS", -STEP), ("BOw", -float(BIG))):
+        for name, c in (("BO", 1.0), ("BOS", 16 * STEP), ("nBOS", -16 * STEP), ("BO16", 16.0), ("BOw", -float(BIG))):
             pick(V("BOa"), V("nil"), [[16, 8], [0, 16]], Op.is_gt, 0, -1, c)
             pick(V(name), V("BOa"), [[16, 8], [0, 16]], Op.is_ge, 15, -1)
-        ts(V("DG"), V("JB"), C(2), EQ)
+        unit(V("JB", p1=16), [[0, 8], [-1, 16]], 0)
+        for a in (0, HN):
+            mm(PS(5, a, HN), V("JB", p1=16), V("JB", p1=16))
+        cp(V("DG", 0, HN), PS(5, 0, HN))
         pick(V("TRI"), V("BOw"), [[1, 128]], Op.is_gt, 0, -1)
-        act(V("cp"), V("cj"), C(2))
-        for name, c in (("cn", -1.0), ("c16", 0.0625), ("n16", -0.0625)):
-            act(V(name), V("cp"), 0.0, c)
-        act(C(20), C(2), -8.875, 0.125)
-        ts(V("BOp"), V("BO"), R("c16", 0), MU)
+        ts(V("BOp"), V("BO"), C(2), MU)
         ts(V("c2"), V("DG", 0, HN), -22.0, AD)
-        ts(V("cq"), V("DG", 0, HN), R("cp", -5), AD)
-        ts2(V("NEG"), V("DG"), 4096.0, MU, -4064.0, AD)
+        ts2(V("cq"), V("DG", 0, HN), C(2), AD, -5.0, AD)
+        move("v", V("NEG"), PS(5, 0, LN), -4064.0, 4096.0)
         ts2(V("N16"), V("DG", 0, HN), float(BIG), MU, -float(BIG), AD)
         ts2(V("two"), V("m2"), C(2), AD, C(2), AD)
-        ts(V("sp"), V("msp"), R("cn", 0), AD)
-        pick(N_("SPd", 0, 32, 16), V("sp"), [[0, 32]], Op.is_ge, 0, 0)
-        ts(V("pi", 3, 4), V("pi", 0, 1), 7, Op.bitwise_and)
-        ts(V("pi", 4, 5), V("pi", 0, 1), 8, Op.bitwise_and)
-        cp(V("col", 16, 18), V("pi", 3, 5))
-        ts(C(18), C(17), 2.0, MU)
-        ts2(C(19), C(16), float(HN), MU, C(18), AD)
-        ts(V("rp"), V("m8", 0, 4), C(18), AD)
-        ts(V("LC"), V("m8"), C(19), AD)
-        cp(V("ex"), V("exi"))
+        ts(V("sp"), V("msp"), C(2), AD)
+        for par in (0, 1):
+            move("g", N_("SPd", LN * par, 16, 16), N_("sp", 16 * par, 16))
+        ts(V("rp"), V("m8", 0, 4), C(7), AD)
+        ts(V("LC"), V("m8"), C(8), AD)
+        move("g", V("ex"), V("exi"))
+        EARLY.extend(i for i in range(first, len(ops)) if ops[i][0] == "v" and ops[i][3][0][0] in ("pi", "col"))
 
-    def spread():
-        def row(r, lo, n, st=16): return N_("T0", SD0 + WA + lo, n)[:4] + (r, 128, st)
-        after = [N_("land", 0, 96)]
-        dma("y", row(0, 0, 4 * M), ext(T.sb[:, 0:4 * M]), after)
-        dma("y", row(0, 4 * M, M), ext(T.th[:, :]), after)
-        dma("y", row(0, E, G), ext(T.sb[:, 4 * M:4 * M + G]), after)
-        for s in (8, 4, 2, 1):
-            dma("y", row(s, 0, NONE, 2 * s), row(0, 0, NONE, 2 * s), [N_("land", 96, 96)] if s == 2 else [])
-        act(V("thB"), N_("T0", SD0 + acol(4), M), 127.0 + 256.0, -1.0)
+    def behind(pairs):
+        TURN.append(([i for i in range(len(ops)) if ops[i][0] == "y"][-1], len(ops)))
+        dmas("y", pairs)
+
+    def spread(l):
+        def row(r, lo, n): return N_("T0", SD0 + WA + lo, n)[:4] + (r, 128, 16)
+        def rows(lo, n, src): behind([(row(r, lo, n), ext(src)) for r in range(16)])
+        if l == 0:
+            dma("y", N_("T0", 2 * M, 3 * M), N_("T1", 2 * M, 3 * M), [N_("land", 0, 96), V("LT"), V("R8"), V("R16")])
+            dma("g", N_("W", WA + 2 * M, 3 * M), ext(T.av[:, 2 * M:E]), [V("LT")])
+            behind([(N_("W", 0, M), N_("W", M, M)), (V("W", WA + E, WN), N_("W", M, WN - WA - E))]
+                   + [(N_(H, 0, 5 * HN), N_("W", M, 5 * HN)) for H in ("H0", "H1")])
+        if l == 1:
+            behind([(N_("U", a, min(M, WN - a)), N_("U", 0, min(M, WN - a))) for a in range(IX + 4 * M, WN, M)])
+            rows(4 * M, M, T.th[:, :])
+        if l == 2:
+            rows(0, 4 * M, T.sb[:, 0:4 * M])
+            rows(E, G, T.sb[:, 4 * M:4 * M + G])
+            for H in ("H0", "H1"):
+                for a, n, c in ((15, 8, LOW), (2 * HN + 15, 16, BIG)):
+                    iota(N_(H, a, n, 16), [[0, n]], c, 0)
+                    ops[-1][2].extend(sent[-1:])
+        if l == 3:
+            for par in (0, 1):
+                move("g", N_("thB", LN * par, LN), N_("T0", SD0 + acol(4) + par, LN, 2))
 
     def level(t, l, fill):
         plan, n = (PLAN, M) if l < 4 else (PLANT, LN)
@@ -366,8 +404,10 @@ def build(rank, T, send):
         at, scanned, done = {"F": 0, "S": nf, "R": 0}, {"F": 0, "S": nf}, {"F": 0, "S": nf}
 
         def cols(j):
-            a, kk = [x for x in parts(l) if x[0] <= at["F"]][-1]
-            return N_("LU", lu + a + j * (kk // 2) + (at["F"] - a) // 2, k // 2)
+            if l > 1:
+                return N_("LP", j * HP + sum(PAIRS[:l - 2]) + at["F"] // 2, k // 2)
+            a, kk = [x for x in parts() if x[0] <= at["F"]][-1]
+            return N_("LU", a + j * (kk // 2) + (at["F"] - a) // 2, k // 2)
 
         def finish(c0, k0, w):
             for c, k in runs(l, c0, k0):
@@ -375,9 +415,9 @@ def build(rank, T, send):
                 u = N_("U", IX + l * M + c, k) if l < 4 else N_("U", IX + l * M + (t & 1) + 2 * e, k, 2)
                 tt(u, N_("SO", w * c + w - 1, k, w), PS(l % 2, e, k), MN)
                 if l < 4:
-                    move("v" if j == len(plan) - 1 else "s", N_(TW(l + 1), l * M + c, k), u, HALF)
+                    move("v" if k <= SHORT else "s", N_(TW(l + 1), l * M + c, k), u, HALF)
                 else:
-                    move(DATEQ[c // HN], N_("Ti", e, k), u, HALF)
+                    move(DATEQ[c // HN], N_("k2", e, k), u, 16 * HALF + TOP, 16.0)
 
         for j, (kind, k, fin) in enumerate(plan):
             if kind in "FW":
@@ -388,7 +428,7 @@ def build(rank, T, send):
             elif kind == "R":
                 act(N_("GS", 8192 + 16 * at["R"], 16 * k), IND(win, N_("DLU", 96 * (l - 1) + at["R"], k)), 127.0)
                 at["R"] += k
-            if kind not in "VW":
+            if kind != "W":
                 chain.append(len(ops) - 1)
             if j == 0:
                 fill()
@@ -402,8 +442,6 @@ def build(rank, T, send):
                 continue
             if kind in "FW":
                 tt(N_("PR", e0, e), IND(win, cols(1)), N_("PF", e0, e), MN)
-            if kind == "V":
-                cp(N_("GS", 16 * at["S"], 16 * k), IND(win, N_("LU", lu + at["S"], k)))
             z, w, src, step = ("F", 8, "PR", "R8") if kind in "FW" else ("S", 16, "GS", "R16")
             at[z] += k
             if fin:
@@ -419,12 +457,10 @@ def build(rank, T, send):
             move("v" if NW <= j < NW + NV else "s", N_("GS", 256 * j, 256), IND(V(TW(4), 0, NONE + 1), N_("OLU", 16 * j, 16)), 127.0)
 
     def odd_tops():
-        if NW < 16:
-            act(N_("OLU", 16 * NW, LN - 16 * NW), N_("W", IX + 4 * M + 1 + 32 * NW, LN - 16 * NW, 2))
         odd_gathers(range(NW, 16))
         for a, n in ((0, 96), (96, 96), (192, 48), (240, 16)):
             scan(N_("SB", 16 * a, 16 * n), N_("R16", 0, 16 * n), N_("GS", 16 * a, 16 * n), MX, MN)
-            tt(N_("yrs", 1 + 2 * a, n, 2), N_("SB", 16 * a + 15, n, 16), N_("Ao", a, n), MN)
+        tt(N_("yrs", 1, LN, 2), N_("SB", 15, LN, 16), V("Ao"), MN)
 
     def views(h, nh=1):
         def Hf(name): return N_(name, HN * h, HN * nh)
@@ -436,12 +472,10 @@ def build(rank, T, send):
     def aside(h, nh, par):
         Hf, Tops, L, B = views(h, nh)
         a, b = PS(1 - h if nh == 1 else 1, LN, HN * nh), PS(1 - h if nh == 1 else 1, LN + HN if nh == 1 else 0, HN * nh)
-        total(a, [(V("I"), Tops("thB", par)), (V("I16th"), Hf("k2")), (V("nI16"), Hf("DM"))])
-        act(Hf("ok"), a, R("n16", 9), -1.0, Fn.Sign)
+        total(a, [(V("nI"), N_("thB", LN * par + HN * h, HN * nh)), (V("I16th"), Hf("k2")), (V("nI256"), Hf("DM"))])
+        act(Hf("ok"), a, (TOP - 8) / 16 - 383.0, -1.0, Fn.Sign)
         total(b, [(V("I"), N_("NEG", 0, HN * nh)), (V("BO"), Hf("ok"))])
         scan(Hf("SW"), N_("RM0", 0, HN * nh), b, MU, MX)
-        total(a, [(V("I16th"), Hf("k2")), (V("I8"), Hf("ok"))])
-        act(Tops("U", acol(4) + par), a, C(20))
         for k in range(h, h + nh):
             act(N_("nl", 64 * k, 64), IND(N_("SW", HN * k, HN), V("rp")), 94208.0, -5376.0)
 
@@ -450,16 +484,17 @@ def build(rank, T, send):
         H = "H%d" % h
         const(N_(H, HN + 15, 8, 16), (WA - par - 0.25) / 8)
         pick(N_(H, 4 * HN + 15, 8, 16), L("two", 16 * par), [[0, 8]], Op.is_ge, 0, 0)
-        move(DATEQ[1 - h], Hf("k2"), Hf("Ti"), R("cn", 1), 16.0)
         tr(Hf("k2a"), Hf("k2"))
-        scan(Hf("k2b"), V("RM"), Hf("k2a"), AD, MX)
+        scan(Hf("k2b"), Hf("k2a"), V("RM"), MX, AD)
         tr(Hf("k2c"), Hf("k2b"))
-        total(B(2), [(V("I16f"), Tops("U", IX + 4 * M + par)), (V("I31"), Hf("k2")), (V("S32"), Hf("k2c"))])
-        above(FIRSTQ[1 - h], Hf("X1"), B(2), R("cn", -31))
-        total(B(0), [(V("nI"), Hf("k2")), (V("S15"), Hf("k2c"))])
-        act(Hf("DM"), B(0), 16.0, -16.0, RELU)
+        total(B(2), [(V("I32"), Tops("U", IX + 4 * M + par)), (V("I31"), Hf("k2")), (V("S32"), Hf("k2c"))])
+        above(FIRSTQ[1 - h], Hf("X1"), B(2), C(5))
+        if MASKQ[1 - h] == "v":
+            ts(Hf("DM"), Hf("X1"), 0.0, Op.is_gt)
+        else:
+            act(Hf("DM"), Hf("X1"), 0.0, 1.0, Fn.Sign)
         total(B(0, 1), [(V("S15"), Hf("k2c")), (V("BOp"), Hf("DM"))])
-        act(Hf("n1"), B(0, 1), R("cp", -14))
+        move(BASEQ[1 - h], Hf("n1"), B(0, 1), C(6))
         if JOIN == 1 or h == 0:
             aside(h, JOIN, par)
         for s in range(1, 5):
@@ -484,29 +519,33 @@ def build(rank, T, send):
         Hf, Tops, L, B = views(h)
         H, tg, fu = "H%d" % h, N_("tf", 16 * h, 8), N_("tf", 16 * h + 8, 8)
         tt(N_("GG", HN * h, 64), IND(N_(H, 0, 8 * HN), V("LC", 0, 4)), N_("nl", 64 * h, 64), AD)
+        act(Tops("U", acol(4) + par), Hf("n1"), 0.0, 0.0625)
         walk = IND(N_(H, HN, 8 * HN), V("LC"))
         tt(Hf("CC"), walk, Hf("GG"), MN)
         act(Hf("Z"), walk, 0.0, -8.0)
         scan(Hf("FT"), Hf("Z"), Hf("CC"), AD, MX)
-        act(N_("tf", 16 * h, 16), N_("FT", HN * h + 7, 16, 8))
+        move(AIMQ[1 - h], N_("tf", 16 * h, 16), N_("FT", HN * h + 7, 16, 8))
         ids = IND(Hf("FT"), V("ex"))
         tt(Hf("XI"), ids, V("DG", 0, HN), MU)
         act(Hf("AE"), ids)
         mm(B(1), V("BO"), Hf("XI"))
         tt(Hf("XL"), IND(V("U"), tg), Hf("DM"), MU)
-        total(B(0), [(V("nI"), Hf("n1")), (V("BO"), Hf("XL"))])
-        act(Hf("ab"), B(0), 0.0, 1.0, Fn.Abs)
-        act(Hf("KL"), Hf("ab"), 1.0, -1.0, RELU)
+        total(B(0), [(V("nI"), Hf("n1")), (V("BO16"), Hf("ok")), (V("BO16"), Hf("XL"))])
+        if PLACEQ[1 - h] == "v":
+            ts(Hf("KL"), B(0), -14.0 * 16, EQ)
+        else:
+            act(Hf("ab"), B(0), 14.0 * 16, 1.0, Fn.Abs)
+            act(Hf("KL"), Hf("ab"), 1.0, -1.0, RELU)
         act(Hf("old"), IND(V("W"), tg), -1024.0)
         a, b, new = PS(1 - h, LN, HN), B(0, 1), IND(N_("T0", SD0, WN), fu)
         if LINKQ[1 - h] == "s":
             act(Hf("sub"), new, -1024.0)
-            total(b, [(V("I"), Hf("sub")), (V("nI4k"), Hf("ab"))])
-            act(Hf("ZD"), b, 1024.0, 1.0, RELU)
+            total(b, [(V("nI"), Hf("sub")), (V("nI4k"), Hf("KL"))])
+            act(Hf("ZD"), b, 1024.0 - 4096.0, -1.0, RELU)
         else:
             tt(Hf("ZD"), new, Hf("KL"), MU)
-        total(a, [(V("nI"), Hf("DM")), (V("I8"), Hf("ok")), (V("I"), Hf("old")), (V("nI4k"), Hf("KL"))])
-        act(Hf("oW"), a, 1024.0 + 8.0, 1.0, RELU)
+        total(a, [(V("nI16"), Hf("DM")), (V("I8"), Hf("ok")), (V("I"), Hf("old")), (V("nI4k"), Hf("KL"))])
+        above(OLDQ[1 - h], Hf("oW"), a, 1024.0 + 8.0)
         x2, b0 = B(2), B(1)
         mm(x2, V("I"), V("N16"), True, False)
         mm(x2, V("BO"), Hf("XI"), False, False)
@@ -521,15 +560,15 @@ def build(rank, T, send):
     for t in range(NP):
         par, last = t & 1, t == NP - 1
         if t == 0:
-            first = len(ops)
             late_setup()
-            EARLY.extend(i for i in range(first, len(ops)) if ops[i][0] in "vs")
-        for l in range(2, 5):
-            lists(l, par)
+        lists(t)
+        released(2); released(3)
         if last:
-            act(N_("OLU", 0, 16 * NW), N_("W", IX + 4 * M + 1, 16 * NW, 2))
-            act(V("Ao"), N_("W", acol(4) + 1, LN, 2))
+            move("g", V("OLU"), N_("W", IX + 4 * M + 1, LN, 2))
+            move("g", V("Ao"), N_("W", acol(4) + 1, LN, 2))
         ghosts(4 * t, 0)
+        if t == 0:
+            spread(0)
         for l in range(1, 5):
             def fill(l=l):
                 if l < 4:
@@ -537,25 +576,21 @@ def build(rank, T, send):
             level(t, l, fill)
             if l < 4:
                 ghosts(4 * t + l, l)
-            if t == 0 and l == 1:
-                spread()
-        first = len(ops)
+            if t == 0:
+                spread(l)
         lanes(1, par)
-        UPPER.extend(range(first, len(ops)))
         lanes(0, par)
-        first = len(ops)
         writes(1, par)
-        UPPER.extend(range(first, len(ops)))
         writes(0, par)
         if last:
-            act(V("yrs", 0, M, 2), V("Ti"), 127.0)
+            act(V("yrs", 0, M, 2), V("k2"), 127.0 - TOP / 16, 0.0625)
             odd_gathers(range(NW))
         nd = 16 // BLOCKS
         for b in range(BLOCKS - 1, -1, -1):
             tt(IND(V("W"), N_("off", nd * b, nd)), N_("oW", 16 * nd * b, 16 * nd), N_("ZD", 16 * nd * b, 16 * nd), AD)
         if not last:
             release0(t + 1)
-            lists(1, 0)
+            lists1()
             own_keys(1, 0)
         else:
             dma("y", ext(T.yd[:, :]), N_("W", IX + M, 4 * M))
@@ -566,21 +601,27 @@ def build(rank, T, send):
 
 
 def arrange(ops, deps, chain):
-    n = len(ops)
+    n, wake = len(ops), COST["WAKE"]
     soft = {b: a for a, b in zip(chain, chain[1:]) if a not in deps[b]}
+    opening = [[i for i in range(n) if ops[i][0] == "g" and (ops[i][3] or ops[i][2])[0][:2] == x][0] for x in OPENING]
+    soft.update(zip(opening[1:], opening))
     soft.update((b, a) for a, b in TURN)
+    soft.update((i, opening[-1]) for i in range(n)
+                if ops[i][0] == "g" and i not in opening and not any(ops[j][0] == "g" for j in deps[i]))
     deps = [d | {soft[i]} if i in soft else d for i, d in enumerate(deps)]
     after = [[] for _ in range(n)]
     for i in range(n):
         for j in deps[i]:
             after[j].append(i)
-    busy = [x[5][0] for x in ops]
+    busy, whole = zip(*[span(COST, *x[5]) for x in ops])
 
     def lag(a, b):
-        return ops[a][5][1] - busy[a] + (0.0 if (ops[a][0] == "p" and ops[b][0] == "p") else WAKE) if soft.get(b) != a else 0.0
+        if soft.get(b) == a or (a, b) in LOOSE:
+            return 0.0
+        return whole[a] - busy[a] + (0.0 if (ops[a][0] == "p" and ops[b][0] == "p") else wake)
 
     def run(prio, before, behind, back):
-        left, ready, end = [len(d) for d in before], [ops[i][5][1] - busy[i] if back else 0.0 for i in range(n)], [0.0] * n
+        left, ready, end = [len(d) for d in before], [whole[i] - busy[i] if back else 0.0 for i in range(n)], [0.0] * n
         free = {q: 0.0 for q in "vspgyx"}
         open_ = {q: [i for i in range(n) if ops[i][0] == q and not before[i]] for q in free}
         order, engines = [], 0.0
@@ -603,8 +644,8 @@ def arrange(ops, deps, chain):
             free[q] = end[b] = s + busy[b]
             late = 0.0
             if ops[b][4] == "d" and not back:
-                late = max(0.0, engines - s - DMA)
-                engines = s + late + ops[b][5][1]
+                late = max(0.0, engines - s - COST["DMA"])
+                engines = s + late + whole[b]
             for k in behind[b]:
                 ready[k] = max(ready[k], end[b] + (late if soft.get(k) != b else 0.0) + (lag(k, b) if back else lag(b, k)))
                 left[k] -= 1
@@ -614,23 +655,82 @@ def arrange(ops, deps, chain):
 
     prio = [0.0] * n
     for i in range(n - 1, -1, -1):
-        prio[i] = ops[i][5][1] + max([prio[k] + WAKE for k in after[i]], default=0.0)
+        prio[i] = whole[i] + max([prio[k] + wake for k in after[i]], default=0.0)
     best = None
     for _ in range(ROUNDS):
-        for i in UPPER:
-            prio[i] += AHEAD
         early = set(EARLY)
         for i in range(chain[0] - 1, -1, -1):
             if i in early or any(k in early for k in after[i]):
                 early.add(i)
-                prio[i] = max([prio[i], prio[chain[0]] - SOON] + [prio[k] + ops[i][5][1] for k in after[i] if k in early])
+                prio[i] = max([prio[i], prio[chain[0]] - SOON] + [prio[k] + whole[i] for k in after[i] if k in early])
         order, end = run(prio, deps, after, False)
-        length = max(end[i] + ops[i][5][1] - busy[i] for i in range(n))
+        length = max(end[i] + whole[i] - busy[i] for i in range(n))
         if best is None or length < best[0]:
             best = (length, order)
         prio = run(end, after, deps, True)[1]
-    LENGTH[0] = best[0]
     return best[1]
+
+
+def refine(ops, deps, order):
+    n, queue = len(ops), ["vspgyx".index(x[0]) for x in ops]
+    after = [set() for _ in range(n)]
+    for i in range(n):
+        for j in deps[i]:
+            after[j].add(i)
+    sets = []
+    for c in COSTS:
+        busy, whole = zip(*[span(c, *x[5]) for x in ops])
+        waits = [[(j, 0.0 if (j, i) in LOOSE or queue[i] == queue[j] == 2 else c["WAKE"]) for j in deps[i]] for i in range(n)]
+        sets.append((busy, whole, waits, [c["DMA"] if x[4] == "d" else 0.0 for x in ops], [0.0] * n))
+
+    def replay(steps, start):
+        out = []
+        for (busy, whole, waits, way, done), free in zip(sets, start):
+            free = list(free)
+            for i in steps:
+                s = free[queue[i]]
+                for j, w in waits[i]:
+                    if done[j] + w > s:
+                        s = done[j] + w
+                free[queue[i]] = s + busy[i]
+                if way[i]:
+                    done[i] = free[6] = max(s, free[6] - way[i]) + whole[i]
+                else:
+                    done[i] = s + whole[i]
+            out.append(free)
+        return out
+
+    fixed = {i for i in range(n) if ops[i][4] != "c" or (queue[i] > 2 and ops[i][3][0][0] not in ("FL", "tf", "H0", "H1"))}
+    seed, start = 7, [[0.0] * 7 for _ in sets]
+    for a, SPAN, TRIES, heat in [(a, s, t, h) for s, t, h in SWEEPS for a in range(0, n, s)]:
+        start = start if a else [[0.0] * 7 for _ in sets]
+        part, ahead = order[a:a + SPAN + REACH], order[a + SPAN + REACH:a + SPAN + REACH + AFTER]
+        def length(): return sum((f[0] + f[1] if ahead else 2 * f[6]) / b for f, b in zip(replay(part + ahead, start), scale))
+        scale = [c["GAT"] + c["CYC"] for c in COSTS]
+        best = length()
+        for k in range(TRIES):
+            seed = (seed * 1103515245 + 12345) % 2147483648
+            p = (seed >> 8) % len(part)
+            lo = hi = p
+            if part[p] in fixed:
+                continue
+            while lo > 0 and p - lo < REACH and part[lo - 1] not in deps[part[p]]:
+                lo -= 1
+            while hi < len(part) - 1 and hi - p < REACH and part[hi + 1] not in after[part[p]]:
+                hi += 1
+            seed = (seed * 1103515245 + 12345) % 2147483648
+            z = lo + (seed >> 8) % (hi - lo + 1)
+            other = [i for i in part[min(p, z):max(p, z) + 1] if queue[i] == queue[part[p]]]
+            part.insert(z, part.pop(p))
+            if len(other) > 1:
+                now = length()
+                if now <= best + heat * (1 - k / TRIES) ** 2 * ((seed >> 4) % 8) / 8:
+                    best = now
+                else:
+                    part.insert(p, part.pop(z))
+        order[a:a + len(part)] = part
+        start = replay(order[a:a + SPAN], start)
+    return order
 
 
 def emit(g, T, steps, landed, sent):
@@ -663,7 +763,7 @@ def emit(g, T, steps, landed, sent):
         d.discard(i)
         deps.append(d)
     if not ORDER:
-        ORDER.extend(arrange(ops, deps, chain))
+        ORDER.extend(refine(ops, deps, arrange(ops, deps, chain)))
     order = ORDER
     place = {i: k for k, i in enumerate(order)}
     upto, known, need, marked = {q: {} for q in "vspgyx"}, {}, {}, set()
@@ -672,7 +772,7 @@ def emit(g, T, steps, landed, sent):
         best = {}
         for j in deps[i]:
             key = ops[j][0] if ops[j][4] == "c" else j
-            if key not in best or place[j] > place[best[key]]:
+            if (j, i) not in LOOSE and (key not in best or place[j] > place[best[key]]):
                 best[key] = j
         w = []
         if kind != "x":
@@ -686,7 +786,7 @@ def emit(g, T, steps, landed, sent):
         need[i] = w
         known[i] = dict(upto[q]) if kind != "x" else {}
     queue = {"v": g.vector, "s": g.scalar, "p": g.tensor, "g": g, "y": g.sync}
-    token, count, nd = {}, {k: 0 for k in ESEM}, 0
+    token, count, moved = {}, {k: 0 for k in ESEM}, []
     for i in order:
         q, call, kind = ops[i][0], ops[i][1], ops[i][4]
         if kind == "x":
@@ -696,15 +796,16 @@ def emit(g, T, steps, landed, sent):
             queue[q].wait_ge(*token[j])
         ins = call(g)
         if kind == "d":
-            token[i] = (T.sem["dm%d" % nd], 16)
-            ins.then_inc(token[i][0], 16)
-            nd += 1
+            token[i] = (T.sem["dm%d" % len(moved)], 16 * len(ins))
+            for x in ins:
+                x.then_inc(token[i][0], 16)
+            moved.append(token[i])
         elif kind == "c" and i in marked:
             count[q] += 1
             token[i] = (T.sem[ESEM[q]], count[q])
             ins.then_inc(token[i][0], 1)
-    for k in range(nd):
-        g.sync.wait_ge(T.sem["dm%d" % k], 16)
+    for x in moved:
+        g.sync.wait_ge(*x)
     g.wait_ge(T.sem.sent, sent)
 
 

from concourse.bass import DstId, RemoteDMATransfer
from concourse.mybir import AluOpType as Op, ActivationFunctionType as Fn

M, E, G, NONE, LN, NP = 512, 2560, 384, 2944, 256, 3
IX = 4
WA, WN = IX + E, 5520
STOP = -1000
HN = LN // 2
JOIN = 2
STEP, OFF, LO, HI = 7168.0, -984.0, -5020.0, 2148.0
BIG, LOW = 16384, -30000
TOP = 24560
NW, NV = 10, 3
BLOCKS = 4
PLAN = [("W", 88, 0), ("F", 104, 1), ("F", 72, 2), ("R", 96, 1), ("F", 132, 2), ("S", 76, 1), ("S", 24, 1), ("S", 16, 2)]
SHORT = 160
PLANT = [("W", 24, 0), ("F", 40, 1), ("F", 64, 2), ("S", 48, 1), ("F", 32, 2), ("S", 32, 1), ("S", 16, 2)]
RELQ = "vsv"
LINKS0Q = "ggg"
DATEQ, FIRSTQ, NEXTQ, LINKQ, OFFQ = "vv", "vv", "vv", "vs", "vv"
MASKQ, BASEQ, AIMQ, PLACEQ, OLDQ = "vv", "ss", "vv", "sv", "ss"
RN = 1536

S_, P_ = "sbuf", "psum"
f32, bf, f16, i32, u16 = "float32", "bfloat16", "float16", "int32", "uint16"
PFN = 8 * sum(x[1] for x in PLAN if x[0] in "FW")
PAIRS = [sum(x[1] for x in p if x[0] in "FW") // 2 for p in (PLAN, PLAN, PLANT)]
HP = sum(PAIRS)
SD0 = 400
BUF = {
    "W": (f32, WN), "U": (f32, WN), "T0": (i32, SD0 + WN), "T1": (i32, 2960), "A0": (bf, M), "thB": (bf, 512),
    "bdi": (i32, 24), "bd0": (u16, 6), "bdW": (u16, 24),
    "GS": (bf, 9728), "SO": (f16, 8192), "SB": (bf, 4096), "PF": (f32, PFN), "PR": (f16, 4096),
    "LU": (u16, 2048), "LP": (u16, 2 * HP), "LT": (u16, 2 * HP), "DLU": (u16, 288), "OLU": (u16, 256),
    "R16": (bf, RN), "R8": (bf, RN), "RM": (bf, 128), "RM0": (bf, 256),
    "stg": (bf, 12 * 96), "land": (bf, 12 * 96), "yrs": (bf, 512), "Ao": (bf, 256),
    "k2": (f16, 256), "k2a": (f16, 256), "k2b": (f16, 256), "k2c": (f16, 256), "DM": (bf, 256), "n1": (f16, 256),
    "X": (f16, 256), "X1": (f16, 256), "Dg": (f16, 256), "Y": (f16, 256), "SW": (f32, 256), "FL": (u16, 64),
    "H0": (f32, 9 * HN), "H1": (f32, 9 * HN), "nl": (f32, 128), "GG": (f32, 256), "CC": (f32, 256), "Z": (f32, 256), "FT": (f32, 256),
    "sp": (f32, 32), "msp": (f32, 32), "two": (f32, 32), "SPd": (f32, 512), "m2": (f32, 32), "m8": (f32, 8), "exi": (i32, 8),
    "ex": (u16, 8), "LC": (u16, 8), "rp": (u16, 4), "tf": (u16, 32), "off": (u16, 16),
    "XI": (f16, 256), "AE": (f16, 256), "EQ": (bf, 1024), "OF": (f32, 256), "XL": (f16, 256), "ab": (bf, 256), "KL": (bf, 256),
    "ok": (bf, 256), "old": (f16, 256), "sub": (f16, 256), "oW": (f32, 256), "ZD": (f32, 256),
    "pi": (i32, 5), "col": (f32, 28), "JB": (bf, 128),
    "nil": (bf, 128), "I": (bf, 128), "I32": (f32, 128), "nI256": (bf, 128), "nI": (bf, 128), "nI16": (bf, 128), "I31": (bf, 128),
    "I8": (bf, 128), "I16th": (bf, 128), "nI4k": (bf, 128), "IS": (bf, 128), "nIS": (bf, 128),
    "BO": (bf, 128), "BOa": (bf, 128), "BO16": (bf, 128), "BOS": (bf, 128), "nBOS": (bf, 128), "BOw": (bf, 128), "BOp": (bf, 128), "S15": (bf, 128), "S32": (bf, 128),
    "P1": (bf, 128), "P2": (bf, 128), "V0": (f32, 128), "V1": (f32, 128), "S0": (f32, 128), "S1": (f32, 128),
    "CW": (bf, 128), "CB": (bf, 128), "one": (bf, 512), "DG": (bf, 256), "NEG": (bf, 256), "N16": (bf, 128), "TRI": (bf, 128),
    "cq": (bf, 128), "c2": (bf, 128),
}
SIZE = {f32: 4, i32: 4, bf: 2, f16: 2, u16: 2}
COST = dict(GAT=1.6, FAR=2500.0, NEAR=2100.0, WAKE=160.0, PE=0.5, VFIX=48.0, SFIX=250.0, CYC=1.0, DMA=1900.0, GP=1.8)
COSTS = [dict(GAT=0.83 * f * x, FAR=2300.0, NEAR=1900.0, WAKE=160.0, PE=0.42 * f, VFIX=40.0 * f, SFIX=210.0 * f, CYC=0.83 * f,
              DMA=1600.0, GP=0.84 * f) for f, x in ((1.0, 1.56), (1.15, 1.15), (1.2, 1.85), (1.45, 2.05))]
FIRST, HOLD, GAP, RATE, SOON = 600.0, 0.4, 300.0, 550.0, 5000.0
EARLY = []
OPENING = [("pi", 0), ("W", M), ("S0", 0), ("S1", 0), ("V0", 0), ("V1", 0), ("stg", 0), ("W", WA), ("P1", 0), ("P2", 16), ("P2", 0),
           ("I", 0), ("nil", 0), ("CW", 0), ("I32", 0), ("JB", 0), ("m8", 0), ("m2", 0), ("msp", 0)]
TURN = []
HALF = 0.498
ORDER, ROUNDS = [], 4
REACH, AFTER = 30, 50
SWEEPS = [(100, 8000, 150.0), (70, 6000, 40.0)]
LOOSE = set()
HOME, _fill = {}, {}
for _k, (_d, _n) in BUF.items():
    if _n <= 128 and _k != "bdi":
        HOME[_k] = ("sm_" + _d, _fill.get(_d, 0))
        _fill[_d] = _fill.get(_d, 0) + -(-_n // 16) * 16
SCRATCH = {k: (S_, [128, n], d) for k, (d, n) in BUF.items() if k not in HOME}
for _d, _n in _fill.items():
    SCRATCH["sm_" + _d] = (S_, [128, _n], _d)
for _b in range(8):
    SCRATCH["ps%d" % _b] = (P_, [128, 512], f32)
NDMA = 56
SEMAPHORES = ["sv", "ss", "sp", "sg", "sent"] + ["dm%d" % k for k in range(NDMA)] + ["ar%d" % k for k in range(12)]
ESEM = {"v": "sv", "s": "ss", "p": "sp", "g": "sg"}


def V(name, lo=0, hi=None, st=1, p0=0, p1=128):
    return (name, lo, BUF[name][1] if hi is None else hi, st, p0, p1)


def N_(name, lo, n, st=1):
    return (name, lo, lo + (n - 1) * st + 1, st, 0, 128)


def IND(win, off):
    return ("*", win, off)


def span(c, q, out, ins, kind, two):
    if kind == "x":
        return (0.0, 0.0)
    if kind == "r":
        hold = 300.0 + (0.0 if two else FIRST)
        return (hold, hold + c["FAR" if two % 4 else "NEAR"])
    if kind == "d":
        x, n = (out if out[0] != "@" else ins[0]), max(1, two)
        size = n * len(range(*x[4:])) * (x[2] - x[1]) * (2 if q == "g" and out[0] == "@" else SIZE[BUF[x[0]][0]])
        return (60.0 * n if q != "g" else 600.0, c["DMA"] + 60.0 * (n - 1) + size / RATE)
    vs = [x for x in [out] + ins if isinstance(x, tuple)]
    ind = [x for x in vs if x[0] == "*"]
    if ind:
        t = 50.0 + 16 * (ind[0][2][2] - ind[0][2][1]) * (3.8 if out[0] == "*" else c["GAT"])
    else:
        n = len(range(out[1], out[2], out[3]))
        big = [x for x in vs if x[2] - x[1] > 1 or n == 1]
        ps = any(x[0].startswith("ps") for x in big)
        if q == "p":
            t = 30.0 + c["PE"] * max(64, n) * (4 if BUF[ins[0][0]][0] == f32 else 1)
        elif q == "g":
            t = c["GP" if n > 16 else "CYC"] * (170.0 + 2 * n)
        elif q == "s":
            t = c["SFIX"] + c["CYC"] * max(64, n)
        else:
            half = 0.5 if not ps and all(SIZE[BUF[x[0]][0]] == 2 for x in big) else 1.0
            t = c["VFIX"] + c["CYC"] * max(64, n * half * (2 if two and not ps else 1))
    return (t, t)


def build(rank, T, send):
    ops, chain, sent = [], [], []

    def ap(x):
        if not isinstance(x, tuple):
            return x
        if x[0] == "*":
            return ap(x[1]).indirect(ap(x[2]))
        if x[0] == "@":
            return x[1]
        name, o = HOME.get(x[0], (x[0], 0))
        if len(x) > 6:
            return T[name][x[4]:x[5]:x[6], x[1]:x[2]]
        return T[name][x[4]:x[5], o + x[1]:o + x[2]:x[3]] if x[3] != 1 else T[name][x[4]:x[5], o + x[1]:o + x[2]]

    def add(q, call, out, ins, kind="c", two=False):
        rd, wr = [], []
        for x in ins:
            if isinstance(x, tuple) and x[0] == "*":
                rd += [x[1], x[2]]
            elif isinstance(x, tuple) and x[0] != "@":
                rd.append(x)
        if out is not None and out[0] == "*":
            rd.append(out[2])
            wr.append(out[1])
        elif out is not None and out[0] != "@":
            wr.append(out)
        ops.append((q, call, rd, wr, kind, (q, out, ins, kind, two)))

    def tt(o, a, b, op): add("v", lambda g: g.vector.tensor_tensor(ap(o), ap(a), ap(b), op), o, [a, b], two=True)
    def ts(o, a, s1, op0): add("v", lambda g: g.vector.tensor_scalar(ap(o), ap(a), ap(s1), None, op0), o, [a, s1])
    def ts2(o, a, s1, op0, s2, op1): add("v", lambda g: g.vector.tensor_scalar(ap(o), ap(a), ap(s1), ap(s2), op0, op1), o, [a, s1, s2])
    def cp(o, a): add("v", lambda g: g.vector.tensor_copy(ap(o), ap(a)), o, [a])
    def ms(o, c): add("v", lambda g: g.vector.memset(ap(o), c), o, [])
    def tr(o, a): add("v", lambda g: g.vector.transpose(ap(o), ap(a)), o, [a])
    def scan(o, a, b, op0, op1, also=()):
        add("v", lambda g: g.vector.tensor_tensor_scan(ap(o), ap(a), ap(b), 0.0, op0, op1), o, [a, b] + list(also))
    def act(o, a, bias=0.0, scale=1.0, fn=Fn.Identity, also=()):
        add("s", lambda g: g.scalar.activation(ap(o), ap(a), fn, bias=ap(bias), scale=ap(scale)), o, [a, bias, scale] + list(also))
    def move(q, o, a, c=0.0, scale=1.0):
        if q == "g":
            pick(o, a, [[0, len(range(o[1], o[2], o[3]))]], Op.is_ge, 0, 0)
            ops[-1][2].extend(sent[-1:])
        elif q == "s":
            act(o, a, c, scale)
        elif scale != 1.0:
            ts2(o, a, scale, MU, c, AD)
        elif c != 0.0:
            ts(o, a, c, AD)
        else:
            cp(o, a)
    def above(q, o, a, c):
        if q == "s":
            act(o, a, c, 1.0, RELU)
        else:
            ts2(o, a, c, AD, 0.0, MX)
    def mm(o, l, r, st=True, en=True): add("p", lambda g: g.tensor.matmul(ap(o), ap(l), ap(r), st, en), o, [l, r])
    def total(o, terms):
        for j, (l, r) in enumerate(terms):
            mm(o, l, r, j == 0, j == len(terms) - 1)
    def iota(o, pat, base, ch):
        if BUF[o[0]][0] == i32:
            add("g", lambda g: g.iota(ap(o), pat, base, ch), o, [])
        else:
            add("g", lambda g: g.iota(ap(o), pat, base, ch, allow_small_or_imprecise_dtypes=True), o, [])
    def pick(o, a, pat, op, base, ch, c=0.0): add("g", lambda g: g.affine_select(ap(o), ap(a), pat, op, c, base, ch), o, [a])
    def eye(name, c, pat=((-1, 128),), base=0): pick(V(name), V("nil"), [list(x) for x in pat], Op.not_equal, base, 1, c)
    def unit(o, pat, base):
        pick(o, V("one", 0, o[2] - o[1], p1=o[5]), pat, Op.is_equal, base, 1)
    def const(o, c):
        n = len(range(o[1], o[2], o[3]))
        pick(o, V("nil", 0, n, p0=o[4], p1=o[5]), [[0, n]], Op.is_gt, 0, 0, c)
    def dmas(q, pairs, also=()):
        add(q, lambda g: [{"y": g.sync, "s": g.scalar, "g": g}[q].dma_start(ap(o), ap(a)) for o, a in pairs], pairs[0][0],
            [a for o, a in pairs] + list(also), "d", len(pairs))
        ops[-1][3].extend(o for o, a in pairs[1:])
    def dma(q, o, a, also=()): dmas(q, [(o, a)], also)
    def PS(b, lo, n, st=1): return ("ps%d" % b, lo, lo + (n - 1) * st + 1, st, 0, 128)
    def C(j): return V("col", j, j + 1)
    def ext(x): return ("@", x)
    def TW(l): return "T%d" % (l % 2)
    def acol(l): return WA + l * M
    AD, SU, MU, MX, MN, EQ = Op.add, Op.subtract, Op.mult, Op.max, Op.min, Op.is_equal
    RELU = Fn.Relu

    dma("y", V("A0"), ext(T.av[:, 0:M]))
    dma("s", V("bdi"), ext(T.bd[:, :]))
    dma("y", V("T1", M, 2 * M), ext(T.dp[:, 0:M]))
    for l in (2, 3, 4):
        dma("y", N_("T1", l * M, M), ext(T.dp[:, (l - 1) * M:l * M]))

    def fill_s(name, lo, hi, c):
        for a in range(lo, hi, M):
            n = min(M, hi - a)
            act(N_(name, a, n), N_("one", 0, n), 0.0, c)

    def fill_g(name, lo, hi, c):
        for a in range(lo, hi, 260):
            n = min(260, hi - a)
            iota(N_(name, a, n), [[0, n]], c, 0)

    ms(V("one"), 1.0)
    iota(V("pi", 0, 1), [[0, 1]], 0, 1)
    for name, far, base in (("S0", -999, 0), ("S1", 999, -999), ("V0", -999, -8), ("V1", 999, -999 - 8)):
        unit(V(name), [[-16, 8], [far, 2], [-1, 8]], base)
    fill_s("T1", E, 2960, 128.0)
    for name, st in (("R8", 8), ("R16", 16)):
        ms(V(name, 0, M), -0.0625); ms(V(name, 0, M, st), 512.0)
        dmas("y", [(N_(name, a, M), V(name, 0, M)) for a in range(M, RN, M)])
    iota(V("nil"), [[0, 128]], 0, 0)
    cp(V("bd0"), V("bdi", 0, 6))

    def exchange(k):
        sent.append(N_("stg", 96 * k, 96))
        add("g", send(k), None, [N_("stg", 96 * k, 96)], "r", k)

    def mirror(l, first):
        dmas("y", [(N_(TW(l), a, n), N_(TW(l + 1), a, n)) for a, n in ((l * M, M), (E + 96 * l, 2960 - E if first else 96))])

    def ghosts(k, l):
        add("x", k, N_("land", 96 * k, 96), [], "x")
        for d, P in ((1, "P1"), (2, "P2"), (3, "I")):
            mm(PS(4, 32 * (d - 1), 32), V(P), N_("land", 96 * k + 32 * (d - 1), 32))
        move("s" if l else "v", N_(TW(l + 1), E + 96 * l, 96), PS(4, 0, 96), -127.0)
        if l < 3:
            mirror(l, k == 0)

    def release0(t):
        if t == 0:
            cp(N_("stg", 0, 96), IND(V("A0"), V("bd0")))
        else:
            cp(N_("stg", 96 * 4 * t, 96), IND(V("W", E, WA + M), V("bdW", 0, 6)))
        exchange(4 * t)
        act(V("T1", 0, M), V("A0") if t == 0 else N_("W", WA, M), -127.0)

    release0(0)
    dma("g", N_("W", WA, 2 * M), ext(T.av[:, 0:2 * M]), [N_("stg", 0, 96)])
    act(N_("W", IX + M, M), N_("T1", M, M))
    iota(N_("W", M, IX), [[0, IX]], 0, 0)
    ts(V("bdW"), V("bdi"), float(IX), AD)

    def split(plan):
        return sum(x[1] for x in plan if x[0] in "FW")

    def parts():
        ks = [x[1] for x in PLAN if x[0] in "FW"]
        return [(0, ks[0] + ks[1]), (ks[0] + ks[1], sum(ks[2:]))]

    def place(l, c):
        return c if l < 4 else (c + HN) % LN

    def runs(l, c, k):
        return [(c, k)] if l < 4 or c >= HN or c + k <= HN else [(c, HN - c), (HN, c + k - HN)]

    def released(l):
        move(RELQ[l - 1], N_("DLU", 96 * (l - 1), 96), IND(N_("W", l * M, IX + M), V("bdW", 6 * l, 6 * l + 6)))

    def lists1():
        nf, c0 = split(PLAN), IX + M
        released(1)
        cp(N_("LU", nf, M - nf), N_("W", c0 + nf, M - nf))
        for (a, k), bank in zip(parts(), (2, 3)):
            for j, (a0, a1) in enumerate((("S0", "S1"), ("V0", "V1"))):
                total(PS(bank, j * k // 2, k // 2), [(V(a0), N_("W", c0 + a, k // 2, 2)), (V(a1), N_("W", c0 + a + 1, k // 2, 2))])
            cp(N_("LU", a, k), PS(bank, 0, k))

    def lists(t):
        src, ix = ("W", IX) if t else ("T1", 0)
        for paired in (True, False):
            for l in (2, 3, 4):
                nf, n, st = (split(PLAN), M, 1) if l < 4 else (split(PLANT), LN, 2)
                c0 = ix + l * M + (t & 1 if l == 4 else 0)
                for a, k in runs(l, 0, nf) if paired else []:
                    for j in (0, 1):
                        move("g" if t else "vs"[j], N_("LP", j * HP + sum(PAIRS[:l - 2]) + a // 2, k // 2), N_(src, c0 + (place(l, a) + j) * st, k // 2, 2 * st))
                for a, k in runs(l, nf, n - nf) if not paired else []:
                    move("g", N_("LU", (l - 1) * M + a, k), N_(src, c0 + place(l, a) * st, k, st))
            if paired:
                dma("y", V("LT"), V("LP"))
                dmas("y", [(V("LP", HP * (1 - j), HP * (2 - j), 1, 16 * x + 8 * j, 16 * x + 8 * j + 8),
                            V("LT", HP * j, HP * (j + 1), 1, 16 * x + 8 - 8 * j, 16 * x + 16 - 8 * j)) for j in (1, 0) for x in range(8)])

    def own_keys(l, par):
        n, st = (M, 1) if l < 4 else (LN, 2)
        for a in range(0, n, LN):
            total(PS(l % 2, a, LN), [(V("CW", p1=2), V("one", 0, LN, p1=2)),
                                     (V("I32"), N_("W", acol(l) + (par if l == 4 else 0) + a * st, LN, st))])

    lists1()
    unit(V("I"), [[-1, 128]], 0)
    unit(V("P1"), [[16, 8], [-1, 16]], -112)
    unit(V("P2", 0, 16), [[-1, 16]], 0)
    unit(V("P2", 16, 128), [[16, 7], [-1, 16]], -112)
    unit(V("I32"), [[-1, 128]], 0)
    eye("CW", -128.0, ((0, 128),))
    pick(V("CW"), V("CW"), [[0, 128]], Op.not_equal, -1, 1, 1.0 / 256)
    own_keys(1, 0)
    for l in (2, 3, 4):
        move(LINKS0Q[l - 2], N_("W", IX + l * M, M), N_("T1", l * M, M))
    fill_g("T0", 2960, SD0 + WA, 0); fill_g("T0", SD0 + WA + NONE, SD0 + WN, 0)

    def late_setup():
        first = len(ops)
        for j, x in ((2, 15), (3, 7), (4, 8)):
            ts(V("pi", j, j + 1), V("pi", 0, 1), x, Op.bitwise_and)
        cp(V("col", 2, 5), V("pi", 2, 5))
        move("v", C(5), C(2), -31.0 * TOP / 16, -2.0)
        move("v", C(6), C(2), -14.0)
        ts(C(7), C(4), 2.0, MU)
        ts2(C(8), C(3), float(HN), MU, C(7), AD)
        iota(V("msp"), [[1, 2], [-16, 16]], LN - WA, 0)
        iota(V("m2"), [[1, 2], [32, 16]], WA + 4 * M, 0)
        iota(V("m8"), [[0, 2], [32, 4]], 15, 0)
        iota(V("exi"), [[8, 8]], 8, 0)
        fill_g("U", 0, IX + M, STOP)
        for h in (0, 1):
            fill_g("GG", HN * h + 64, HN * h + HN, BIG)
            iota(N_("GG", HN * h + 64, 8, 8), [[0, 8]], LOW, 0)
            fill_g("SPd", LN * h, LN * h + LN, -LOW)
        fill_g("RM", 0, HN, 1); fill_g("RM0", 0, LN, 1)
        iota(V("RM", 15, HN, 16), [[0, 8]], -TOP - 16, 0)
        iota(V("RM0", 0, LN, 16), [[0, 16]], 0, 0)
        for name, c in (("nI", -1.0), ("nI16", -16.0), ("nI256", -256.0), ("I31", 31.0 / 16), ("I8", 8.0), ("I16th", 0.0625),
                        ("nI4k", -4096.0), ("IS", STEP), ("nIS", -STEP)):
            eye(name, c)
        iota(V("CB"), [[0, 8], [int(STEP), 16]], 17 * int(STEP), 0)
        for row, c in ((1, -1024.0), (2, OFF + 1024.0)):
            pick(V("CB"), V("CB"), [[0, 128]], Op.not_equal, -row, 1, c)
        for name, c in (("S15", 1.0), ("S32", -2.0)):
            eye(name, c, ((-16, 8), (0, 16)), -15)
        for name, c in (("BO", 1.0), ("BOS", 16 * STEP), ("nBOS", -16 * STEP), ("BO16", 16.0), ("BOw", -float(BIG))):
            pick(V("BOa"), V("nil"), [[16, 8], [0, 16]], Op.is_gt, 0, -1, c)
            pick(V(name), V("BOa"), [[16, 8], [0, 16]], Op.is_ge, 15, -1)
        unit(V("JB", p1=16), [[0, 8], [-1, 16]], 0)
        for a in (0, HN):
            mm(PS(5, a, HN), V("JB", p1=16), V("JB", p1=16))
        cp(V("DG", 0, HN), PS(5, 0, HN))
        pick(V("TRI"), V("BOw"), [[1, 128]], Op.is_gt, 0, -1)
        ts(V("BOp"), V("BO"), C(2), MU)
        ts(V("c2"), V("DG", 0, HN), -22.0, AD)
        ts2(V("cq"), V("DG", 0, HN), C(2), AD, -5.0, AD)
        move("v", V("NEG"), PS(5, 0, LN), -4064.0, 4096.0)
        ts2(V("N16"), V("DG", 0, HN), float(BIG), MU, -float(BIG), AD)
        ts2(V("two"), V("m2"), C(2), AD, C(2), AD)
        ts(V("sp"), V("msp"), C(2), AD)
        for par in (0, 1):
            move("g", N_("SPd", LN * par, 16, 16), N_("sp", 16 * par, 16))
        ts(V("rp"), V("m8", 0, 4), C(7), AD)
        ts(V("LC"), V("m8"), C(8), AD)
        move("g", V("ex"), V("exi"))
        EARLY.extend(i for i in range(first, len(ops)) if ops[i][0] == "v" and ops[i][3][0][0] in ("pi", "col"))

    def behind(pairs):
        TURN.append(([i for i in range(len(ops)) if ops[i][0] == "y"][-1], len(ops)))
        dmas("y", pairs)

    def spread(l):
        def row(r, lo, n): return N_("T0", SD0 + WA + lo, n)[:4] + (r, 128, 16)
        def rows(lo, n, src): behind([(row(r, lo, n), ext(src)) for r in range(16)])
        if l == 0:
            dma("y", N_("T0", 2 * M, 3 * M), N_("T1", 2 * M, 3 * M), [N_("land", 0, 96), V("LT"), V("R8"), V("R16")])
            dma("g", N_("W", WA + 2 * M, 3 * M), ext(T.av[:, 2 * M:E]), [V("LT")])
            behind([(N_("W", 0, M), N_("W", M, M)), (V("W", WA + E, WN), N_("W", M, WN - WA - E))]
                   + [(N_(H, 0, 5 * HN), N_("W", M, 5 * HN)) for H in ("H0", "H1")])
        if l == 1:
            behind([(N_("U", a, min(M, WN - a)), N_("U", 0, min(M, WN - a))) for a in range(IX + 4 * M, WN, M)])
            rows(4 * M, M, T.th[:, :])
        if l == 2:
            rows(0, 4 * M, T.sb[:, 0:4 * M])
            rows(E, G, T.sb[:, 4 * M:4 * M + G])
            for H in ("H0", "H1"):
                for a, n, c in ((15, 8, LOW), (2 * HN + 15, 16, BIG)):
                    iota(N_(H, a, n, 16), [[0, n]], c, 0)
                    ops[-1][2].extend(sent[-1:])
        if l == 3:
            for par in (0, 1):
                move("g", N_("thB", LN * par, LN), N_("T0", SD0 + acol(4) + par, LN, 2))

    def level(t, l, fill):
        plan, n = (PLAN, M) if l < 4 else (PLANT, LN)
        nf, lu, win = split(plan), (l - 1) * M, V(TW(l), 0, NONE + 1)
        at, scanned, done = {"F": 0, "S": nf, "R": 0}, {"F": 0, "S": nf}, {"F": 0, "S": nf}

        def cols(j):
            if l > 1:
                return N_("LP", j * HP + sum(PAIRS[:l - 2]) + at["F"] // 2, k // 2)
            a, kk = [x for x in parts() if x[0] <= at["F"]][-1]
            return N_("LU", a + j * (kk // 2) + (at["F"] - a) // 2, k // 2)

        def finish(c0, k0, w):
            for c, k in runs(l, c0, k0):
                e = place(l, c)
                u = N_("U", IX + l * M + c, k) if l < 4 else N_("U", IX + l * M + (t & 1) + 2 * e, k, 2)
                tt(u, N_("SO", w * c + w - 1, k, w), PS(l % 2, e, k), MN)
                if l < 4:
                    move("v" if k <= SHORT else "s", N_(TW(l + 1), l * M + c, k), u, HALF)
                else:
                    move(DATEQ[c // HN], N_("k2", e, k), u, 16 * HALF + TOP, 16.0)

        for j, (kind, k, fin) in enumerate(plan):
            if kind in "FW":
                e0, e = 8 * at["F"], 8 * k
                move("s" if kind == "F" else "v", N_("PF", e0, e), IND(win, cols(0)), -0.5)
            elif kind == "S":
                act(N_("GS", 16 * at["S"], 16 * k), IND(win, N_("LU", lu + at["S"], k)))
            elif kind == "R":
                act(N_("GS", 8192 + 16 * at["R"], 16 * k), IND(win, N_("DLU", 96 * (l - 1) + at["R"], k)), 127.0)
                at["R"] += k
            if kind != "W":
                chain.append(len(ops) - 1)
            if j == 0:
                fill()
            if kind == "R" and at["R"] < 96:
                continue
            if kind == "R":
                scan(N_("SB", 0, 1536), N_("R16", 0, 1536), N_("GS", 8192, 1536), MX, MN)
                x = 4 * t + l
                tt(N_("stg", 96 * x, 96), IND(N_("W", E + l * M, IX + M), V("bdW", 6 * l, 6 * l + 6)), N_("SB", 15, 96, 16), MN)
                exchange(x)
                continue
            if kind in "FW":
                tt(N_("PR", e0, e), IND(win, cols(1)), N_("PF", e0, e), MN)
            z, w, src, step = ("F", 8, "PR", "R8") if kind in "FW" else ("S", 16, "GS", "R16")
            at[z] += k
            if fin:
                a, e = w * scanned[z], w * (at[z] - scanned[z])
                scan(N_("SO", a, e), N_(step, 0, e), N_(src, a, e), AD, MN)
                scanned[z] = at[z]
            if fin == 2:
                finish(done[z], at[z] - done[z], w)
                done[z] = at[z]

    def odd_gathers(js):
        for j in js:
            move("v" if NW <= j < NW + NV else "s", N_("GS", 256 * j, 256), IND(V(TW(4), 0, NONE + 1), N_("OLU", 16 * j, 16)), 127.0)

    def odd_tops():
        odd_gathers(range(NW, 16))
        for a, n in ((0, 96), (96, 96), (192, 48), (240, 16)):
            scan(N_("SB", 16 * a, 16 * n), N_("R16", 0, 16 * n), N_("GS", 16 * a, 16 * n), MX, MN)
        tt(N_("yrs", 1, LN, 2), N_("SB", 15, LN, 16), V("Ao"), MN)

    def views(h, nh=1):
        def Hf(name): return N_(name, HN * h, HN * nh)
        def Tops(name, at): return N_(name, at + LN * h, HN * nh, 2)
        def L(name, at=0): return N_(name, at + 8 * h, 8 * nh)
        def B(k, j=0): return PS(((7, 3, 5), (6, 2, 4))[h][k], HN * j, HN)
        return Hf, Tops, L, B

    def aside(h, nh, par):
        Hf, Tops, L, B = views(h, nh)
        a, b = PS(1 - h if nh == 1 else 1, LN, HN * nh), PS(1 - h if nh == 1 else 1, LN + HN if nh == 1 else 0, HN * nh)
        total(a, [(V("nI"), N_("thB", LN * par + HN * h, HN * nh)), (V("I16th"), Hf("k2")), (V("nI256"), Hf("DM"))])
        act(Hf("ok"), a, (TOP - 8) / 16 - 383.0, -1.0, Fn.Sign)
        total(b, [(V("I"), N_("NEG", 0, HN * nh)), (V("BO"), Hf("ok"))])
        scan(Hf("SW"), N_("RM0", 0, HN * nh), b, MU, MX)
        for k in range(h, h + nh):
            act(N_("nl", 64 * k, 64), IND(N_("SW", HN * k, HN), V("rp")), 94208.0, -5376.0)

    def lanes(h, par):
        Hf, Tops, L, B = views(h)
        H = "H%d" % h
        const(N_(H, HN + 15, 8, 16), (WA - par - 0.25) / 8)
        pick(N_(H, 4 * HN + 15, 8, 16), L("two", 16 * par), [[0, 8]], Op.is_ge, 0, 0)
        tr(Hf("k2a"), Hf("k2"))
        scan(Hf("k2b"), Hf("k2a"), V("RM"), MX, AD)
        tr(Hf("k2c"), Hf("k2b"))
        total(B(2), [(V("I32"), Tops("U", IX + 4 * M + par)), (V("I31"), Hf("k2")), (V("S32"), Hf("k2c"))])
        above(FIRSTQ[1 - h], Hf("X1"), B(2), C(5))
        if MASKQ[1 - h] == "v":
            ts(Hf("DM"), Hf("X1"), 0.0, Op.is_gt)
        else:
            act(Hf("DM"), Hf("X1"), 0.0, 1.0, Fn.Sign)
        total(B(0, 1), [(V("S15"), Hf("k2c")), (V("BOp"), Hf("DM"))])
        move(BASEQ[1 - h], Hf("n1"), B(0, 1), C(6))
        if JOIN == 1 or h == 0:
            aside(h, JOIN, par)
        for s in range(1, 5):
            if s == 1:
                x = Hf("X1")
                own = [(V("CB", p1=3), V("one", 0, HN, p1=3)), (V("I32"), Tops("W", IX + 4 * M + par))]
                back = [(V("IS"), V("c2"))]
            else:
                x, lst = Hf("X"), L("FL", 16 * (s - 1))
                act(Hf("Dg"), IND(N_("W", 0, 2960), lst), OFF)
                tt(x, IND(N_("U", 0, 2960), lst), Hf("DM"), MU)
                own = [(V("IS"), Hf("n1")), (V("I"), Hf("Dg"))]
                back = [(V("IS"), V("cq")), (V("nIS"), Hf("n1"))]
            total(B(1), own + [(V("nBOS"), x)])
            ts2(Hf("Y"), B(1), LO, MX, HI, MN)
            total(B(2), back + [(V("BOS"), x), (V("BO"), Hf("Y"))])
            scan(N_(H, (4 + s) * HN, HN), N_("RM0", 0, HN), B(2), MU, MX)
            if s < 4:
                above(NEXTQ[1 - h], L("FL", 16 * s), N_(H, (4 + s) * HN + 15, 8, 16), -float(E))

    def writes(h, par):
        Hf, Tops, L, B = views(h)
        H, tg, fu = "H%d" % h, N_("tf", 16 * h, 8), N_("tf", 16 * h + 8, 8)
        tt(N_("GG", HN * h, 64), IND(N_(H, 0, 8 * HN), V("LC", 0, 4)), N_("nl", 64 * h, 64), AD)
        act(Tops("U", acol(4) + par), Hf("n1"), 0.0, 0.0625)
        walk = IND(N_(H, HN, 8 * HN), V("LC"))
        tt(Hf("CC"), walk, Hf("GG"), MN)
        act(Hf("Z"), walk, 0.0, -8.0)
        scan(Hf("FT"), Hf("Z"), Hf("CC"), AD, MX)
        move(AIMQ[1 - h], N_("tf", 16 * h, 16), N_("FT", HN * h + 7, 16, 8))
        ids = IND(Hf("FT"), V("ex"))
        tt(Hf("XI"), ids, V("DG", 0, HN), MU)
        act(Hf("AE"), ids)
        mm(B(1), V("BO"), Hf("XI"))
        tt(Hf("XL"), IND(V("U"), tg), Hf("DM"), MU)
        total(B(0), [(V("nI"), Hf("n1")), (V("BO16"), Hf("ok")), (V("BO16"), Hf("XL"))])
        if PLACEQ[1 - h] == "v":
            ts(Hf("KL"), B(0), -14.0 * 16, EQ)
        else:
            act(Hf("ab"), B(0), 14.0 * 16, 1.0, Fn.Abs)
            act(Hf("KL"), Hf("ab"), 1.0, -1.0, RELU)
        act(Hf("old"), IND(V("W"), tg), -1024.0)
        a, b, new = PS(1 - h, LN, HN), B(0, 1), IND(N_("T0", SD0, WN), fu)
        if LINKQ[1 - h] == "s":
            act(Hf("sub"), new, -1024.0)
            total(b, [(V("nI"), Hf("sub")), (V("nI4k"), Hf("KL"))])
            act(Hf("ZD"), b, 1024.0 - 4096.0, -1.0, RELU)
        else:
            tt(Hf("ZD"), new, Hf("KL"), MU)
        total(a, [(V("nI16"), Hf("DM")), (V("I8"), Hf("ok")), (V("I"), Hf("old")), (V("nI4k"), Hf("KL"))])
        above(OLDQ[1 - h], Hf("oW"), a, 1024.0 + 8.0)
        x2, b0 = B(2), B(1)
        mm(x2, V("I"), V("N16"), True, False)
        mm(x2, V("BO"), Hf("XI"), False, False)
        for d in list(range(1, 16 // BLOCKS)) + [0]:
            n = HN - 16 * d
            eq = N_("EQ", LN * d + HN * h, n)
            tt(eq, N_("AE", HN * h, n), (b0[0], 16 * d, HN, 1, 0, 128), EQ)
            mm((x2[0], 16 * d, HN, 1, 0, 128), V("BOw" if d else "TRI"), eq, False, d == 0)
        scan(Hf("OF"), N_("SPd", LN * par + HN * h, HN), x2, MN, MX)
        move(OFFQ[1 - h], L("off"), N_("OF", HN * h + 15, 8, 16), WA - par - 0.2)

    for t in range(NP):
        par, last = t & 1, t == NP - 1
        if t == 0:
            late_setup()
        lists(t)
        released(2); released(3)
        if last:
            move("g", V("OLU"), N_("W", IX + 4 * M + 1, LN, 2))
            move("g", V("Ao"), N_("W", acol(4) + 1, LN, 2))
        ghosts(4 * t, 0)
        if t == 0:
            spread(0)
        for l in range(1, 5):
            def fill(l=l):
                if l < 4:
                    own_keys(l + 1, par)
            level(t, l, fill)
            if l < 4:
                ghosts(4 * t + l, l)
            if t == 0:
                spread(l)
        lanes(1, par)
        lanes(0, par)
        writes(1, par)
        writes(0, par)
        if last:
            act(V("yrs", 0, M, 2), V("k2"), 127.0 - TOP / 16, 0.0625)
            odd_gathers(range(NW))
        nd = 16 // BLOCKS
        for b in range(BLOCKS - 1, -1, -1):
            tt(IND(V("W"), N_("off", nd * b, nd)), N_("oW", 16 * nd * b, 16 * nd), N_("ZD", 16 * nd * b, 16 * nd), AD)
        if not last:
            release0(t + 1)
            lists1()
            own_keys(1, 0)
        else:
            dma("y", ext(T.yd[:, :]), N_("W", IX + M, 4 * M))
            dma("g", ext(T.ya[:, :]), N_("W", WA, E))
            odd_tops()
            dma("y", ext(T.yr[:, :]), V("yrs"))
    return ops, chain


def arrange(ops, deps, chain):
    n, wake = len(ops), COST["WAKE"]
    soft = {b: a for a, b in zip(chain, chain[1:]) if a not in deps[b]}
    opening = [[i for i in range(n) if ops[i][0] == "g" and (ops[i][3] or ops[i][2])[0][:2] == x][0] for x in OPENING]
    soft.update(zip(opening[1:], opening))
    soft.update((b, a) for a, b in TURN)
    soft.update((i, opening[-1]) for i in range(n)
                if ops[i][0] == "g" and i not in opening and not any(ops[j][0] == "g" for j in deps[i]))
    deps = [d | {soft[i]} if i in soft else d for i, d in enumerate(deps)]
    after = [[] for _ in range(n)]
    for i in range(n):
        for j in deps[i]:
            after[j].append(i)
    busy, whole = zip(*[span(COST, *x[5]) for x in ops])

    def lag(a, b):
        if soft.get(b) == a or (a, b) in LOOSE:
            return 0.0
        return whole[a] - busy[a] + (0.0 if (ops[a][0] == "p" and ops[b][0] == "p") else wake)

    def run(prio, before, behind, back):
        left, ready, end = [len(d) for d in before], [whole[i] - busy[i] if back else 0.0 for i in range(n)], [0.0] * n
        free = {q: 0.0 for q in "vspgyx"}
        open_ = {q: [i for i in range(n) if ops[i][0] == q and not before[i]] for q in free}
        order, engines = [], 0.0
        while len(order) < n:
            pick = None
            for q, cand in open_.items():
                if not cand:
                    continue
                t = max(free[q], min(ready[i] for i in cand))
                b = max((i for i in cand if ready[i] <= t), key=lambda i: (prio[i], -i))
                for h in cand:
                    if t < ready[h] < t + HOLD * busy[b] and prio[h] > prio[b] + GAP:
                        b = h
                s = max(free[q], ready[b])
                if pick is None or s < pick[0]:
                    pick = (s, q, b)
            s, q, b = pick
            open_[q].remove(b)
            order.append(b)
            free[q] = end[b] = s + busy[b]
            late = 0.0
            if ops[b][4] == "d" and not back:
                late = max(0.0, engines - s - COST["DMA"])
                engines = s + late + whole[b]
            for k in behind[b]:
                ready[k] = max(ready[k], end[b] + (late if soft.get(k) != b else 0.0) + (lag(k, b) if back else lag(b, k)))
                left[k] -= 1
                if not left[k]:
                    open_[ops[k][0]].append(k)
        return order, end

    prio = [0.0] * n
    for i in range(n - 1, -1, -1):
        prio[i] = whole[i] + max([prio[k] + wake for k in after[i]], default=0.0)
    best = None
    for _ in range(ROUNDS):
        early = set(EARLY)
        for i in range(chain[0] - 1, -1, -1):
            if i in early or any(k in early for k in after[i]):
                early.add(i)
                prio[i] = max([prio[i], prio[chain[0]] - SOON] + [prio[k] + whole[i] for k in after[i] if k in early])
        order, end = run(prio, deps, after, False)
        length = max(end[i] + whole[i] - busy[i] for i in range(n))
        if best is None or length < best[0]:
            best = (length, order)
        prio = run(end, after, deps, True)[1]
    return best[1]


def refine(ops, deps, order):
    n, queue = len(ops), ["vspgyx".index(x[0]) for x in ops]
    after = [set() for _ in range(n)]
    for i in range(n):
        for j in deps[i]:
            after[j].add(i)
    sets = []
    for c in COSTS:
        busy, whole = zip(*[span(c, *x[5]) for x in ops])
        waits = [[(j, 0.0 if (j, i) in LOOSE or queue[i] == queue[j] == 2 else c["WAKE"]) for j in deps[i]] for i in range(n)]
        sets.append((busy, whole, waits, [c["DMA"] if x[4] == "d" else 0.0 for x in ops], [0.0] * n))

    def replay(steps, start):
        out = []
        for (busy, whole, waits, way, done), free in zip(sets, start):
            free = list(free)
            for i in steps:
                s = free[queue[i]]
                for j, w in waits[i]:
                    if done[j] + w > s:
                        s = done[j] + w
                free[queue[i]] = s + busy[i]
                if way[i]:
                    done[i] = free[6] = max(s, free[6] - way[i]) + whole[i]
                else:
                    done[i] = s + whole[i]
            out.append(free)
        return out

    fixed = {i for i in range(n) if ops[i][4] != "c" or (queue[i] > 2 and ops[i][3][0][0] not in ("FL", "tf", "H0", "H1"))}
    seed, start = 7, [[0.0] * 7 for _ in sets]
    for a, SPAN, TRIES, heat in [(a, s, t, h) for s, t, h in SWEEPS for a in range(0, n, s)]:
        start = start if a else [[0.0] * 7 for _ in sets]
        part, ahead = order[a:a + SPAN + REACH], order[a + SPAN + REACH:a + SPAN + REACH + AFTER]
        def length(): return sum((f[0] + f[1] if ahead else 2 * f[6]) / b for f, b in zip(replay(part + ahead, start), scale))
        scale = [c["GAT"] + c["CYC"] for c in COSTS]
        best = length()
        for k in range(TRIES):
            seed = (seed * 1103515245 + 12345) % 2147483648
            p = (seed >> 8) % len(part)
            lo = hi = p
            if part[p] in fixed:
                continue
            while lo > 0 and p - lo < REACH and part[lo - 1] not in deps[part[p]]:
                lo -= 1
            while hi < len(part) - 1 and hi - p < REACH and part[hi + 1] not in after[part[p]]:
                hi += 1
            seed = (seed * 1103515245 + 12345) % 2147483648
            z = lo + (seed >> 8) % (hi - lo + 1)
            other = [i for i in part[min(p, z):max(p, z) + 1] if queue[i] == queue[part[p]]]
            part.insert(z, part.pop(p))
            if len(other) > 1:
                now = length()
                if now <= best + heat * (1 - k / TRIES) ** 2 * ((seed >> 4) % 8) / 8:
                    best = now
                else:
                    part.insert(p, part.pop(z))
        order[a:a + len(part)] = part
        start = replay(order[a:a + SPAN], start)
    return order


def emit(g, T, steps, landed, sent):
    ops, chain = steps
    seen, deps, sends = {}, [], []
    for i, (q, call, rd, wr, kind, _) in enumerate(ops):
        d = set()
        if kind == "r":
            d.update(sends[-1:])
            sends.append(i)
        if kind == "x":
            d.add(sends[call])
        for views, w in ((rd, False), (wr, True)):
            for x in views:
                psum = x[0].startswith("ps")
                for (j, lo, hi, rows, jw) in seen.get(x[0], []):
                    a, b = x[1], x[2]
                    if w and jw and (kind == "d") != (ops[j][4] == "d"):
                        e = 16 // SIZE[BUF[x[0]][0]]
                        a, b = a // e * e, -(-b // e) * e
                    meet = lo < b and a < hi and rows & set(range(*x[4:]))
                    if (meet and (w or jw)) or (psum and (ops[j][0] != q or q == "p")):
                        d.add(j)
        for views, w in ((rd, False), (wr, True)):
            for x in views:
                old = seen.get(x[0], [])
                if w:
                    old = [a for a in old if not (x[3] == 1 and x[1] <= a[1] and a[2] <= x[2] and a[3] <= set(range(*x[4:])) and a[0] in d)]
                seen[x[0]] = old + [(i, x[1], x[2], set(range(*x[4:])), w)]
        d.discard(i)
        deps.append(d)
    if not ORDER:
        ORDER.extend(refine(ops, deps, arrange(ops, deps, chain)))
    order = ORDER
    place = {i: k for k, i in enumerate(order)}
    upto, known, need, marked = {q: {} for q in "vspgyx"}, {}, {}, set()
    for i in order:
        q, kind = ops[i][0], ops[i][4]
        best = {}
        for j in deps[i]:
            key = ops[j][0] if ops[j][4] == "c" else j
            if (j, i) not in LOOSE and (key not in best or place[j] > place[best[key]]):
                best[key] = j
        w = []
        if kind != "x":
            for key, j in sorted(best.items(), key=lambda x: -place[x[1]]):
                if ops[j][4] != "r" and not (q == "p" and key == "p") and upto[q].get(key, -1) < place[j]:
                    upto[q][key] = place[j]
                    for k, at in known[j].items():
                        upto[q][k] = max(upto[q].get(k, -1), at)
                    w.append(j)
                    marked.add(j)
        need[i] = w
        known[i] = dict(upto[q]) if kind != "x" else {}
    queue = {"v": g.vector, "s": g.scalar, "p": g.tensor, "g": g, "y": g.sync}
    token, count, moved = {}, {k: 0 for k in ESEM}, []
    for i in order:
        q, call, kind = ops[i][0], ops[i][1], ops[i][4]
        if kind == "x":
            token[i] = (T.sem["ar%d" % call], landed)
            continue
        for j in need[i]:
            queue[q].wait_ge(*token[j])
        ins = call(g)
        if kind == "d":
            token[i] = (T.sem["dm%d" % len(moved)], 16 * len(ins))
            for x in ins:
                x.then_inc(token[i][0], 16)
            moved.append(token[i])
        elif kind == "c" and i in marked:
            count[q] += 1
            token[i] = (T.sem[ESEM[q]], count[q])
            ins.then_inc(token[i][0], 1)
    for x in moved:
        g.sync.wait_ge(*x)
    g.wait_ge(T.sem.sent, sent)


def rank_program(g, core, T, topo):
    rank = T.rank_of(core)
    if rank is None:
        return

    def masks(r):
        src = T.cores[r]
        dsts = {d: T.cores[r ^ d] for d in (1, 2, 3)}
        far = [d for d in dsts if topo.chip(dsts[d]) != topo.chip(src)]
        out, used = {}, set()
        for group in (far, [d for d in dsts if d not in far]):
            for j, d in enumerate(group):
                free = [e for e in topo.engines(src, dsts[d]) if e not in used]
                n = 1
                while 2 * n <= min([len(free) // (len(group) - j)] + [len(x) for x in out.values()]):
                    n *= 2
                out[d] = free[:n]
                used.update(out[d])
        return out

    mine = masks(rank)

    def send(k):
        def call(g):
            tr = []
            for d in (1, 2, 3):
                rid, pid, _ = topo.addr(T.cores[rank ^ d])
                a = 96 * k + 32 * (d - 1)
                tr.append(RemoteDMATransfer(dst_ids=[DstId(rid=rid, pnc=pid)], dma_engine_mask=sum(1 << e for e in mine[d]),
                                            remote_sem=T.sem["ar%d" % k], src=T.stg[:, a:a + 32], dst=T.land[:, a:a + 32]))
            return g.remote_dma_fused(tr, local_sem=T.sem.sent)
        return call

    landed = sum(len(masks(rank ^ d)[d]) for d in (1, 2, 3))
    emit(g, T, build(rank, T, send), landed, 12 * sum(len(mine[d]) for d in mine))
